import numpy as np, ml_dtypes
CORES = [35,38,43,46]
N = 4
import mx_ref
BF = ml_dtypes.bfloat16
def gentries(a):
    return np.ascontiguousarray(a.reshape(8, 16, -1).transpose(0, 2, 1)).reshape(8, -1)
def gtable(e):
    e = np.asarray(e); return np.ascontiguousarray(e.reshape(8, -1, 16).transpose(0, 2, 1)).reshape(128, -1).astype(np.int32)
def gcols(t, e):
    v = np.concatenate([t.reshape(8, 16, -1, 4), np.zeros((8, 16, 1, 4), BF)], axis=2)
    return np.ascontiguousarray(np.stack([v[g][:, e[g]] for g in range(8)])).reshape(128, -1)
def tile(rs):
    return np.stack(rs, axis=2).reshape(128, -1).astype(BF)
def cut(t, i, w=512):
    return t[:, w * i:w * i + w]
def pick(q, e):
    c = np.concatenate([q[0].reshape(128, -1, 4), np.zeros((128, 1, 4), np.uint8)], axis=1); s = np.concatenate([q[1], np.ones((16, 1), np.uint8)], axis=1)
    return (np.ascontiguousarray(c[:, e].reshape(128, -1)), np.ascontiguousarray(s[:, e]))
def join(*qs):
    return (np.concatenate([q[0] for q in qs], axis=1), np.concatenate([q[1] for q in qs], axis=1))
def put(q, e, v):
    c, s = q[0].reshape(128, -1, 4).copy(), q[1].copy(); c[:, e] = v[0].reshape(128, -1, 4); s[:, e] = v[1]
    return (c.reshape(128, -1), s)
def pk(c, s):
    return (np.ascontiguousarray(c), mx_ref.live(s))
def emit(q):
    return q[0], q[1]
def packed(v, rng):
    q = [mx_ref.quantize(np.ascontiguousarray(v[r])) for r in range(N)]
    return np.stack([a for a, b in q]), np.stack([mx_ref.plane(b, rng) for a, b in q])
def values_of_codes():
    e, c = np.zeros((128, 128, 4), np.float32), np.zeros((128, 2, 4), np.uint8)
    e[np.arange(128), np.arange(128), 0] = 1
    c[:127, :, 0] = np.arange(256).reshape(2, 128).T[:127]
    return mx_ref.matmul(mx_ref.quantize(e.reshape(128, 512).astype(BF)), (c.reshape(128, 8), np.full((16, 2), 127, np.uint8))).T.reshape(-1).astype(np.float64)
CODE_VALUE, SCALE_VALUE = values_of_codes(), 2.0 ** (np.arange(256) - 127.0)
def decode(q):
    return (CODE_VALUE[q[0]].reshape(16, 8, -1, 4) * SCALE_VALUE[q[1]][:, None, :, None] + 0.0).reshape(128, -1).astype(np.float32)
def f(rng, *shape):
    return mx_ref.flush((rng.standard_normal(shape, dtype=np.float32) * np.exp2(rng.integers(-2, 3, shape[:-1] + (1,)))).astype(BF))
def wide(rng, *shape, cols=0):
    v = rng.standard_normal(shape, dtype=np.float32) * np.exp2(rng.integers(-12, 13, shape)).astype(np.float32)
    if cols: v *= np.repeat(np.exp2(rng.integers(-cols, cols + 1, shape[:-2] + (1, shape[-1] // 4))) * (rng.random(shape[:-2] + (1, shape[-1] // 4)) > 0.0625), 4, axis=-1).astype(np.float32)
    return mx_ref.flush(v.astype(BF))
C, K, R = 320, 208, 3
def big(v, k):
    v = v.astype(np.float32) * np.float32(k)
    v[np.abs(v) < np.float32(2.0 ** -16)] = 0
    return v.astype(BF)
def numbers_of(rng):
    return {"x": big(f(rng, N, 128, 4 * C), 1), "u": np.array(f(rng, N, 128, 512)), "v": np.array(f(rng, N, 128, 512))}
def ends(a, b):
    return {"ea": np.stack([gtable(e) for e in a]), "eb": np.stack([gtable(e) for e in b])}
def weights(rng, w):
    c, p = packed(w, rng)
    return {"wc": c, "ws": p}
def still(rng):
    w = np.zeros((N, 128, 4, 128, 4), np.float32)
    i = np.arange(128)
    for b in range(4): w[:, i, b, i, b] = 32
    return weights(rng, w.reshape(N, 128, 2048).astype(BF))
def signs(rng):
    return np.stack([rng.permutation(8) % 2 * 2.0 - 1.0 for r in range(N)])
def setup_inputs(rng):
    d = numbers_of(rng)
    a, b = rng.integers(0, C, (2, N, 8, 2 * K))
    return {**d, **ends(a, b), **weights(rng, f(rng, N, 128, 2048))}
def setup_inputs_ties(rng):
    d = numbers_of(rng)
    x = d["x"].reshape(N, 8, 16, C, 4)
    a, b = np.zeros((2, N, 8, 2 * K), int)
    o = rng.permutation(N)
    for r in range(N):
        k = rng.permutation(C) % 3
        three = x[r][:, :8, :3].copy()
        three[:, :, 2] = 0
        x[r][:, :8] = three[:, :, np.zeros(C, int) if r == o[0] else k]
        e = np.argsort(k, kind="stable")
        at = np.searchsorted(k[e], np.arange(3))
        q = np.stack([rng.permutation(2 * K) % 9 for g in range(8)])
        a[r] = e[at[q // 3] + rng.integers(0, C // 3, q.shape)]
        b[r] = e[at[q % 3] + rng.integers(0, C // 3, q.shape)]
    x[o[1], :, :8] = 0
    u = d["u"].reshape(N, 8, 16, 128, 4)
    u[:, :, 8:, ::16] = 0
    w = np.array(f(rng, N, 128, 2048)).reshape(N, 8, 16, 4, 8, 16, 4)
    w[:, :, 8:, :, :, :8] = 0
    return {"x": x.reshape(N, 128, 4 * C), "u": u.reshape(N, 128, 512), "v": d["v"], **ends(a, b), **weights(rng, w.reshape(N, 128, 2048))}
def setup_inputs_near(rng):
    d = numbers_of(rng)
    x = d["x"].astype(np.float32).reshape(N, 8, 16, C, 4)
    x[:, :, :2] = 0
    x[:, :, 8:10] = 0
    x[:, :, 10:] = rng.integers(4, 8, (N, 8, 6, C, 4)) * rng.choice([-1.0, 1.0], (N, 8, 6, C, 4)) * 2.0 ** -20
    u = d["u"].reshape(N, 128, 128, 4)
    u[:, :, ::16] = 0
    a, b = np.zeros((2, N, 8, 2 * K), int)
    s = np.arange(2 * K) * (C // 2) // (2 * K)
    v = ((np.arange(C // 2)[:, None] >> np.arange(8)) & 1) * np.exp2(np.arange(8) - 23.0)
    sg = signs(rng)
    for r in range(N):
        k = rng.permutation(8) % 4
        up, far = k % 2, k // 2
        for g in range(8):
            e = rng.permutation(C)
            p, z = e[:C // 2], e[C // 2:]
            x[r, g, 0, p, 0] = 1
            x[r, g, 1, p, 0] = 2.0 ** -9
            x[r, g, 8, p] = v[:, :4]
            x[r, g, 9, p] = v[:, 4:]
            if far[g]: x[r, g, 0, p[C // 2 - 1], 0] = 2.0 ** 30
            h = 16 * g
            u[r, h:h + 2, h, 0] = sg[r, g]
            u[r, h + 8:h + 10, h] = sg[r, g]
            m = p[s if up[g] else s[rng.permutation(2 * K)]]
            q = z[rng.integers(0, C // 2, 2 * K)]
            first = rng.random(2 * K) < 0.5
            a[r, g] = np.where(first, m, q)
            b[r, g] = np.where(first, q, m)
    return {"x": x.reshape(N, 128, 4 * C).astype(BF), "u": u.reshape(N, 128, 512), "v": d["v"], **ends(a, b), **still(rng)}
def setup_inputs_huge(rng):
    d = numbers_of(rng)
    far = (rng.permutation(N) < N // 2)[:, None, None, None]
    c = np.stack([rng.permutation(C) % 2 * 2.0 - 1.0 for r in range(N)])
    x = np.where(far, 2.0 ** 30, 2.0 ** -15) * (0.6 + 0.4 * rng.random((N, 128, C, 4))) * c[:, None, :, None]
    u = d["u"].reshape(N, 128, 128, 4)
    s = np.where(far, 2.0 ** 30, 2.0 ** -29) * (1 - 0.25 * rng.random((N, 128, 8, 4))) * signs(rng)[:, None, :, None]
    two = np.isin(np.arange(128)[:, None] - 16 * np.arange(8), (0, 1))[None, :, :, None]
    s = np.where(far | two, s, 0.0)
    u[:, :, ::16] = s.astype(np.float32).astype(BF)
    a, b = np.zeros((2, N, 8, 2 * K), int)
    for r in range(N):
        p = np.flatnonzero(c[r] > 0)[rng.integers(0, C // 2, (8, 2 * K))]
        q = np.flatnonzero(c[r] < 0)[rng.integers(0, C // 2, (8, 2 * K))]
        first = rng.random((8, 2 * K)) < 0.5
        a[r] = np.where(first, p, q)
        b[r] = np.where(first, q, p)
    return {"x": x.astype(np.float32).reshape(N, 128, 4 * C).astype(BF), "u": u.reshape(N, 128, 512), "v": d["v"], **ends(a, b), **still(rng)}
def setup_inputs_knots(rng):
    d = numbers_of(rng)
    x = d["x"].reshape(N, 128, C, 4)
    x[:, :, 0] = 0
    x[:, :, 1] = np.abs(x[:, :, 1].astype(np.float32)).astype(BF)
    u = d["u"].reshape(N, 128, 128, 4)
    u[:, :, ::16] = np.abs(u[:, :, ::16].astype(np.float32)).astype(BF)
    a, b = rng.integers(0, C, (2, N, 8, 2 * K))
    for r in range(N):
        g = rng.permutation(8)
        a[r, g[0]] = 0
        b[r, g[0]] = 1
        b[r, g[1]] = a[r, g[1]]
        for h, lo in ((g[2], 0), (g[3], K)):
            a[r, h] = 0
            b[r, h] = 1
            b[r, h, lo:lo + K] = 0
        a[r, g[4]] = C - 1
        a[r, g[5]] = np.arange(2 * K) % C
        b[r, g[5]] = (np.arange(2 * K) + 1) % C
    return {"x": x.reshape(N, 128, 4 * C), "u": u.reshape(N, 128, 512), "v": d["v"], **ends(a, b), **weights(rng, f(rng, N, 128, 2048))}
def setup_inputs_spread(rng):
    d = setup_inputs(rng)
    d["x"] = big(wide(rng, N, 128, 4 * C, cols=6), 1)
    return d
def check_inputs(d):
    b = []
    for k in ("x", "u", "v"):
        a = np.abs(d[k].astype(np.float32))
        if not (np.isfinite(a).all() and ((a == 0) | (a >= 2.0 ** -30) & (a <= 2.0 ** 30)).all()): b.append("a value of " + k)
    for k in ("ea", "eb"):
        if not ((d[k] >= 0) & (d[k] < C)).all(): b.append("an entry of " + k)
    a = np.abs(np.stack([decode(pk(d["wc"][r], d["ws"][r])) for r in range(N)]))
    if not ((a == 0) | (a >= 2.0 ** -30) & (a <= 2.0 ** 30)).all(): b.append("a number that wc and ws hold")
    return b
def reference(x, u, v, ea, eb, wc, ws):
    qu = [mx_ref.quantize(u[r]) for r in range(N)]
    lay = [pk(wc[r], ws[r]) for r in range(N)]
    a, b = [gentries(ea[r]) for r in range(N)], [gentries(eb[r]) for r in range(N)]
    new = [mx_ref.quantize(x[r]) for r in range(N)]
    held = [q for q in new]
    nums = [np.zeros((128, 0), BF) for r in range(N)]
    s = [np.zeros((8, 0), np.float32) for r in range(N)]
    for t in range(1, R + 1):
        got = decode(join(*new)).astype(BF)
        n = C + (t - 1) * K
        for r in range(N):
            nums[r] = np.concatenate([nums[r], cut(got, r, 4 * C if t == 1 else 4 * K)], axis=1)
            s[r] = np.concatenate([s[r], mx_ref.matmul(qu[r], new[r])[::16]], axis=1)
        for r in range(N):
            z = np.abs(np.take_along_axis(s[r], a[r], axis=1) - np.take_along_axis(s[r], b[r], axis=1))
            e = np.sort(np.argsort(-z, axis=1, kind="stable")[:, :K], axis=1)
            p, q = np.take_along_axis(a[r], e, axis=1), np.take_along_axis(b[r], e, axis=1)
            mid = (gcols(nums[r], p).astype(np.float32) + gcols(nums[r], q).astype(np.float32)) * np.float32(0.5)
            m = mx_ref.quantize(np.ascontiguousarray(mid.astype(BF)))
            w = lay[(r + t) % N]
            new[r] = mx_ref.quantize(tile([mx_ref.matmul(pick(w, np.arange(128 * i, 128 * i + 128)), m) * np.float32(0.03125) for i in range(4)]))
            held[r] = join(held[r], new[r])
            at = np.tile(n + np.arange(K), (8, 1))
            a[r], b[r] = np.stack([p, at], axis=2).reshape(8, -1), np.stack([at, q], axis=2).reshape(8, -1)
    y, el = np.zeros((N, 128, C + R * K), np.float32), np.zeros((N, 8, 4 * K), np.float32)
    oc, osc = np.zeros((N, 128, 4 * (C + R * K)), np.uint8), np.zeros((N, 16, C + R * K), np.uint8)
    for r in range(N):
        y[r] = mx_ref.matmul(mx_ref.quantize(v[r]), held[r])
        el[r] = np.concatenate([a[r], b[r]], axis=1)
        oc[r], osc[r] = emit(held[r])
    return {"y": y, "el": el, "oc": oc, "osc": osc}

@@ -1,0 +1,512 @@
+import numpy as np
+from concourse.mybir import dt, AluOpType, AxisListType, ActivationFunctionType
+
+C, K, R = 320, 208, 3
+E2 = 2 * K
+NT = C + R * K
+ND = C + (R - 1) * K
+S15 = 2.0 ** 15
+X4, U8, BF, F32, I32, U16 = "float8_e4m3fn_x4", "uint8", "bfloat16", "float32", "int32", "uint16"
+
+SCRATCH = {}
+for _d, _bufs in (
+    (BF, {"xt": 4 * C, "ut": 512, "vt": 512, "et": 2048, "diag": 128, "z0": E2, "junk": E2, "c8": E2, "s8": E2, "res": E2,
+          "gt": E2, "ge": E2, "cap": E2, "cum": E2, "qn": E2, "ulpb": 2, "dh": 4 * ND, "bg": 4 * K, "mt": 4 * K, "rt": 4 * K}),
+    (X4, {"wq": 512, "wq1": 512, "wq2": 512, "wq3": 512, "tab": NT, "qu": 128, "qg": 128, "qv": 128, "qe": 512, "qm": K}),
+    (U8, {"wp": 512, "wp1": 512, "wp2": 512, "wp3": 512, "tabs": NT, "qus": 128, "qgs": 128, "qvs": 128, "qes": 512, "qms": K}),
+    (I32, {"eab": 52, "uoi": 8, "pidx": 1, "pbit": 2, "xi": 32, "li": 42}),
+    (U16, {"eabu": 52, "uou": 8, "ecu": 2, "lu1": 42, "lu2": 42, "lu3": 42}),
+    (F32, {"rh": 2, "num": E2, "kilo": E2, "half": 32, "k0": 32, "k8": 32, "k8b": 32, "pw": 32, "ca": 24, "cv": 8,
+           "ptab": C, "pg": E2, "dif": E2, "z": E2, "cnt": 16, "bias": 16, "step": 10, "tl": 32, "tt": 96, "tl8": 64, "tt8": 96,
+           "keya": E2, "keyb": E2, "key2": E2, "key3": E2, "dka": E2, "dkb": E2, "sa": E2, "sb": E2, "kq": 32,
+           "pa2": E2, "pb2": E2, "pa3": E2, "pb3": E2, "a2": E2, "b2": E2, "a3": E2, "b3": E2, "elb": 2 * E2, "ysb": NT}),
+):
+    for _n in _bufs:
+        SCRATCH[_n] = ("sbuf", [128, _bufs[_n]], _d)
+for _i in range(7):
+    SCRATCH["ps%d" % _i] = ("psum", [128, 512], F32)
+
+POOL = {"v": 44, "a": 30, "t": 14, "g": 16}
+NDMA = 26
+SEMAPHORES = ["arr1", "arr2", "arr3", "sent"] + ["d%d" % _i for _i in range(NDMA)]
+for _q in POOL:
+    SEMAPHORES += ["%s%d" % (_q, _i) for _i in range(POOL[_q])]
+
+A = AluOpType
+AF = ActivationFunctionType
+
+
+def v(name, a=0, b=None, s=1):
+    return ("v", name, a, SCRATCH[name][1][1] if b is None else b, s)
+
+
+def col(name, j):
+    return v(name, j, j + 1)
+
+
+def sub(x, a, b):
+    return v(x[1], x[2] + a, x[2] + b)
+
+
+def ind(win, off, words=False):
+    return ("i", win, off, words)
+
+
+def send_mask(T, topo, src, dst):
+    far = set()
+    for c in T.cores:
+        if topo.chip(c) != topo.chip(src):
+            far |= set(topo.engines(src, c))
+    es = topo.engines(src, dst)
+    if topo.chip(src) == topo.chip(dst):
+        rest = [e for e in es if e not in far]
+        if rest and 128 % len(rest) == 0:
+            es = rest
+    return sum(1 << e for e in es), len(es)
+
+
+def program(g, T):
+    ops = []
+    last_w = {n: np.full(SCRATCH[n][1][1], -1) for n in SCRATCH}
+    readers = {n: [] for n in SCRATCH}
+    queue = {"v": g.vector, "a": g.scalar, "t": g.tensor, "g": g, "s": g.sync}
+
+    def ap(x):
+        if not isinstance(x, tuple):
+            return x
+        if x[0] == "i":
+            w = ap(x[1])
+            if x[3]:
+                w = w.bitcast(dt.uint32)
+            return w.indirect(ap(x[2]))
+        return T[x[1]][:, x[2]:x[3]] if x[4] == 1 else T[x[1]][:, x[2]:x[3]:x[4]]
+
+    def views(xs):
+        out = []
+        for x in xs:
+            if isinstance(x, tuple):
+                out += [x[1], x[2]] if x[0] == "i" else [x]
+        return out
+
+    def cols(x):
+        return np.arange(512) if SCRATCH[x[1]][0] == "psum" else np.arange(x[2], x[3], x[4])
+
+    def add(q, fn, reads, writes, kind="c", sem=None):
+        me, deps = len(ops), set()
+        for x in views(reads):
+            n = x[1]
+            if SCRATCH[n][0] == "psum":
+                deps |= {o for o, ix in readers[n] if ops[o]["q"] != q}
+            deps |= set(int(o) for o in last_w[n][cols(x)])
+        for x in views(writes):
+            n, idx = x[1], cols(x)
+            deps |= set(int(o) for o in last_w[n][idx])
+            m = np.zeros(len(last_w[n]), bool)
+            m[idx] = True
+            deps |= {o for o, ix in readers[n] if m[ix].any()}
+            readers[n] = [(o, ix[~m[ix]]) for o, ix in readers[n] if not m[ix].all()]
+            last_w[n][idx] = me
+        for x in views(reads):
+            readers[x[1]].append((me, cols(x)))
+        deps.discard(-1)
+        deps.discard(me)
+        ops.append({"q": q, "fn": fn, "deps": deps, "kind": kind, "sem": sem})
+
+    def emit():
+        known = {q: 0 for q in queue}
+        after, waits, needed = [], [], set()
+        for i, o in enumerate(ops):
+            w = []
+            if o["kind"] != "r":
+                for d in sorted(o["deps"], reverse=True):
+                    if not known[o["q"]] >> d & 1:
+                        w.append(d)
+                        known[o["q"]] |= after[d]
+                o["known"] = known[o["q"]]
+            after.append((o["known"] if o["kind"] != "r" else 0) | 1 << i)
+            waits.append(w)
+            needed |= set(w)
+        pool = {q: [[None, 0] for j in range(POOL[q])] for q in POOL}
+        nd, turn, tail = [0], {q: 0 for q in POOL}, []
+        for i, o in enumerate(ops):
+            if o["kind"] == "r":
+                continue
+            q = o["q"]
+            for d in reversed(waits[i]):
+                queue[q].wait_ge(T.sem[ops[d]["sem"][0]], ops[d]["sem"][1])
+            ins = o["fn"]()
+            if o["kind"] == "d":
+                o["sem"] = ("d%d" % nd[0], 16)
+                nd[0] += 1
+                ins.then_inc(T.sem[o["sem"][0]], 16)
+                if i not in needed:
+                    tail.append((q, o["sem"]))
+            elif o["kind"] == "c" and i in needed:
+                for k in range(POOL[q]):
+                    j = (turn[q] + k) % POOL[q]
+                    p = pool[q][j]
+                    if p[0] is None or o["known"] >> p[0] & 1:
+                        break
+                else:
+                    raise ValueError("no free semaphore on " + q)
+                turn[q] = j + 1
+                p[0] = i
+                p[1] += 1
+                o["sem"] = ("%s%d" % (q, j), p[1])
+                ins.then_inc(T.sem[o["sem"][0]], 1)
+        for q, s in tail:
+            queue[q].wait_ge(T.sem[s[0]], s[1])
+
+    return ap, add, emit
+
+
+def rank_program(g, core, T, topo):
+    rank = T.rank_of(core)
+    if rank is None:
+        return
+    n_ranks = len(T.cores)
+    ap, add, emit = program(g, T)
+    V, S, PE = g.vector, g.scalar, g.tensor
+
+    def ts(out, in0, s1, op0, s2=None, op1=None):
+        if op1 is None:
+            add("v", lambda: V.tensor_scalar(ap(out), ap(in0), ap(s1), None, op0), [in0, s1], [out])
+        else:
+            add("v", lambda: V.tensor_scalar(ap(out), ap(in0), ap(s1), ap(s2), op0, op1), [in0, s1, s2], [out])
+
+    def tt(out, in0, in1, op):
+        add("v", lambda: V.tensor_tensor(ap(out), ap(in0), ap(in1), op), [in0, in1], [out])
+
+    def cp(out, in_):
+        add("v", lambda: V.tensor_copy(ap(out), ap(in_)), [in_], [out])
+
+    def red(out, in_, op, negate=False):
+        add("v", lambda: V.tensor_reduce(ap(out), ap(in_), AxisListType.X, op, negate=negate), [in_], [out])
+
+    def scan(out, d0, d1, init, op0, op1):
+        add("v", lambda: V.tensor_tensor_scan(ap(out), ap(d0), ap(d1), ap(init), op0, op1), [d0, d1, init], [out])
+
+    def tr(out, in_):
+        add("v", lambda: V.transpose(ap(out), ap(in_)), [in_], [out])
+
+    def fill(out, c):
+        add("v", lambda: V.memset(ap(out), c), [], [out])
+
+    def quant(q, s, in_):
+        add("v", lambda: V.quantize_mx(ap(q), ap(s), ap(in_)), [in_], [q, s])
+
+    def act(out, in_, f, bias=None, scale=None, acc=None):
+        kw = {k: x for k, x in (("bias", bias), ("scale", scale), ("accum_out", acc)) if x is not None}
+        add("a", lambda: S.activation(ap(out), ap(in_), f, **{k: ap(x) for k, x in kw.items()}), [in_, bias, scale], [out, acc])
+
+    def mm(out, wq, ws, xq, xs):
+        add("t", lambda: PE.matmul_mx(ap(out), ap(wq), ap(ws), ap(xq), ap(xs), True, True), [wq, ws, xq, xs], [out])
+
+    def iota(out, pattern, base, cm):
+        if SCRATCH[out[1]][2] == I32:
+            add("g", lambda: g.iota(ap(out), pattern, base, cm), [], [out])
+        else:
+            add("g", lambda: g.iota(ap(out), pattern, base, cm, allow_small_or_imprecise_dtypes=True), [], [out])
+
+    def dma(q, out, in_, reads, writes):
+        eng = g.sync if q == "s" else g.scalar
+        add(q, lambda: eng.dma_start(out(), in_()), reads, writes, "d")
+
+    def codes(x):
+        return ap(x).bitcast(dt.uint8)
+
+    def tabv(a, b):
+        return v("tab", a, b), v("tabs", a, b)
+
+    def store_y(q, a, b):
+        dma(q, lambda: T.y[:, a:b], lambda: T.ysb[:, a:b], [v("ysb", a, b)], [])
+
+    def store(a, b, qs):
+        dma(qs[0], lambda: T.oc[:, 4 * a:4 * b], lambda: codes(v("tab", a, b)), [v("tab", a, b)], [])
+        for k in range(4):
+            dma(qs[1 + k], lambda k=k: T.osc[4 * k:4 * k + 4, a:b], lambda k=k: T.tabs[32 * k:32 * k + 4, a:b], [v("tabs", a, b)], [])
+
+    def unpack(a, b):
+        for i in range(4):
+            mm(v("ps%d" % i, 0, b - a), v("qe", 128 * i, 128 * i + 128), v("qes", 128 * i, 128 * i + 128), *tabv(a, b))
+
+    rr, hh = col("rh", 0), col("rh", 1)
+    C2, CC, RP1, INITB, RM, SROW = 0, 2, 7, 8, 9, 12
+    SC2, T6, BIAS1, M12, BCNT = 0, 1, 2, 3, 4
+
+    dma("s", lambda: T.xt[:], lambda: T.x[:], [], [v("xt")])
+    dma("a", lambda: T.ut[:], lambda: T.u[:], [], [v("ut")])
+    dma("a", lambda: T.eab[:, 0:26], lambda: T.ea[:], [], [v("eab", 0, 26)])
+    dma("a", lambda: T.eab[:, 26:52], lambda: T.eb[:], [], [v("eab", 26, 52)])
+    dma("s", lambda: codes(v("wq")), lambda: T.wc[:], [], [v("wq")])
+    dma("s", lambda: T.wp[:], lambda: T.ws[:], [], [v("wp")])
+    dma("s", lambda: T.vt[:], lambda: T.v[:], [], [v("vt")])
+
+    iota(v("pidx"), [[0, 1]], 0, 1)
+    iota(v("uoi"), [[16, 8]], 0, 0)
+    iota(v("diag"), [[-1, 128]], 0, 1)
+    iota(v("half"), [[1, 2], [0, 16]], 0, 0)
+    iota(v("num"), [[1, E2]], 0, 0)
+    iota(v("kilo"), [[1024, E2]], 0, 0)
+    fill(v("et"), 0.0)
+    ts(col("pbit", 0), v("pidx"), 15, A.bitwise_and)
+    ts(col("pbit", 1), v("pidx"), 4, A.arith_shift_right, 1, A.bitwise_and)
+    cp(v("uou"), v("uoi"))
+    cp(v("rh"), v("pbit"))
+    for b in range(4):
+        ts(v("et", 513 * b, 512 * (b + 1), 4), v("diag"), 0.0, A.is_equal)
+    fill(col("dka", 0), 0.0)
+    fill(col("dkb", 0), 0.0)
+    quant(v("qe"), v("qes"), v("et"))
+
+    def lin(out, a, b):
+        act(out, rr, AF.Identity, bias=float(b), scale=float(a))
+
+    st = [2.0 ** (-4 * (k + 1)) for k in range(5)]
+    lin(col("ca", RM), -S15, -89 * S15)
+    lin(col("ca", C2), 1 / 32, 0.5)
+    lin(col("ca", C2 + 1), 0, 0.5)
+    for k in range(4):
+        lin(col("ca", CC + k), st[k + 1] - st[k], -st[k])
+    lin(col("ca", CC + 4), -st[4], -st[4])
+    for k in range(5):
+        lin(col("ca", SROW + k), 0, st[k])
+    lin(col("ca", SROW + 5), 0, 2.0 ** -23)
+    lin(col("ca", RP1), 1, 1)
+    lin(col("ca", INITB), S15, 104.5 * S15)
+    lin(col("z0", 0), S15, -103.5 * S15)
+
+    sent = [0]
+    for t in range(1, R + 1):
+        dst = T.cores[(rank - t) % n_ranks]
+        rid, pid = topo.addr(dst)[0], topo.addr(dst)[1]
+        m, ne = send_mask(T, topo, core, dst)
+        sent[0] += 2 * ne
+        add("g", lambda t=t, rid=rid, pid=pid, m=m: g.remote_dma(codes(v("wq%d" % t)), codes(v("wq")), T.sem["arr%d" % t], T.sem.sent, pid, rid, m),
+            [v("wq")], [], "x")
+        add("g", lambda t=t, rid=rid, pid=pid, m=m: g.remote_dma(ap(v("wp%d" % t)), ap(v("wp")), T.sem["arr%d" % t], T.sem.sent, pid, rid, m),
+            [v("wp")], [], "x")
+        src = T.cores[(rank + t) % n_ranks]
+        add("g", None, [], [v("wq%d" % t), v("wp%d" % t)], "r", ("arr%d" % t, 2 * send_mask(T, topo, src, core)[1]))
+    for t, (ra, rb, o) in enumerate((("a2", "b2", 0), ("a3", "b3", 0), ("elb", "elb", E2))):
+        iota(v(ra, 1, E2, 2), [[1, K]], C + t * K, 0)
+        iota(v(rb, o, o + E2, 2), [[1, K]], C + t * K, 0)
+
+    def key1(name, o, a, b):
+        tt(v(name, 16 * a, 16 * b), ind(v("num", 0, C), v("eabu", o + a, o + b)), v("kilo", 16 * a, 16 * b), A.add)
+
+    def dk(name, key):
+        scan(v(name, 1, E2), v(key, 0, E2 - 1), v(key, 1, E2), 0.0, A.max, A.subtract)
+
+    ts(v("pw", 0, 16), v("num", 1, 17), rr, A.is_gt, 0.5, A.max)
+    ts(v("pw", 16, 32), v("num", 1, 17), rr, A.is_gt, 2.0 ** -6, A.max)
+    ts(v("k0"), v("half"), hh, A.not_equal, 1000.0, A.mult)
+    ts(v("k8b"), v("half"), hh, A.is_equal, K * S15, A.mult)
+    ts(col("cv", M12), rr, 12.0, A.min, 16 * S15, A.mult)
+    red(col("cv", T6), v("pw", 16, 32), A.mult)
+    cp(v("eabu"), v("eab"))
+    quant(v("qu"), v("qus"), v("ut"))
+    red(col("cv", SC2), v("pw", 0, 16), A.mult)
+    add("v", lambda: V.tensor_copy(ap(v("qg")).bitcast(dt.uint32), ap(ind(v("qu"), v("uou"), True))), [ind(v("qu"), v("uou"))], [v("qg")])
+    act(v("qgs"), ind(v("qus"), v("uou")), AF.Copy)
+    ts(col("cv", BIAS1), col("cv", T6), -2.0 ** 80, A.mult, col("cv", T6), A.mult)
+    quant(v("tab", 0, C), v("tabs", 0, C), v("xt"))
+    mm(v("ps4", 0, C), v("qg"), v("qgs"), *tabv(0, C))
+    unpack(0, C)
+    act(v("ptab"), v("ps4", 0, C), AF.Copy)
+    key1("keya", 0, 14, 26)
+    ts(v("k8"), v("k0"), 2.0 ** 30, A.mult, K * S15, A.add)
+    tt(col("cv", BCNT), col("cv", M12), col("ca", RM), A.add)
+    fill(v("z0", 1, E2), 0.0)
+    cp(v("pg", 288, E2), ind(v("ptab"), v("eabu", 44, 52)))
+    for a, b in ((0, 10), (10, 18)):
+        act(v("pg", 16 * a, 16 * b), ind(v("ptab"), v("eabu", 26 + a, 26 + b)), AF.Copy)
+    for a, b in ((18, 26), (0, 10), (10, 18)):
+        tt(v("dif", 16 * a, 16 * b), ind(v("ptab"), v("eabu", a, b)), v("pg", 16 * a, 16 * b), A.subtract)
+        act(v("z", 16 * a, 16 * b), v("dif", 16 * a, 16 * b), AF.Abs)
+
+    def lists(t):
+        lu = "lu%d" % t
+        if t == 1:
+            return v(lu, 0, 13), v(lu, 16, 29), None
+        return v(lu, 0, 13), v(lu, 14, 27), v(lu, 28, 41)
+
+    def next_key(t, par):
+        l1, l2, le = lists(t)
+        src = ind(v("num", 0, C), (l1, l2)[par]) if t == 1 else ind(v(("a2", "b2")[par]), le)
+        tt(v("key%d" % (t + 1), par, E2, 2), src, v("kilo", par, E2, 2), A.add)
+
+    def next_ends(t, par, on_scalar):
+        l1, l2, le = lists(t)
+        src = ind(v("num", 0, C), (l1, l2)[par]) if t == 1 else ind(v("ab"[par] + str(t)), le)
+        out = v("ab"[par] + str(t + 1), par, E2, 2) if t < R else v("elb", par * (E2 + 1), (par + 1) * E2, 2)
+        if on_scalar:
+            act(out, src, AF.Copy)
+        else:
+            cp(out, src)
+
+    def y_product(a, b):
+        mm(v("ps5", 0, b - a), v("qv"), v("qvs"), *tabv(a, b))
+
+    def y_out(a, b):
+        act(v("ysb", a, b), v("ps5", 0, b - a), AF.Copy)
+        store_y("s", a, b)
+
+    def keep_p():
+        cp(v("pa2", 1, E2, 2), v("ps4", 0, K))
+        cp(v("pb2", 0, E2, 2), v("ps4", 0, K))
+
+    for t in range(1, R + 1):
+        n = C + (t - 1) * K
+        n0 = 0 if t == 1 else n - K
+        if t == 1:
+            side = [lambda: key1("keya", 0, 0, 14), lambda: key1("keyb", 26, 0, 14), lambda: key1("keyb", 26, 14, 26),
+                    lambda: dk("dka", "keya"), lambda: dk("dkb", "keyb"), lambda: quant(v("qv"), v("qvs"), v("vt"))]
+        else:
+            side = [lambda: next_key(t - 1, 0), lambda: next_key(t - 1, 1), lambda: next_ends(t - 1, 0, False),
+                    lambda: dk("dka", "key%d" % t), lambda: next_ends(t - 1, 1, False)]
+            if t < R:
+                side.append(keep_p)
+        z = v("z")
+        mid = v("tt", 32, 64)
+        nbase, nulp, rulp = col("step", 6), col("step", 7), col("step", 8)
+
+        def bias(k):
+            return col("bias", k)
+
+        for k in range(1, 8):
+            s = col("cnt", k)
+            if k == 1:
+                act(v("junk"), z, AF.Sign, bias=col("cv", BIAS1), acc=s)
+            elif k == 2:
+                act(v("junk"), z, AF.Sign, bias=bias(2), scale=col("cv", SC2), acc=s)
+                ts(v("tt", 31, 65, 33), v("ca", C2, C2 + 2), bias(2), A.mult)
+            else:
+                act(v("junk"), z, AF.Sign, bias=bias(k), acc=s)
+                if k == 3:
+                    ts(v("step", 0, 6), v("ca", SROW, SROW + 6), nbase, A.mult)
+                if k < 7:
+                    ts(col("tt", 31), col("ca", CC + k - 3), nbase, A.mult, bias(k), A.add)
+                else:
+                    ts(v("res"), z, bias(7), A.add)
+                if k == 4:
+                    ts(nulp, col("step", 5), -2.0 ** -115, A.min)
+                if k == 5:
+                    ts(rulp, col("ca", RP1), nulp, A.mult)
+                if k == 6:
+                    ts(col("tt", 64), col("ca", CC + 4), nbase, A.mult, rulp, A.add)
+            if side:
+                side.pop(0)()
+            if k == 1:
+                ts(v("tl"), v("k0"), s, A.is_le, col("cv", BIAS1), A.mult)
+            elif k == 2:
+                ts(v("tl"), v("k0"), s, A.is_le, 1.0, A.add)
+            else:
+                ts(v("tl"), v("k0"), s, A.is_le, col("step", k - 3), A.mult)
+            tr(mid, v("tl"))
+            if k == 1:
+                red(bias(2), mid, A.min)
+            elif k == 2:
+                red(bias(3), v("tt", 31, 64), A.mult)
+                red(nbase, v("tt", 32, 65), A.mult)
+            elif k < 7:
+                red(bias(k + 1), v("tt", 31, 64), A.add)
+            else:
+                red(bias(8), v("tt", 32, 65), A.add, negate=True)
+        act(col("ulpb", 0), nulp, AF.Copy)
+        for b in range(4):
+            act(v("dh", ND * b + n0, ND * b + n), v("ps%d" % b, 0, n - n0), AF.Identity, scale=0.5)
+        if t > 1:
+            y_out(n0, n)
+        ts(v("c8"), v("res"), bias(8), A.is_ge, S15, A.mult)
+        ts(col("tt8", 31), rulp, -1.0, A.mult, bias(8), A.subtract)
+        scan(v("s8"), v("c8"), v("c8"), 0.0, A.add, A.max)
+        tot = col("s8", E2 - 1)
+        ts(v("tl8", 0, 32), v("k8"), tot, A.is_le, col("ulpb", 0), A.mult)
+        ts(v("tl8", 32, 64), v("k8b"), tot, A.is_gt, tot, A.mult)
+        tr(v("tt8", 32, 96), v("tl8"))
+        red(bias(10), v("tt8", 31, 64), A.add, negate=True)
+        red(bias(11), v("tt8", 64, 96), A.max)
+        ts(v("gt"), v("res"), bias(10), A.is_gt, -S15, A.mult)
+        ts(v("ge"), v("res"), bias(10), A.is_ge, -S15, A.mult)
+        scan(v("cap"), v("z0"), v("gt"), bias(11), A.add, A.add)
+        scan(v("cum"), v("ge"), v("cap"), col("ca", INITB), A.add, A.max)
+        act(v("junk"), v("cum"), AF.Sign, bias=col("cv", BCNT), acc=col("cnt", 8))
+        ts(v("qn"), v("cum"), 1.5 * 2.0 ** 42, A.add, 1.5 * 2.0 ** 42, A.subtract)
+        ec = col("ecu", 0)
+        lu = "lu%d" % t
+        if t == 1:
+            scan(v("sa"), v("dka"), v("qn"), 2.0 ** 23, A.add, A.min)
+            ts(ec, col("cnt", 8), 0.5, A.mult, float(K), A.add)
+            scan(v("sb"), v("dkb"), v("qn"), 2.0 ** 23, A.add, A.min)
+            act(v("kq", 0, 16), ind(v("keya"), ec), AF.Copy)
+            act(v("kq", 16, 32), ind(v("keyb"), ec), AF.Copy)
+            tt(v("xi", 0, 16), ind(v("sa"), ec), v("kq", 0, 16), A.add)
+            tt(v("xi", 16, 32), ind(v("sb"), ec), v("kq", 16, 32), A.add)
+            ts(v("li", 0, 32), v("xi"), 1023, A.bitwise_and)
+            cp(v(lu, 0, 32), v("li", 0, 32))
+        else:
+            scan(v("sa", 0, K), v("dka", 0, K), v("qn", 0, K), 2.0 ** 23, A.add, A.min)
+            ts(ec, col("cnt", 8), 0.5, A.mult, float(K), A.add)
+            scan(v("sa", K, E2), v("dka", K, E2), v("qn", K, E2), col("sa", K - 1), A.add, A.min)
+            act(v("kq", 0, 16), ind(v("key%d" % t), ec), AF.Copy)
+            tt(v("xi", 0, 16), ind(v("sa"), ec), v("kq", 0, 16), A.add)
+            x14 = v("xi", 0, 14)
+            ts(v("li", 14, 28), x14, 11, A.arith_shift_right, 255, A.bitwise_and)
+            ts(v("li", 0, 14), x14, 1023, A.bitwise_and)
+            ts(v("li", 28, 42), x14, 10, A.arith_shift_right, 511, A.bitwise_and)
+            cp(v(lu), v("li"))
+        l1, l2, le = lists(t)
+
+        def far_end(b, a, c):
+            return v("bg", K * b + 16 * a, K * b + 16 * c), ind(v("dh", ND * b + n0, ND * b + n), sub(l2, a, c))
+
+        def midpoint(b, a, c):
+            tt(v("mt", 64 * a + b, 64 * c, 4), ind(v("dh", ND * b, ND * b + n), sub(l1, a, c)), v("bg", K * b + 16 * a, K * b + 16 * c), A.add)
+
+        cp(*far_end(3, 6, 13))
+        for b in range(3):
+            act(*far_end(b, 0, 13), AF.Copy)
+        act(*far_end(3, 0, 6), AF.Copy)
+        midpoint(3, 6, 13)
+        for b in range(3):
+            midpoint(b, 0, 13)
+        midpoint(3, 0, 6)
+        quant(v("qm"), v("qms"), v("mt"))
+        for par in range(2):
+            if t == 1:
+                act(v("p" + "ab"[par] + "2", par, E2, 2), ind(v("ptab"), (l1, l2)[par]), AF.Copy)
+            elif t < R:
+                act(v("p" + "ab"[par] + "3", par, E2, 2), ind(v("p" + "ab"[par] + "2"), le), AF.Copy)
+            else:
+                next_ends(t, par, True)
+        if t == R:
+            dma("s", lambda: T.el[:], lambda: T.elb[0:128:16, :], [v("elb")], [])
+        for b in range(4):
+            mm(v("ps%d" % b, 0, K), v("wq%d" % t, 128 * b, 128 * b + 128), v("wp%d" % t, 128 * b, 128 * b + 128), v("qm"), v("qms"))
+        if t == 1:
+            y_product(0, C)
+        for b in range(4):
+            if b % 2 == 0:
+                ts(v("rt", b, 4 * K, 4), v("ps%d" % b, 0, K), 0.03125, A.mult)
+            else:
+                act(v("rt", b, 4 * K, 4), v("ps%d" % b, 0, K), AF.Identity, scale=0.03125)
+        quant(v("tab", n, n + K), v("tabs", n, n + K), v("rt"))
+        if t == 1:
+            y_out(0, C)
+        if t < R:
+            mm(v("ps4", 0, K), v("qg"), v("qgs"), *tabv(n, n + K))
+            unpack(n, n + K)
+            y_product(n, n + K)
+            for par in range(2):
+                tt(v("dif", K * par, K * par + K), v("p" + "ab"[par] + str(t + 1), par, E2, 2), v("ps4", 0, K), A.subtract)
+                act(v("z", par, E2, 2), v("dif", K * par, K * par + K), AF.Abs)
+            if t == R - 1:
+                store(0, ND, "sssss")
+        else:
+            mm(v("ps6", 0, K), v("qv"), v("qvs"), *tabv(n, n + K))
+            store(ND, NT, "sssaa")
+            cp(v("ysb", ND, NT), v("ps6", 0, K))
+            store_y("a", ND, NT)
+    emit()
+    g.wait_ge(T.sem.sent, sent[0])

@@ -11,14 +11,15 @@ X4, U8, BF, F32, I32, U16 = "float8_e4m3fn_x4", "uint8", "bfloat16", "float32", 
 SCRATCH = {}
 for _d, _bufs in (
     (BF, {"xt": 4 * C, "ut": 512, "vt": 512, "et": 2048, "diag": 128, "z0": E2, "junk": E2, "c8": E2, "s8": E2, "res": E2,
-          "gt": E2, "ge": E2, "cap": E2, "cum": E2, "qn": E2, "ulpb": 2, "dh": 4 * ND, "bg": 4 * K, "mt": 4 * K, "rt": 4 * K}),
+          "gt": E2, "ge": E2, "cap": E2, "cum": E2, "qn": E2, "ulpb": 2, "dh": 4 * ND, "bg": 4 * K, "mt": 4 * K, "rt": 4 * K,
+          "mall": 4 * E2}),
     (X4, {"wq": 512, "wq1": 512, "wq2": 512, "wq3": 512, "tab": NT, "qu": 128, "qg": 128, "qv": 128, "qe": 512, "qm": K}),
     (U8, {"wp": 512, "wp1": 512, "wp2": 512, "wp3": 512, "tabs": NT, "qus": 128, "qgs": 128, "qvs": 128, "qes": 512, "qms": K}),
-    (I32, {"eab": 52, "uoi": 8, "pidx": 1, "pbit": 2, "xi": 32, "li": 42}),
-    (U16, {"eabu": 52, "uou": 8, "ecu": 2, "lu1": 42, "lu2": 42, "lu3": 42}),
-    (F32, {"rh": 2, "num": E2, "kilo": E2, "half": 32, "k0": 32, "k8": 32, "k8b": 32, "pw": 32, "ca": 24, "cv": 8,
+    (I32, {"eab": 52, "uoi": 8, "pidx": 1, "pbit": 2, "xi": 32, "li": 32, "lw": 98}),
+    (U16, {"eabu": 52, "uou": 8, "ecu": 2, "lu1": 32, "lu2": 14, "lu3": 14, "lab": 28}),
+    (F32, {"rh": 2, "num": E2, "kilo": E2, "half": 32, "k0": 32, "k1": 32, "k8": 32, "k8b": 32, "pw": 32, "ca": 24, "cv": 8,
            "ptab": C, "pg": E2, "dif": E2, "z": E2, "cnt": 16, "bias": 16, "step": 10, "tl": 32, "tt": 96, "tl8": 64, "tt8": 96,
-           "keya": E2, "keyb": E2, "key2": E2, "key3": E2, "dka": E2, "dkb": E2, "sa": E2, "sb": E2, "kq": 32,
+           "keya": E2, "keyb": E2, "key2": E2, "dka": E2, "dkb": E2, "dkc": E2, "sa": E2, "sb": E2, "kq": 32, "qrow": 16, "xe": 16,
            "pa2": E2, "pb2": E2, "pa3": E2, "pb3": E2, "a2": E2, "b2": E2, "a3": E2, "b3": E2, "elb": 2 * E2, "ysb": NT}),
 ):
     for _n in _bufs:
@@ -238,7 +239,7 @@ def rank_program(g, core, T, topo):
     dma("a", lambda: T.ut[:], lambda: T.u[:], [], [v("ut")])
     dma("a", lambda: T.eab[:, 0:26], lambda: T.ea[:], [], [v("eab", 0, 26)])
     dma("a", lambda: T.eab[:, 26:52], lambda: T.eb[:], [], [v("eab", 26, 52)])
-    dma("s", lambda: codes(v("wq")), lambda: T.wc[:], [], [v("wq")])
+    dma("s", lambda: codes(v("wq")), lambda: T.wc[:], [v("xt")], [v("wq")])
     dma("s", lambda: T.wp[:], lambda: T.ws[:], [], [v("wp")])
     dma("s", lambda: T.vt[:], lambda: T.v[:], [], [v("vt")])
 
@@ -248,6 +249,7 @@ def rank_program(g, core, T, topo):
     iota(v("half"), [[1, 2], [0, 16]], 0, 0)
     iota(v("num"), [[1, E2]], 0, 0)
     iota(v("kilo"), [[1024, E2]], 0, 0)
+    iota(v("dkc"), [[0, E2]], -1024, 0)
     fill(v("et"), 0.0)
     ts(col("pbit", 0), v("pidx"), 15, A.bitwise_and)
     ts(col("pbit", 1), v("pidx"), 4, A.arith_shift_right, 1, A.bitwise_and)
@@ -311,39 +313,36 @@ def rank_program(g, core, T, topo):
     act(v("qgs"), ind(v("qus"), v("uou")), AF.Copy)
     ts(col("cv", BIAS1), col("cv", T6), -2.0 ** 80, A.mult, col("cv", T6), A.mult)
     quant(v("tab", 0, C), v("tabs", 0, C), v("xt"))
-    mm(v("ps4", 0, C), v("qg"), v("qgs"), *tabv(0, C))
+    H = C // 2
+    mm(v("ps4", 0, H), v("qg"), v("qgs"), *tabv(0, H))
+    mm(v("ps6", 0, H), v("qg"), v("qgs"), *tabv(H, C))
     unpack(0, C)
-    act(v("ptab"), v("ps4", 0, C), AF.Copy)
+    act(v("ptab", 0, H), v("ps4", 0, H), AF.Copy)
     key1("keya", 0, 14, 26)
+    cp(v("ptab", H, C), v("ps6", 0, H))
     ts(v("k8"), v("k0"), 2.0 ** 30, A.mult, K * S15, A.add)
     tt(col("cv", BCNT), col("cv", M12), col("ca", RM), A.add)
-    fill(v("z0", 1, E2), 0.0)
-    cp(v("pg", 288, E2), ind(v("ptab"), v("eabu", 44, 52)))
-    for a, b in ((0, 10), (10, 18)):
+    cp(v("pg", 0, 128), ind(v("ptab"), v("eabu", 26, 34)))
+    for a, b in ((8, 18), (18, 26)):
         act(v("pg", 16 * a, 16 * b), ind(v("ptab"), v("eabu", 26 + a, 26 + b)), AF.Copy)
-    for a, b in ((18, 26), (0, 10), (10, 18)):
+    fill(v("z0", 1, E2), 0.0)
+    for a, b in ((0, 8), (8, 18), (18, 26)):
         tt(v("dif", 16 * a, 16 * b), ind(v("ptab"), v("eabu", a, b)), v("pg", 16 * a, 16 * b), A.subtract)
         act(v("z", 16 * a, 16 * b), v("dif", 16 * a, 16 * b), AF.Abs)
+    ts(v("qrow"), v("num", 0, 16), -6.0, A.add, 16 * S15, A.mult)
 
-    def lists(t):
-        lu = "lu%d" % t
-        if t == 1:
-            return v(lu, 0, 13), v(lu, 16, 29), None
-        return v(lu, 0, 13), v(lu, 14, 27), v(lu, 28, 41)
+    def ends(t):
+        return (v("lu1", 0, 13), v("lu1", 16, 29)) if t == 1 else (v("lab", 0, 13), v("lab", 14, 27))
 
-    def next_key(t, par):
-        l1, l2, le = lists(t)
-        src = ind(v("num", 0, C), (l1, l2)[par]) if t == 1 else ind(v(("a2", "b2")[par]), le)
-        tt(v("key%d" % (t + 1), par, E2, 2), src, v("kilo", par, E2, 2), A.add)
+    def split(t):
+        return v("lu%d" % t, 0, 13)
 
-    def next_ends(t, par, on_scalar):
-        l1, l2, le = lists(t)
-        src = ind(v("num", 0, C), (l1, l2)[par]) if t == 1 else ind(v("ab"[par] + str(t)), le)
-        out = v("ab"[par] + str(t + 1), par, E2, 2) if t < R else v("elb", par * (E2 + 1), (par + 1) * E2, 2)
-        if on_scalar:
-            act(out, src, AF.Copy)
-        else:
-            cp(out, src)
+    def next_key(par):
+        tt(v("key2", par, E2, 2), ind(v("num", 0, C), ends(1)[par]), v("kilo", par, E2, 2), A.add)
+
+    def next_ends(t, par):
+        src = ind(v("num", 0, C), ends(1)[par]) if t == 1 else ind(v("ab"[par] + str(t)), split(t))
+        act(v("ab"[par] + str(t + 1), par, E2, 2) if t < R else v("elb", par * (E2 + 1), (par + 1) * E2, 2), src, AF.Copy)
 
     def y_product(a, b):
         mm(v("ps5", 0, b - a), v("qv"), v("qvs"), *tabv(a, b))
@@ -352,21 +351,34 @@ def rank_program(g, core, T, topo):
         act(v("ysb", a, b), v("ps5", 0, b - a), AF.Copy)
         store_y("s", a, b)
 
-    def keep_p():
-        cp(v("pa2", 1, E2, 2), v("ps4", 0, K))
-        cp(v("pb2", 0, E2, 2), v("ps4", 0, K))
+    def lw(j):
+        return v("lw", 14 * j, 14 * j + 14)
 
     for t in range(1, R + 1):
         n = C + (t - 1) * K
         n0 = 0 if t == 1 else n - K
+
+        def half_d(b):
+            ts(v("dh", ND * b + n0, ND * b + n), v("ps%d" % b, 0, K), 0.5, A.mult)
+
+        def all_mid(j, a=0, c=13):
+            b, par = j // 2, j % 2
+            return lambda: tt(v("mall", E2 * b + 32 * a + par, E2 * b + 32 * c, 2), ind(v("dh", ND * b, ND * b + n0), sub(ends(t - 1)[par], a, c)),
+                              v("dh", ND * b + n0 + 16 * a, ND * b + n0 + 16 * c), A.add)
+
+        def halves(j, *first):
+            return [list(first) + [all_mid(j, 0, 6)], [all_mid(j, 6, 13)]]
+
+        evac = [lambda b=b: half_d(b) for b in range(4)]
         if t == 1:
-            side = [lambda: key1("keya", 0, 0, 14), lambda: key1("keyb", 26, 0, 14), lambda: key1("keyb", 26, 14, 26),
-                    lambda: dk("dka", "keya"), lambda: dk("dkb", "keyb"), lambda: quant(v("qv"), v("qvs"), v("vt"))]
+            side = [[[lambda: key1("keya", 0, 0, 14)], []], [[lambda: key1("keyb", 26, 0, 14)], []], [[lambda: key1("keyb", 26, 14, 26)], []],
+                    [[lambda: dk("dka", "keya")], []], [[lambda: dk("dkb", "keyb")], []], [[lambda: quant(v("qv"), v("qvs"), v("vt"))], []], [[], []]]
+        elif t == 2:
+            side = [[evac + [all_mid(0)], []], halves(1, lambda: next_key(0)), [[lambda: next_key(1)], []], halves(2, lambda: dk("dka", "key2")),
+                    halves(3, all_mid(4)), halves(5, all_mid(6)), halves(7)]
         else:
-            side = [lambda: next_key(t - 1, 0), lambda: next_key(t - 1, 1), lambda: next_ends(t - 1, 0, False),
-                    lambda: dk("dka", "key%d" % t), lambda: next_ends(t - 1, 1, False)]
-            if t < R:
-                side.append(keep_p)
+            side = [[evac[0:1] + [lambda: cp(v("lab"), v("lw", 70, 98))] + evac[1:4], []], halves(1, all_mid(2)), [[all_mid(3)], []],
+                    halves(4, all_mid(5)), halves(0, all_mid(6)), [[all_mid(7)], []], [[], []]]
         z = v("z")
         mid = v("tt", 32, 64)
         nbase, nulp, rulp = col("step", 6), col("step", 7), col("step", 8)
@@ -377,33 +389,39 @@ def rank_program(g, core, T, topo):
         for k in range(1, 8):
             s = col("cnt", k)
             if k == 1:
-                act(v("junk"), z, AF.Sign, bias=col("cv", BIAS1), acc=s)
+                z1, z2 = (v("z", 0, 288), v("z", 288, E2)) if t == 1 else (v("z", 0, E2, 2), v("z", 1, E2, 2))
+                m = 288 if t == 1 else K
+                act(v("junk", 0, m), z1, AF.Sign, bias=col("cv", BIAS1), acc=col("cnt", 9))
+                act(v("junk", m, E2), z2, AF.Sign, bias=col("cv", BIAS1), acc=s)
             elif k == 2:
                 act(v("junk"), z, AF.Sign, bias=bias(2), scale=col("cv", SC2), acc=s)
-                ts(v("tt", 31, 65, 33), v("ca", C2, C2 + 2), bias(2), A.mult)
             else:
                 act(v("junk"), z, AF.Sign, bias=bias(k), acc=s)
                 if k == 3:
                     ts(v("step", 0, 6), v("ca", SROW, SROW + 6), nbase, A.mult)
+                if k == 7:
+                    ts(v("res"), z, bias(7), A.add)
+            for f in side[k - 1][0]:
+                f()
+            if k == 1:
+                ts(v("k1"), v("k0"), col("cnt", 9), A.subtract)
+                ts(v("tl"), v("k1"), s, A.is_le, col("cv", BIAS1), A.mult)
+            elif k == 2:
+                ts(v("tl"), v("k0"), s, A.is_le, 1.0, A.add)
+                ts(v("tt", 31, 65, 33), v("ca", C2, C2 + 2), bias(2), A.mult)
+            else:
+                ts(v("tl"), v("k0"), s, A.is_le, col("step", k - 3), A.mult)
                 if k < 7:
                     ts(col("tt", 31), col("ca", CC + k - 3), nbase, A.mult, bias(k), A.add)
-                else:
-                    ts(v("res"), z, bias(7), A.add)
                 if k == 4:
                     ts(nulp, col("step", 5), -2.0 ** -115, A.min)
                 if k == 5:
                     ts(rulp, col("ca", RP1), nulp, A.mult)
                 if k == 6:
                     ts(col("tt", 64), col("ca", CC + 4), nbase, A.mult, rulp, A.add)
-            if side:
-                side.pop(0)()
-            if k == 1:
-                ts(v("tl"), v("k0"), s, A.is_le, col("cv", BIAS1), A.mult)
-            elif k == 2:
-                ts(v("tl"), v("k0"), s, A.is_le, 1.0, A.add)
-            else:
-                ts(v("tl"), v("k0"), s, A.is_le, col("step", k - 3), A.mult)
             tr(mid, v("tl"))
+            for f in side[k - 1][1]:
+                f()
             if k == 1:
                 red(bias(2), mid, A.min)
             elif k == 2:
@@ -414,9 +432,15 @@ def rank_program(g, core, T, topo):
             else:
                 red(bias(8), v("tt", 32, 65), A.add, negate=True)
         act(col("ulpb", 0), nulp, AF.Copy)
-        for b in range(4):
-            act(v("dh", ND * b + n0, ND * b + n), v("ps%d" % b, 0, n - n0), AF.Identity, scale=0.5)
-        if t > 1:
+        if t == 1:
+            for b in range(4):
+                act(v("dh", ND * b, ND * b + n), v("ps%d" % b, 0, n), AF.Identity, scale=0.5)
+        else:
+            if t == 2:
+                act(v("pa2", 1, E2, 2), v("ps4", 0, K), AF.Copy)
+                act(v("pb2", 0, E2, 2), v("ps4", 0, K), AF.Copy)
+            next_ends(t - 1, 0)
+            next_ends(t - 1, 1)
             y_out(n0, n)
         ts(v("c8"), v("res"), bias(8), A.is_ge, S15, A.mult)
         ts(col("tt8", 31), rulp, -1.0, A.mult, bias(8), A.subtract)
@@ -434,7 +458,7 @@ def rank_program(g, core, T, topo):
         act(v("junk"), v("cum"), AF.Sign, bias=col("cv", BCNT), acc=col("cnt", 8))
         ts(v("qn"), v("cum"), 1.5 * 2.0 ** 42, A.add, 1.5 * 2.0 ** 42, A.subtract)
         ec = col("ecu", 0)
-        lu = "lu%d" % t
+        x14 = v("xi", 0, 14)
         if t == 1:
             scan(v("sa"), v("dka"), v("qn"), 2.0 ** 23, A.add, A.min)
             ts(ec, col("cnt", 8), 0.5, A.mult, float(K), A.add)
@@ -443,55 +467,74 @@ def rank_program(g, core, T, topo):
             act(v("kq", 16, 32), ind(v("keyb"), ec), AF.Copy)
             tt(v("xi", 0, 16), ind(v("sa"), ec), v("kq", 0, 16), A.add)
             tt(v("xi", 16, 32), ind(v("sb"), ec), v("kq", 16, 32), A.add)
-            ts(v("li", 0, 32), v("xi"), 1023, A.bitwise_and)
-            cp(v(lu, 0, 32), v("li", 0, 32))
+            ts(v("li"), v("xi"), 1023, A.bitwise_and)
+            cp(v("lu1"), v("li"))
+            l1, l2 = ends(1)
+
+            def far_end(b, a, c):
+                return v("bg", K * b + 16 * a, K * b + 16 * c), ind(v("dh", ND * b, ND * b + n), sub(l2, a, c))
+
+            def midpoint(b, a, c):
+                tt(v("mt", 64 * a + b, 64 * c, 4), ind(v("dh", ND * b, ND * b + n), sub(l1, a, c)), v("bg", K * b + 16 * a, K * b + 16 * c), A.add)
+
+            cp(*far_end(3, 6, 13))
+            for b in range(3):
+                act(*far_end(b, 0, 13), AF.Copy)
+            act(*far_end(3, 0, 6), AF.Copy)
+            midpoint(3, 6, 13)
+            for b in range(3):
+                midpoint(b, 0, 13)
+            midpoint(3, 0, 6)
         else:
-            scan(v("sa", 0, K), v("dka", 0, K), v("qn", 0, K), 2.0 ** 23, A.add, A.min)
+            scan(v("sa", 0, K), v("dkc", 0, K), v("qn", 0, K), 2.0 ** 23, A.add, A.min)
             ts(ec, col("cnt", 8), 0.5, A.mult, float(K), A.add)
-            scan(v("sa", K, E2), v("dka", K, E2), v("qn", K, E2), col("sa", K - 1), A.add, A.min)
-            act(v("kq", 0, 16), ind(v("key%d" % t), ec), AF.Copy)
-            tt(v("xi", 0, 16), ind(v("sa"), ec), v("kq", 0, 16), A.add)
-            x14 = v("xi", 0, 14)
-            ts(v("li", 14, 28), x14, 11, A.arith_shift_right, 255, A.bitwise_and)
-            ts(v("li", 0, 14), x14, 1023, A.bitwise_and)
-            ts(v("li", 28, 42), x14, 10, A.arith_shift_right, 511, A.bitwise_and)
-            cp(v(lu), v("li"))
-        l1, l2, le = lists(t)
+            scan(v("sa", K, E2), v("dkc", K, E2), v("qn", K, E2), col("sa", K - 1), A.add, A.min)
+            tt(v("kq", 0, 16), ind(v("kilo"), ec), v("qrow"), A.add)
+            tt(v("xe"), ind(v("sa"), ec), v("kq", 0, 16), A.add)
+            ts(v("lu%d" % t), v("xe", 0, 14), 2.0 ** -10, A.mult)
+            if t == 2:
+                act(v("kq", 16, 32), ind(v("key2"), ec), AF.Copy)
+            for b in range(4):
+                src = ind(v("mall", E2 * b, E2 * (b + 1)), split(t))
+                if b % 2:
+                    cp(v("mt", b, 4 * K, 4), src)
+                else:
+                    act(v("mt", b, 4 * K, 4), src, AF.Copy)
 
-        def far_end(b, a, c):
-            return v("bg", K * b + 16 * a, K * b + 16 * c), ind(v("dh", ND * b + n0, ND * b + n), sub(l2, a, c))
-
-        def midpoint(b, a, c):
-            tt(v("mt", 64 * a + b, 64 * c, 4), ind(v("dh", ND * b, ND * b + n), sub(l1, a, c)), v("bg", K * b + 16 * a, K * b + 16 * c), A.add)
-
-        cp(*far_end(3, 6, 13))
-        for b in range(3):
-            act(*far_end(b, 0, 13), AF.Copy)
-        act(*far_end(3, 0, 6), AF.Copy)
-        midpoint(3, 6, 13)
-        for b in range(3):
-            midpoint(b, 0, 13)
-        midpoint(3, 0, 6)
-        quant(v("qm"), v("qms"), v("mt"))
-        for par in range(2):
+        def carry(par):
             if t == 1:
-                act(v("p" + "ab"[par] + "2", par, E2, 2), ind(v("ptab"), (l1, l2)[par]), AF.Copy)
+                act(v("p" + "ab"[par] + "2", par, E2, 2), ind(v("ptab"), ends(1)[par]), AF.Copy)
             elif t < R:
-                act(v("p" + "ab"[par] + "3", par, E2, 2), ind(v("p" + "ab"[par] + "2"), le), AF.Copy)
+                act(v("p" + "ab"[par] + "3", par, E2, 2), ind(v("p" + "ab"[par] + "2"), split(t)), AF.Copy)
             else:
-                next_ends(t, par, True)
-        if t == R:
-            dma("s", lambda: T.el[:], lambda: T.elb[0:128:16, :], [v("elb")], [])
+                next_ends(t, par)
+
+        quant(v("qm"), v("qms"), v("mt"))
+        carry(0)
+        if t == 2:
+            scan(v("sb"), v("dka"), v("qn"), 2.0 ** 23, A.add, A.min)
         for b in range(4):
             mm(v("ps%d" % b, 0, K), v("wq%d" % t, 128 * b, 128 * b + 128), v("wp%d" % t, 128 * b, 128 * b + 128), v("qm"), v("qms"))
         if t == 1:
             y_product(0, C)
         for b in range(4):
-            if b % 2 == 0:
+            if b % 2:
                 ts(v("rt", b, 4 * K, 4), v("ps%d" % b, 0, K), 0.03125, A.mult)
             else:
                 act(v("rt", b, 4 * K, 4), v("ps%d" % b, 0, K), AF.Identity, scale=0.03125)
+            if t == 2 and b == 1:
+                tt(v("xi", 0, 16), ind(v("sb"), ec), v("kq", 16, 32), A.add)
+        if t == 2:
+            ts(lw(0), x14, 1023, A.bitwise_and)
+            ts(lw(1), x14, 11, A.arith_shift_right, 255, A.bitwise_and)
+            ts(lw(2), x14, 10, A.arith_shift_right, 1, A.bitwise_and)
         quant(v("tab", n, n + K), v("tabs", n, n + K), v("rt"))
+        carry(1)
+        if t == R:
+            dma("s", lambda: T.el[:], lambda: T.elb[0:128:16, :], [v("elb")], [])
+        if t == 2:
+            ts(lw(1), lw(1), float(n0), A.add)
+            tt(lw(3), lw(1), lw(0), A.subtract)
         if t == 1:
             y_out(0, C)
         if t < R:
@@ -501,8 +544,11 @@ def rank_program(g, core, T, topo):
             for par in range(2):
                 tt(v("dif", K * par, K * par + K), v("p" + "ab"[par] + str(t + 1), par, E2, 2), v("ps4", 0, K), A.subtract)
                 act(v("z", par, E2, 2), v("dif", K * par, K * par + K), AF.Abs)
-            if t == R - 1:
+            if t == 2:
+                tt(lw(4), lw(3), lw(2), A.mult)
                 store(0, ND, "sssss")
+                tt(lw(5), lw(0), lw(4), A.add)
+                tt(lw(6), lw(1), lw(4), A.subtract)
         else:
             mm(v("ps6", 0, K), v("qv"), v("qvs"), *tabv(n, n + K))
             store(ND, NT, "sssaa")

@@ -10,16 +10,16 @@ X4, U8, BF, F32, I32, U16 = "float8_e4m3fn_x4", "uint8", "bfloat16", "float32", 
 
 SCRATCH = {}
 for _d, _bufs in (
-    (BF, {"xt": 4 * C, "ut": 512, "vt": 512, "et": 2048, "diag": 128, "z0": E2, "junk": E2, "c8": E2, "s8": E2, "res": E2,
-          "gt": E2, "ge": E2, "cap": E2, "cum": E2, "qn": E2, "ulpb": 2, "dh": 4 * ND, "bg": 4 * K, "mt": 4 * K, "rt": 4 * K,
-          "mall": 4 * E2}),
+    (BF, {"xt": 4 * C, "ut": 512, "vt": 512, "et": 2048, "diag": 128, "z0": E2, "junk": E2, "res": E2,
+          "gt": E2, "ge": E2, "cap": E2, "cum": E2, "qn": E2, "dh": 4 * ND, "mt": 4 * K, "rt": 4 * K,
+          "mall": 4 * E2, "da1": 4 * E2, "db1": 4 * E2, "da2": 4 * E2, "db2": 4 * E2}),
     (X4, {"wq": 512, "wq1": 512, "wq2": 512, "wq3": 512, "tab": NT, "qu": 128, "qg": 128, "qv": 128, "qe": 512, "qm": K}),
     (U8, {"wp": 512, "wp1": 512, "wp2": 512, "wp3": 512, "tabs": NT, "qus": 128, "qgs": 128, "qvs": 128, "qes": 512, "qms": K}),
-    (I32, {"eab": 52, "uoi": 8, "pidx": 1, "pbit": 2, "xi": 32, "li": 32, "lw": 98}),
-    (U16, {"eabu": 52, "uou": 8, "ecu": 2, "lu1": 32, "lu2": 14, "lu3": 14, "lab": 28}),
-    (F32, {"rh": 2, "num": E2, "kilo": E2, "half": 32, "k0": 32, "k1": 32, "k8": 32, "k8b": 32, "pw": 32, "ca": 24, "cv": 8,
-           "ptab": C, "pg": E2, "dif": E2, "z": E2, "cnt": 16, "bias": 16, "step": 10, "tl": 32, "tt": 96, "tl8": 64, "tt8": 96,
-           "keya": E2, "keyb": E2, "key2": E2, "dka": E2, "dkb": E2, "dkc": E2, "sa": E2, "sb": E2, "kq": 32, "qrow": 16, "xe": 16,
+    (I32, {"eab": 52, "uoi": 8, "pidx": 1, "pbit": 2}),
+    (U16, {"eabu": 52, "uou": 8, "ecu": 2, "lu1": 14, "lu2": 14, "lu3": 14}),
+    (F32, {"rh": 2, "num": E2, "kilo": E2, "half": 32, "k0": 32, "k1": 32, "k8b": 32, "pw": 32, "ca": 24, "cv": 8,
+           "ptab": C, "pa1": E2, "pb1": E2, "dif": E2, "z": E2, "cnt": 16, "bias": 16, "step": 10, "tl": 32, "tt": 96, "tl8": 64, "tt8": 96,
+           "a1": E2, "b1": E2, "dkc": E2, "sa": E2, "kq": 16, "qrow": 16, "xe": 16,
            "pa2": E2, "pb2": E2, "pa3": E2, "pb3": E2, "a2": E2, "b2": E2, "a3": E2, "b3": E2, "elb": 2 * E2, "ysb": NT}),
 ):
     for _n in _bufs:
@@ -27,7 +27,7 @@ for _d, _bufs in (
 for _i in range(7):
     SCRATCH["ps%d" % _i] = ("psum", [128, 512], F32)
 
-POOL = {"v": 44, "a": 30, "t": 14, "g": 16}
+POOL = {"v": 44, "a": 44, "t": 14, "g": 16}
 NDMA = 26
 SEMAPHORES = ["arr1", "arr2", "arr3", "sent"] + ["d%d" % _i for _i in range(NDMA)]
 for _q in POOL:
@@ -43,10 +43,6 @@ def v(name, a=0, b=None, s=1):
 
 def col(name, j):
     return v(name, j, j + 1)
-
-
-def sub(x, a, b):
-    return v(x[1], x[2] + a, x[2] + b)
 
 
 def ind(win, off, words=False):
@@ -257,8 +253,6 @@ def rank_program(g, core, T, topo):
     cp(v("rh"), v("pbit"))
     for b in range(4):
         ts(v("et", 513 * b, 512 * (b + 1), 4), v("diag"), 0.0, A.is_equal)
-    fill(col("dka", 0), 0.0)
-    fill(col("dkb", 0), 0.0)
     quant(v("qe"), v("qes"), v("et"))
 
     def lin(out, a, b):
@@ -274,7 +268,7 @@ def rank_program(g, core, T, topo):
     for k in range(5):
         lin(col("ca", SROW + k), 0, st[k])
     lin(col("ca", SROW + 5), 0, 2.0 ** -23)
-    lin(col("ca", RP1), 1, 1)
+    lin(col("ca", RP1), 1, 0.5)
     lin(col("ca", INITB), S15, 104.5 * S15)
     lin(col("z0", 0), S15, -103.5 * S15)
 
@@ -294,12 +288,6 @@ def rank_program(g, core, T, topo):
         iota(v(ra, 1, E2, 2), [[1, K]], C + t * K, 0)
         iota(v(rb, o, o + E2, 2), [[1, K]], C + t * K, 0)
 
-    def key1(name, o, a, b):
-        tt(v(name, 16 * a, 16 * b), ind(v("num", 0, C), v("eabu", o + a, o + b)), v("kilo", 16 * a, 16 * b), A.add)
-
-    def dk(name, key):
-        scan(v(name, 1, E2), v(key, 0, E2 - 1), v(key, 1, E2), 0.0, A.max, A.subtract)
-
     ts(v("pw", 0, 16), v("num", 1, 17), rr, A.is_gt, 0.5, A.max)
     ts(v("pw", 16, 32), v("num", 1, 17), rr, A.is_gt, 2.0 ** -6, A.max)
     ts(v("k0"), v("half"), hh, A.not_equal, 1000.0, A.mult)
@@ -311,6 +299,7 @@ def rank_program(g, core, T, topo):
     red(col("cv", SC2), v("pw", 0, 16), A.mult)
     add("v", lambda: V.tensor_copy(ap(v("qg")).bitcast(dt.uint32), ap(ind(v("qu"), v("uou"), True))), [ind(v("qu"), v("uou"))], [v("qg")])
     act(v("qgs"), ind(v("qus"), v("uou")), AF.Copy)
+    act(v("a1"), ind(v("num", 0, C), v("eabu", 0, 26)), AF.Copy)
     ts(col("cv", BIAS1), col("cv", T6), -2.0 ** 80, A.mult, col("cv", T6), A.mult)
     quant(v("tab", 0, C), v("tabs", 0, C), v("xt"))
     H = C // 2
@@ -318,30 +307,23 @@ def rank_program(g, core, T, topo):
     mm(v("ps6", 0, H), v("qg"), v("qgs"), *tabv(H, C))
     unpack(0, C)
     act(v("ptab", 0, H), v("ps4", 0, H), AF.Copy)
-    key1("keya", 0, 14, 26)
-    cp(v("ptab", H, C), v("ps6", 0, H))
-    ts(v("k8"), v("k0"), 2.0 ** 30, A.mult, K * S15, A.add)
-    tt(col("cv", BCNT), col("cv", M12), col("ca", RM), A.add)
-    cp(v("pg", 0, 128), ind(v("ptab"), v("eabu", 26, 34)))
-    for a, b in ((8, 18), (18, 26)):
-        act(v("pg", 16 * a, 16 * b), ind(v("ptab"), v("eabu", 26 + a, 26 + b)), AF.Copy)
     fill(v("z0", 1, E2), 0.0)
-    for a, b in ((0, 8), (8, 18), (18, 26)):
-        tt(v("dif", 16 * a, 16 * b), ind(v("ptab"), v("eabu", a, b)), v("pg", 16 * a, 16 * b), A.subtract)
-        act(v("z", 16 * a, 16 * b), v("dif", 16 * a, 16 * b), AF.Abs)
+    cp(v("ptab", H, C), v("ps6", 0, H))
+    tt(col("cv", BCNT), col("cv", M12), col("ca", RM), A.add)
     ts(v("qrow"), v("num", 0, 16), -6.0, A.add, 16 * S15, A.mult)
-
-    def ends(t):
-        return (v("lu1", 0, 13), v("lu1", 16, 29)) if t == 1 else (v("lab", 0, 13), v("lab", 14, 27))
+    cp(v("pb1", 0, 128), ind(v("ptab"), v("eabu", 26, 34)))
+    for a, b in ((8, 18), (18, 26)):
+        act(v("pb1", 16 * a, 16 * b), ind(v("ptab"), v("eabu", 26 + a, 26 + b)), AF.Copy)
+    cp(v("pa1", 0, 128), ind(v("ptab"), v("eabu", 0, 8)))
+    for a, b in ((0, 8), (8, 18), (18, 26)):
+        tt(v("dif", 16 * a, 16 * b), ind(v("ptab"), v("eabu", a, b)), v("pb1", 16 * a, 16 * b), A.subtract)
+        act(v("z", 16 * a, 16 * b), v("dif", 16 * a, 16 * b), AF.Abs)
 
     def split(t):
         return v("lu%d" % t, 0, 13)
 
-    def next_key(par):
-        tt(v("key2", par, E2, 2), ind(v("num", 0, C), ends(1)[par]), v("kilo", par, E2, 2), A.add)
-
     def next_ends(t, par):
-        src = ind(v("num", 0, C), ends(1)[par]) if t == 1 else ind(v("ab"[par] + str(t)), split(t))
+        src = ind(v("ab"[par] + str(t)), split(t))
         act(v("ab"[par] + str(t + 1), par, E2, 2) if t < R else v("elb", par * (E2 + 1), (par + 1) * E2, 2), src, AF.Copy)
 
     def y_product(a, b):
@@ -351,34 +333,59 @@ def rank_program(g, core, T, topo):
         act(v("ysb", a, b), v("ps5", 0, b - a), AF.Copy)
         store_y("s", a, b)
 
-    def lw(j):
-        return v("lw", 14 * j, 14 * j + 14)
+    def plane(name, b, a=0, s=1):
+        return v(name, E2 * b + a, E2 * (b + 1), s)
 
     for t in range(1, R + 1):
         n = C + (t - 1) * K
         n0 = 0 if t == 1 else n - K
 
+        def new_d(b):
+            return v("dh", ND * b + n0, ND * b + n)
+
         def half_d(b):
-            ts(v("dh", ND * b + n0, ND * b + n), v("ps%d" % b, 0, K), 0.5, A.mult)
+            if b % 2:
+                return lambda: act(new_d(b), v("ps%d" % b, 0, n - n0), AF.Identity, scale=0.5)
+            return lambda: ts(new_d(b), v("ps%d" % b, 0, n - n0), 0.5, A.mult)
 
-        def all_mid(j, a=0, c=13):
+        def end_d(par, b):
+            return lambda: act(plane("d%s1" % "ab"[par], b), ind(new_d(b), v("eabu", 26 * par, 26 * par + 26)), AF.Copy)
+
+        def mid1(b):
+            return lambda: tt(plane("mall", b), ind(new_d(b), v("eabu", 0, 26)), plane("db1", b), A.add)
+
+        def all_mid(j):
             b, par = j // 2, j % 2
-            return lambda: tt(v("mall", E2 * b + 32 * a + par, E2 * b + 32 * c, 2), ind(v("dh", ND * b, ND * b + n0), sub(ends(t - 1)[par], a, c)),
-                              v("dh", ND * b + n0 + 16 * a, ND * b + n0 + 16 * c), A.add)
+            return lambda: tt(plane("mall", b, par, 2), ind(plane("d%s%d" % ("ab"[par], t - 1), b), split(t - 1)), new_d(b), A.add)
 
-        def halves(j, *first):
-            return [list(first) + [all_mid(j, 0, 6)], [all_mid(j, 6, 13)]]
+        def carry_d(par, b):
+            name = "d%s2" % "ab"[par]
 
-        evac = [lambda b=b: half_d(b) for b in range(4)]
+            def f():
+                act(plane(name, b, par, 2), ind(plane("d%s1" % "ab"[par], b), split(1)), AF.Copy)
+                act(plane(name, b, 1 - par, 2), new_d(b), AF.Copy)
+            return f
+
+        def new_p(par):
+            return lambda: act(v("p%s2" % "ab"[par], 1 - par, E2, 2), v("ps4", 0, K), AF.Copy)
+
         if t == 1:
-            side = [[[lambda: key1("keya", 0, 0, 14)], []], [[lambda: key1("keyb", 26, 0, 14)], []], [[lambda: key1("keyb", 26, 14, 26)], []],
-                    [[lambda: dk("dka", "keya")], []], [[lambda: dk("dkb", "keyb")], []], [[lambda: quant(v("qv"), v("qvs"), v("vt"))], []], [[], []]]
-        elif t == 2:
-            side = [[evac + [all_mid(0)], []], halves(1, lambda: next_key(0)), [[lambda: next_key(1)], []], halves(2, lambda: dk("dka", "key2")),
-                    halves(3, all_mid(4)), halves(5, all_mid(6)), halves(7)]
+            side = [[half_d(0), half_d(2)], [lambda: cp(v("pa1", 128, E2), ind(v("ptab"), v("eabu", 8, 26)))],
+                    [lambda: quant(v("qv"), v("qvs"), v("vt"))], [mid1(0)], [mid1(1)], [mid1(2)], [], [mid1(3)]]
+            aside = [[half_d(1), half_d(3)], [end_d(1, 0)], [end_d(1, 1)], [end_d(1, 2)], [end_d(1, 3)], [end_d(0, 0)], [end_d(0, 1)],
+                     [end_d(0, 2), end_d(0, 3)]]
         else:
-            side = [[evac[0:1] + [lambda: cp(v("lab"), v("lw", 70, 98))] + evac[1:4], []], halves(1, all_mid(2)), [[all_mid(3)], []],
-                    halves(4, all_mid(5)), halves(0, all_mid(6)), [[all_mid(7)], []], [[], []]]
+            side = [[half_d(0), half_d(2)], [all_mid(0), all_mid(1)], [all_mid(2)], [all_mid(3), all_mid(4)], [all_mid(5), all_mid(6)],
+                    [all_mid(7)], [], []]
+            rows = [lambda: next_ends(t - 1, 0), lambda: next_ends(t - 1, 1)]
+            yo = [lambda: y_out(n0, n)]
+            if t == 2:
+                aside = [[half_d(1), half_d(3), new_p(0), new_p(1)], [carry_d(0, 0)] + yo, [carry_d(0, 1), rows[0]], [carry_d(0, 2)],
+                         [carry_d(0, 3)], [carry_d(1, 0), rows[1]], [carry_d(1, 1)], [carry_d(1, 2), carry_d(1, 3)]]
+                side[2].append(lambda: cp(v("b1", 0, 192), ind(v("num", 0, C), v("eabu", 26, 38))))
+                side[5].insert(0, lambda: cp(v("b1", 192, E2), ind(v("num", 0, C), v("eabu", 38, 52))))
+            else:
+                aside = [[half_d(1), half_d(3)] + yo, rows, [], [], [], [], [], []]
         z = v("z")
         mid = v("tt", 32, 64)
         nbase, nulp, rulp = col("step", 6), col("step", 7), col("step", 8)
@@ -401,7 +408,7 @@ def rank_program(g, core, T, topo):
                     ts(v("step", 0, 6), v("ca", SROW, SROW + 6), nbase, A.mult)
                 if k == 7:
                     ts(v("res"), z, bias(7), A.add)
-            for f in side[k - 1][0]:
+            for f in side[k - 1] + aside[k - 1]:
                 f()
             if k == 1:
                 ts(v("k1"), v("k0"), col("cnt", 9), A.subtract)
@@ -420,8 +427,6 @@ def rank_program(g, core, T, topo):
                 if k == 6:
                     ts(col("tt", 64), col("ca", CC + 4), nbase, A.mult, rulp, A.add)
             tr(mid, v("tl"))
-            for f in side[k - 1][1]:
-                f()
             if k == 1:
                 red(bias(2), mid, A.min)
             elif k == 2:
@@ -430,25 +435,17 @@ def rank_program(g, core, T, topo):
             elif k < 7:
                 red(bias(k + 1), v("tt", 31, 64), A.add)
             else:
-                red(bias(8), v("tt", 32, 65), A.add, negate=True)
-        act(col("ulpb", 0), nulp, AF.Copy)
-        if t == 1:
-            for b in range(4):
-                act(v("dh", ND * b, ND * b + n), v("ps%d" % b, 0, n), AF.Identity, scale=0.5)
-        else:
-            if t == 2:
-                act(v("pa2", 1, E2, 2), v("ps4", 0, K), AF.Copy)
-                act(v("pb2", 0, E2, 2), v("ps4", 0, K), AF.Copy)
-            next_ends(t - 1, 0)
-            next_ends(t - 1, 1)
-            y_out(n0, n)
-        ts(v("c8"), v("res"), bias(8), A.is_ge, S15, A.mult)
-        ts(col("tt8", 31), rulp, -1.0, A.mult, bias(8), A.subtract)
-        scan(v("s8"), v("c8"), v("c8"), 0.0, A.add, A.max)
-        tot = col("s8", E2 - 1)
-        ts(v("tl8", 0, 32), v("k8"), tot, A.is_le, col("ulpb", 0), A.mult)
-        ts(v("tl8", 32, 64), v("k8b"), tot, A.is_gt, tot, A.mult)
-        tr(v("tt8", 32, 96), v("tl8"))
+                red(bias(8), v("tt", 32, 65), A.add)
+        tot, tot2 = col("cnt", 10), col("cnt", 11)
+        act(v("junk"), v("res"), AF.Sign, bias=bias(8), acc=tot)
+        for f in side[7] + aside[7]:
+            f()
+        ts(col("tt8", 31), rulp, -1.0, A.mult, bias(8), A.add)
+        ts(tot2, tot, S15 / 2, A.mult, K * S15, A.add)
+        ts(v("tl8", 0, 32), v("k0"), tot, A.is_le, nulp, A.mult)
+        ts(v("tl8", 32, 64), v("k8b"), tot2, A.is_gt, tot2, A.mult)
+        tr(v("tt8", 32, 64), v("tl8", 0, 32))
+        tr(v("tt8", 64, 96), v("tl8", 32, 64))
         red(bias(10), v("tt8", 31, 64), A.add, negate=True)
         red(bias(11), v("tt8", 64, 96), A.max)
         ts(v("gt"), v("res"), bias(10), A.is_gt, -S15, A.mult)
@@ -458,61 +455,27 @@ def rank_program(g, core, T, topo):
         act(v("junk"), v("cum"), AF.Sign, bias=col("cv", BCNT), acc=col("cnt", 8))
         ts(v("qn"), v("cum"), 1.5 * 2.0 ** 42, A.add, 1.5 * 2.0 ** 42, A.subtract)
         ec = col("ecu", 0)
-        x14 = v("xi", 0, 14)
-        if t == 1:
-            scan(v("sa"), v("dka"), v("qn"), 2.0 ** 23, A.add, A.min)
-            ts(ec, col("cnt", 8), 0.5, A.mult, float(K), A.add)
-            scan(v("sb"), v("dkb"), v("qn"), 2.0 ** 23, A.add, A.min)
-            act(v("kq", 0, 16), ind(v("keya"), ec), AF.Copy)
-            act(v("kq", 16, 32), ind(v("keyb"), ec), AF.Copy)
-            tt(v("xi", 0, 16), ind(v("sa"), ec), v("kq", 0, 16), A.add)
-            tt(v("xi", 16, 32), ind(v("sb"), ec), v("kq", 16, 32), A.add)
-            ts(v("li"), v("xi"), 1023, A.bitwise_and)
-            cp(v("lu1"), v("li"))
-            l1, l2 = ends(1)
-
-            def far_end(b, a, c):
-                return v("bg", K * b + 16 * a, K * b + 16 * c), ind(v("dh", ND * b, ND * b + n), sub(l2, a, c))
-
-            def midpoint(b, a, c):
-                tt(v("mt", 64 * a + b, 64 * c, 4), ind(v("dh", ND * b, ND * b + n), sub(l1, a, c)), v("bg", K * b + 16 * a, K * b + 16 * c), A.add)
-
-            cp(*far_end(3, 6, 13))
-            for b in range(3):
-                act(*far_end(b, 0, 13), AF.Copy)
-            act(*far_end(3, 0, 6), AF.Copy)
-            midpoint(3, 6, 13)
-            for b in range(3):
-                midpoint(b, 0, 13)
-            midpoint(3, 0, 6)
-        else:
-            scan(v("sa", 0, K), v("dkc", 0, K), v("qn", 0, K), 2.0 ** 23, A.add, A.min)
-            ts(ec, col("cnt", 8), 0.5, A.mult, float(K), A.add)
-            scan(v("sa", K, E2), v("dkc", K, E2), v("qn", K, E2), col("sa", K - 1), A.add, A.min)
-            tt(v("kq", 0, 16), ind(v("kilo"), ec), v("qrow"), A.add)
-            tt(v("xe"), ind(v("sa"), ec), v("kq", 0, 16), A.add)
-            ts(v("lu%d" % t), v("xe", 0, 14), 2.0 ** -10, A.mult)
-            if t == 2:
-                act(v("kq", 16, 32), ind(v("key2"), ec), AF.Copy)
-            for b in range(4):
-                src = ind(v("mall", E2 * b, E2 * (b + 1)), split(t))
-                if b % 2:
-                    cp(v("mt", b, 4 * K, 4), src)
-                else:
-                    act(v("mt", b, 4 * K, 4), src, AF.Copy)
+        scan(v("sa", 0, K), v("dkc", 0, K), v("qn", 0, K), 2.0 ** 23, A.add, A.min)
+        ts(ec, col("cnt", 8), 0.5, A.mult, float(K), A.add)
+        scan(v("sa", K, E2), v("dkc", K, E2), v("qn", K, E2), col("sa", K - 1), A.add, A.min)
+        tt(v("kq"), ind(v("kilo"), ec), v("qrow"), A.add)
+        tt(v("xe"), ind(v("sa"), ec), v("kq"), A.add)
+        ts(v("lu%d" % t), v("xe", 0, 14), 2.0 ** -10, A.mult)
+        for b in range(4):
+            src = ind(plane("mall", b), split(t))
+            if b % 2:
+                cp(v("mt", b, 4 * K, 4), src)
+            else:
+                act(v("mt", b, 4 * K, 4), src, AF.Copy)
 
         def carry(par):
-            if t == 1:
-                act(v("p" + "ab"[par] + "2", par, E2, 2), ind(v("ptab"), ends(1)[par]), AF.Copy)
-            elif t < R:
-                act(v("p" + "ab"[par] + "3", par, E2, 2), ind(v("p" + "ab"[par] + "2"), split(t)), AF.Copy)
+            if t < R:
+                act(v("p%s%d" % ("ab"[par], t + 1), par, E2, 2), ind(v("p%s%d" % ("ab"[par], t)), split(t)), AF.Copy)
             else:
                 next_ends(t, par)
 
         quant(v("qm"), v("qms"), v("mt"))
         carry(0)
-        if t == 2:
-            scan(v("sb"), v("dka"), v("qn"), 2.0 ** 23, A.add, A.min)
         for b in range(4):
             mm(v("ps%d" % b, 0, K), v("wq%d" % t, 128 * b, 128 * b + 128), v("wp%d" % t, 128 * b, 128 * b + 128), v("qm"), v("qms"))
         if t == 1:
@@ -522,19 +485,10 @@ def rank_program(g, core, T, topo):
                 ts(v("rt", b, 4 * K, 4), v("ps%d" % b, 0, K), 0.03125, A.mult)
             else:
                 act(v("rt", b, 4 * K, 4), v("ps%d" % b, 0, K), AF.Identity, scale=0.03125)
-            if t == 2 and b == 1:
-                tt(v("xi", 0, 16), ind(v("sb"), ec), v("kq", 16, 32), A.add)
-        if t == 2:
-            ts(lw(0), x14, 1023, A.bitwise_and)
-            ts(lw(1), x14, 11, A.arith_shift_right, 255, A.bitwise_and)
-            ts(lw(2), x14, 10, A.arith_shift_right, 1, A.bitwise_and)
         quant(v("tab", n, n + K), v("tabs", n, n + K), v("rt"))
         carry(1)
         if t == R:
             dma("s", lambda: T.el[:], lambda: T.elb[0:128:16, :], [v("elb")], [])
-        if t == 2:
-            ts(lw(1), lw(1), float(n0), A.add)
-            tt(lw(3), lw(1), lw(0), A.subtract)
         if t == 1:
             y_out(0, C)
         if t < R:
@@ -545,10 +499,7 @@ def rank_program(g, core, T, topo):
                 tt(v("dif", K * par, K * par + K), v("p" + "ab"[par] + str(t + 1), par, E2, 2), v("ps4", 0, K), A.subtract)
                 act(v("z", par, E2, 2), v("dif", K * par, K * par + K), AF.Abs)
             if t == 2:
-                tt(lw(4), lw(3), lw(2), A.mult)
                 store(0, ND, "sssss")
-                tt(lw(5), lw(0), lw(4), A.add)
-                tt(lw(6), lw(1), lw(4), A.subtract)
         else:
             mm(v("ps6", 0, K), v("qv"), v("qvs"), *tabv(n, n + K))
             store(ND, NT, "sssaa")

@@ -11,10 +11,10 @@ X4, U8, BF, F32, I32, U16 = "float8_e4m3fn_x4", "uint8", "bfloat16", "float32", 
 SCRATCH = {}
 for _d, _bufs in (
     (BF, {"xt": 4 * C, "ut": 512, "vt": 512, "et": 2048, "diag": 128, "z0": E2, "junk": E2, "res": E2,
-          "gt": E2, "ge": E2, "cap": E2, "cum": E2, "qn": E2, "dh": 4 * ND, "mt": 4 * K, "rt": 4 * K,
+          "gt": E2, "ge": E2, "cap": E2, "cum": E2, "qn": E2, "dh": 4 * ND, "mt": 1024, "rt": 1024,
           "mall": 4 * E2, "da1": 4 * E2, "db1": 4 * E2, "da2": 4 * E2, "db2": 4 * E2}),
-    (X4, {"wq": 512, "wq1": 512, "wq2": 512, "wq3": 512, "tab": NT, "qu": 128, "qg": 128, "qv": 128, "qe": 512, "qm": K}),
-    (U8, {"wp": 512, "wp1": 512, "wp2": 512, "wp3": 512, "tabs": NT, "qus": 128, "qgs": 128, "qvs": 128, "qes": 512, "qms": K}),
+    (X4, {"wq": 512, "wq1": 512, "wq2": 512, "wq3": 512, "tab": NT + 48, "qu": 128, "qg": 128, "qv": 128, "qe": 512, "qm": 256}),
+    (U8, {"wp": 512, "wp1": 512, "wp2": 512, "wp3": 512, "tabs": NT + 48, "qus": 128, "qgs": 128, "qvs": 128, "qes": 512, "qms": 256}),
     (I32, {"eab": 52, "uoi": 8, "pidx": 1, "pbit": 2}),
     (U16, {"eabu": 52, "uou": 8, "ecu": 2, "lu1": 14, "lu2": 14, "lu3": 14}),
     (F32, {"rh": 2, "num": E2, "kilo": E2, "half": 32, "k0": 32, "k1": 32, "k8b": 32, "pw": 32, "ca": 24, "cv": 8,
@@ -24,7 +24,7 @@ for _d, _bufs in (
 ):
     for _n in _bufs:
         SCRATCH[_n] = ("sbuf", [128, _bufs[_n]], _d)
-for _i in range(7):
+for _i in range(8):
     SCRATCH["ps%d" % _i] = ("psum", [128, 512], F32)
 
 POOL = {"v": 44, "a": 44, "t": 14, "g": 16}
@@ -218,21 +218,25 @@ def rank_program(g, core, T, topo):
     def store_y(q, a, b):
         dma(q, lambda: T.y[:, a:b], lambda: T.ysb[:, a:b], [v("ysb", a, b)], [])
 
-    def store(a, b, qs):
-        dma(qs[0], lambda: T.oc[:, 4 * a:4 * b], lambda: codes(v("tab", a, b)), [v("tab", a, b)], [])
+    def store_codes(q, a, b):
+        dma(q, lambda: T.oc[:, 4 * a:4 * b], lambda: codes(v("tab", a, b)), [v("tab", a, b)], [])
+
+    def store_scales(qs, a, b):
         for k in range(4):
-            dma(qs[1 + k], lambda k=k: T.osc[4 * k:4 * k + 4, a:b], lambda k=k: T.tabs[32 * k:32 * k + 4, a:b], [v("tabs", a, b)], [])
+            dma(qs[k], lambda k=k: T.osc[4 * k:4 * k + 4, a:b], lambda k=k: T.tabs[32 * k:32 * k + 4, a:b], [v("tabs", a, b)], [])
 
     def unpack(a, b):
         for i in range(4):
-            mm(v("ps%d" % i, 0, b - a), v("qe", 128 * i, 128 * i + 128), v("qes", 128 * i, 128 * i + 128), *tabv(a, b))
+            mm(v("ps%d" % (4 + i), 0, b - a), v("qe", 128 * i, 128 * i + 128), v("qes", 128 * i, 128 * i + 128), *tabv(a, b))
 
     rr, hh = col("rh", 0), col("rh", 1)
     C2, CC, RP1, INITB, RM, SROW = 0, 2, 7, 8, 9, 12
     SC2, T6, BIAS1, M12, BCNT = 0, 1, 2, 3, 4
+    H = C // 2
 
-    dma("s", lambda: T.xt[:], lambda: T.x[:], [], [v("xt")])
     dma("a", lambda: T.ut[:], lambda: T.u[:], [], [v("ut")])
+    dma("s", lambda: T.xt[:, 0:4 * H], lambda: T.x[:, 0:4 * H], [], [v("xt", 0, 4 * H)])
+    dma("s", lambda: T.xt[:, 4 * H:4 * C], lambda: T.x[:, 4 * H:4 * C], [], [v("xt", 4 * H, 4 * C)])
     dma("a", lambda: T.eab[:, 0:26], lambda: T.ea[:], [], [v("eab", 0, 26)])
     dma("a", lambda: T.eab[:, 26:52], lambda: T.eb[:], [], [v("eab", 26, 52)])
     dma("s", lambda: codes(v("wq")), lambda: T.wc[:], [v("xt")], [v("wq")])
@@ -250,27 +254,31 @@ def rank_program(g, core, T, topo):
     ts(col("pbit", 0), v("pidx"), 15, A.bitwise_and)
     ts(col("pbit", 1), v("pidx"), 4, A.arith_shift_right, 1, A.bitwise_and)
     cp(v("uou"), v("uoi"))
-    cp(v("rh"), v("pbit"))
     for b in range(4):
         ts(v("et", 513 * b, 512 * (b + 1), 4), v("diag"), 0.0, A.is_equal)
-    quant(v("qe"), v("qes"), v("et"))
+        if b == 1:
+            cp(v("rh"), v("pbit"))
 
     def lin(out, a, b):
         act(out, rr, AF.Identity, bias=float(b), scale=float(a))
 
     st = [2.0 ** (-4 * (k + 1)) for k in range(5)]
+    quant(v("qu"), v("qus"), v("ut"))
+    for k in range(5):
+        lin(col("ca", SROW + k), 0, st[k])
+    lin(col("ca", SROW + 5), 0, 2.0 ** -23)
+    act(v("qgs"), ind(v("qus"), v("uou")), AF.Copy)
     lin(col("ca", RM), -S15, -89 * S15)
     lin(col("ca", C2), 1 / 32, 0.5)
     lin(col("ca", C2 + 1), 0, 0.5)
     for k in range(4):
         lin(col("ca", CC + k), st[k + 1] - st[k], -st[k])
-    lin(col("ca", CC + 4), -st[4], -st[4])
-    for k in range(5):
-        lin(col("ca", SROW + k), 0, st[k])
-    lin(col("ca", SROW + 5), 0, 2.0 ** -23)
-    lin(col("ca", RP1), 1, 0.5)
-    lin(col("ca", INITB), S15, 104.5 * S15)
-    lin(col("z0", 0), S15, -103.5 * S15)
+
+    def late_constants():
+        lin(col("ca", CC + 4), -st[4], -st[4])
+        lin(col("ca", RP1), 1, 0.5)
+        lin(col("ca", INITB), S15, 104.5 * S15)
+        lin(col("z0", 0), S15, -103.5 * S15)
 
     sent = [0]
     for t in range(1, R + 1):
@@ -288,53 +296,64 @@ def rank_program(g, core, T, topo):
         iota(v(ra, 1, E2, 2), [[1, K]], C + t * K, 0)
         iota(v(rb, o, o + E2, 2), [[1, K]], C + t * K, 0)
 
-    ts(v("pw", 0, 16), v("num", 1, 17), rr, A.is_gt, 0.5, A.max)
+    quant(*tabv(0, H), v("xt", 0, 4 * H))
+    add("v", lambda: V.tensor_copy(ap(v("qg")).bitcast(dt.uint32), ap(ind(v("qu"), v("uou"), True))), [ind(v("qu"), v("uou"))], [v("qg")])
+    quant(*tabv(H, C), v("xt", 4 * H, 4 * C))
+    mm(v("ps0", 0, H), v("qg"), v("qgs"), *tabv(0, H))
+    mm(v("ps1", 0, H), v("qg"), v("qgs"), *tabv(H, C))
+    act(v("ptab", 0, H), v("ps0", 0, H), AF.Copy)
+    late_constants()
     ts(v("pw", 16, 32), v("num", 1, 17), rr, A.is_gt, 2.0 ** -6, A.max)
+    ts(v("pw", 0, 16), v("num", 1, 17), rr, A.is_gt, 0.5, A.max)
     ts(v("k0"), v("half"), hh, A.not_equal, 1000.0, A.mult)
     ts(v("k8b"), v("half"), hh, A.is_equal, K * S15, A.mult)
-    ts(col("cv", M12), rr, 12.0, A.min, 16 * S15, A.mult)
-    red(col("cv", T6), v("pw", 16, 32), A.mult)
     cp(v("eabu"), v("eab"))
-    quant(v("qu"), v("qus"), v("ut"))
+    red(col("cv", T6), v("pw", 16, 32), A.mult)
+    cp(v("ptab", H, C), v("ps1", 0, H))
     red(col("cv", SC2), v("pw", 0, 16), A.mult)
-    add("v", lambda: V.tensor_copy(ap(v("qg")).bitcast(dt.uint32), ap(ind(v("qu"), v("uou"), True))), [ind(v("qu"), v("uou"))], [v("qg")])
-    act(v("qgs"), ind(v("qus"), v("uou")), AF.Copy)
-    act(v("a1"), ind(v("num", 0, C), v("eabu", 0, 26)), AF.Copy)
+    ts(col("cv", M12), rr, 12.0, A.min, 16 * S15, A.mult)
     ts(col("cv", BIAS1), col("cv", T6), -2.0 ** 80, A.mult, col("cv", T6), A.mult)
-    quant(v("tab", 0, C), v("tabs", 0, C), v("xt"))
-    H = C // 2
-    mm(v("ps4", 0, H), v("qg"), v("qgs"), *tabv(0, H))
-    mm(v("ps6", 0, H), v("qg"), v("qgs"), *tabv(H, C))
-    unpack(0, C)
-    act(v("ptab", 0, H), v("ps4", 0, H), AF.Copy)
-    fill(v("z0", 1, E2), 0.0)
-    cp(v("ptab", H, C), v("ps6", 0, H))
-    tt(col("cv", BCNT), col("cv", M12), col("ca", RM), A.add)
-    ts(v("qrow"), v("num", 0, 16), -6.0, A.add, 16 * S15, A.mult)
     cp(v("pb1", 0, 128), ind(v("ptab"), v("eabu", 26, 34)))
     for a, b in ((8, 18), (18, 26)):
         act(v("pb1", 16 * a, 16 * b), ind(v("ptab"), v("eabu", 26 + a, 26 + b)), AF.Copy)
-    cp(v("pa1", 0, 128), ind(v("ptab"), v("eabu", 0, 8)))
+    cp(v("pa1", 0, 96), ind(v("ptab"), v("eabu", 0, 6)))
     for a, b in ((0, 8), (8, 18), (18, 26)):
         tt(v("dif", 16 * a, 16 * b), ind(v("ptab"), v("eabu", a, b)), v("pb1", 16 * a, 16 * b), A.subtract)
         act(v("z", 16 * a, 16 * b), v("dif", 16 * a, 16 * b), AF.Abs)
+    quant(v("qe"), v("qes"), v("et"))
+    unpack(0, C)
 
-    def split(t):
-        return v("lu%d" % t, 0, 13)
+    HS = ((0, 128), (128, K))
+
+    def split(t, a=0, c=K):
+        return v("lu%d" % t, a // 16, c // 16)
 
     def next_ends(t, par):
         src = ind(v("ab"[par] + str(t)), split(t))
         act(v("ab"[par] + str(t + 1), par, E2, 2) if t < R else v("elb", par * (E2 + 1), (par + 1) * E2, 2), src, AF.Copy)
 
     def y_product(a, b):
-        mm(v("ps5", 0, b - a), v("qv"), v("qvs"), *tabv(a, b))
+        mm(v("ps2", 0, b - a), v("qv"), v("qvs"), *tabv(a, b))
 
     def y_out(a, b):
-        act(v("ysb", a, b), v("ps5", 0, b - a), AF.Copy)
+        act(v("ysb", a, b), v("ps2", 0, b - a), AF.Copy)
         store_y("s", a, b)
 
     def plane(name, b, a=0, s=1):
         return v(name, E2 * b + a, E2 * (b + 1), s)
+
+    def first_row(par):
+        return lambda: act(v("ab"[par] + "1"), ind(v("num", 0, C), v("eabu", 26 * par, 26 * par + 26)), AF.Copy)
+
+    def rows(t):
+        return [lambda: next_ends(t, 0), lambda: next_ends(t, 1)]
+
+    def list_constants():
+        tt(col("cv", BCNT), col("cv", M12), col("ca", RM), A.add)
+        ts(v("qrow"), v("num", 0, 16), -6.0, A.add, 16 * S15, A.mult)
+
+    def first_p(a, b):
+        return lambda: cp(v("pa1", 16 * a, 16 * b), ind(v("ptab"), v("eabu", a, b)))
 
     for t in range(1, R + 1):
         n = C + (t - 1) * K
@@ -345,8 +364,8 @@ def rank_program(g, core, T, topo):
 
         def half_d(b):
             if b % 2:
-                return lambda: act(new_d(b), v("ps%d" % b, 0, n - n0), AF.Identity, scale=0.5)
-            return lambda: ts(new_d(b), v("ps%d" % b, 0, n - n0), 0.5, A.mult)
+                return lambda: act(new_d(b), v("ps%d" % (4 + b), 0, n - n0), AF.Identity, scale=0.5)
+            return lambda: ts(new_d(b), v("ps%d" % (4 + b), 0, n - n0), 0.5, A.mult)
 
         def end_d(par, b):
             return lambda: act(plane("d%s1" % "ab"[par], b), ind(new_d(b), v("eabu", 26 * par, 26 * par + 26)), AF.Copy)
@@ -367,25 +386,27 @@ def rank_program(g, core, T, topo):
             return f
 
         def new_p(par):
-            return lambda: act(v("p%s2" % "ab"[par], 1 - par, E2, 2), v("ps4", 0, K), AF.Copy)
+            def f():
+                for h, (a, c) in enumerate(HS):
+                    act(v("p%s2" % "ab"[par], 2 * a + 1 - par, 2 * c, 2), v("ps%d" % h, 0, c - a), AF.Copy)
+            return f
 
         if t == 1:
-            side = [[half_d(0), half_d(2)], [lambda: cp(v("pa1", 128, E2), ind(v("ptab"), v("eabu", 8, 26)))],
-                    [lambda: quant(v("qv"), v("qvs"), v("vt"))], [mid1(0)], [mid1(1)], [mid1(2)], [], [mid1(3)]]
+            side = [[lambda: fill(v("z0", 1, E2), 0.0)], [half_d(0), half_d(2), lambda: fill(v("mt", 4 * K, 1024), 0.0)],
+                    [first_p(6, 26), lambda: fill(v("rt", 4 * K, 1024), 0.0)],
+                    [mid1(0), list_constants], [mid1(1), lambda: quant(v("qv"), v("qvs"), v("vt")), lambda: y_product(0, C)], [mid1(2)],
+                    [lambda: cp(v("ysb", 0, C), v("ps2", 0, C)), lambda: store_y("s", 0, C)], [mid1(3)]]
             aside = [[half_d(1), half_d(3)], [end_d(1, 0)], [end_d(1, 1)], [end_d(1, 2)], [end_d(1, 3)], [end_d(0, 0)], [end_d(0, 1)],
                      [end_d(0, 2), end_d(0, 3)]]
         else:
-            side = [[half_d(0), half_d(2)], [all_mid(0), all_mid(1)], [all_mid(2)], [all_mid(3), all_mid(4)], [all_mid(5), all_mid(6)],
-                    [all_mid(7)], [], []]
-            rows = [lambda: next_ends(t - 1, 0), lambda: next_ends(t - 1, 1)]
             yo = [lambda: y_out(n0, n)]
+            side = [[half_d(0), half_d(2)], [all_mid(0), all_mid(1)], [all_mid(2)], [all_mid(3), all_mid(4)], [all_mid(5)],
+                    [all_mid(6)], [], [all_mid(7)]]
             if t == 2:
-                aside = [[half_d(1), half_d(3), new_p(0), new_p(1)], [carry_d(0, 0)] + yo, [carry_d(0, 1), rows[0]], [carry_d(0, 2)],
-                         [carry_d(0, 3)], [carry_d(1, 0), rows[1]], [carry_d(1, 1)], [carry_d(1, 2), carry_d(1, 3)]]
-                side[2].append(lambda: cp(v("b1", 0, 192), ind(v("num", 0, C), v("eabu", 26, 38))))
-                side[5].insert(0, lambda: cp(v("b1", 192, E2), ind(v("num", 0, C), v("eabu", 38, 52))))
+                aside = [[half_d(1), half_d(3), new_p(0)], [carry_d(0, 0)] + yo, [carry_d(0, 1), new_p(1)], [carry_d(0, 2)],
+                         [carry_d(0, 3)], [carry_d(1, 0)], [carry_d(1, 1)], [carry_d(1, 2), carry_d(1, 3)]]
             else:
-                aside = [[half_d(1), half_d(3)] + yo, rows, [], [], [], [], [], []]
+                aside = [[half_d(1), half_d(3)] + yo, [first_row(0)], [first_row(1)], rows(1), rows(2), [], [], []]
         z = v("z")
         mid = v("tt", 32, 64)
         nbase, nulp, rulp = col("step", 6), col("step", 7), col("step", 8)
@@ -396,10 +417,8 @@ def rank_program(g, core, T, topo):
         for k in range(1, 8):
             s = col("cnt", k)
             if k == 1:
-                z1, z2 = (v("z", 0, 288), v("z", 288, E2)) if t == 1 else (v("z", 0, E2, 2), v("z", 1, E2, 2))
-                m = 288 if t == 1 else K
-                act(v("junk", 0, m), z1, AF.Sign, bias=col("cv", BIAS1), acc=col("cnt", 9))
-                act(v("junk", m, E2), z2, AF.Sign, bias=col("cv", BIAS1), acc=s)
+                act(v("junk", 0, K), v("z", 0, K), AF.Sign, bias=col("cv", BIAS1), acc=col("cnt", 9))
+                act(v("junk", K, E2), v("z", K, E2), AF.Sign, bias=col("cv", BIAS1), acc=s)
             elif k == 2:
                 act(v("junk"), z, AF.Sign, bias=bias(2), scale=col("cv", SC2), acc=s)
             else:
@@ -461,12 +480,14 @@ def rank_program(g, core, T, topo):
         tt(v("kq"), ind(v("kilo"), ec), v("qrow"), A.add)
         tt(v("xe"), ind(v("sa"), ec), v("kq"), A.add)
         ts(v("lu%d" % t), v("xe", 0, 14), 2.0 ** -10, A.mult)
-        for b in range(4):
-            src = ind(plane("mall", b), split(t))
+
+        def pick(h, b):
+            a, c = HS[h]
+            src, out = ind(plane("mall", b), split(t, a, c)), v("mt", 4 * a + b, 4 * c, 4)
             if b % 2:
-                cp(v("mt", b, 4 * K, 4), src)
+                cp(out, src)
             else:
-                act(v("mt", b, 4 * K, 4), src, AF.Copy)
+                act(out, src, AF.Copy)
 
         def carry(par):
             if t < R:
@@ -474,36 +495,63 @@ def rank_program(g, core, T, topo):
             else:
                 next_ends(t, par)
 
-        quant(v("qm"), v("qms"), v("mt"))
-        carry(0)
-        for b in range(4):
-            mm(v("ps%d" % b, 0, K), v("wq%d" % t, 128 * b, 128 * b + 128), v("wp%d" % t, 128 * b, 128 * b + 128), v("qm"), v("qms"))
-        if t == 1:
-            y_product(0, C)
-        for b in range(4):
-            if b % 2:
-                ts(v("rt", b, 4 * K, 4), v("ps%d" % b, 0, K), 0.03125, A.mult)
+        def layer(h):
+            a = 128 * h
+            quant(v("qm", a, a + 128), v("qms", a, a + 128), v("mt", 4 * a, 4 * a + 512))
+            for b in range(4):
+                mm(v("ps%d" % (4 * h + b), 0, 128), v("wq%d" % t, 128 * b, 128 * b + 128), v("wp%d" % t, 128 * b, 128 * b + 128),
+                   v("qm", a, a + 128), v("qms", a, a + 128))
+
+        def evac(h, b):
+            a, c = HS[h]
+            out, src = v("rt", 4 * a + b, 4 * c, 4), v("ps%d" % (4 * h + b), 0, c - a)
+            if b % 2 and (h == 0 or b == 3):
+                ts(out, src, 0.03125, A.mult)
             else:
-                act(v("rt", b, 4 * K, 4), v("ps%d" % b, 0, K), AF.Identity, scale=0.03125)
-        quant(v("tab", n, n + K), v("tabs", n, n + K), v("rt"))
-        carry(1)
-        if t == R:
-            dma("s", lambda: T.el[:], lambda: T.elb[0:128:16, :], [v("elb")], [])
-        if t == 1:
-            y_out(0, C)
+                act(out, src, AF.Identity, scale=0.03125)
+
+        def new_cols(h):
+            a = 128 * h
+            quant(*tabv(n + a, n + a + 128), v("rt", 4 * a, 4 * a + 512))
+            by = ("qg", "qgs") if t < R else ("qv", "qvs")
+            mm(v("ps%d" % h, 0, 128), v(by[0]), v(by[1]), *tabv(n + a, n + a + 128))
+
+        def scores(h):
+            a, c = HS[h]
+            for par in range(2):
+                tt(v("dif", 2 * a + par, 2 * c, 2), v("p" + "ab"[par] + str(t + 1), 2 * a + par, 2 * c, 2), v("ps%d" % h, 0, c - a), A.subtract)
+            act(v("z", 2 * a, 2 * c), v("dif", 2 * a, 2 * c), AF.Abs)
+
+        for h in range(2):
+            for b in range(4):
+                pick(h, b)
+        layer(0)
+        carry(0)
+        layer(1)
+        for b in range(4):
+            evac(0, b)
+        evac(1, 3)
+        new_cols(0)
+        for b in range(3):
+            evac(1, b)
         if t < R:
-            mm(v("ps4", 0, K), v("qg"), v("qgs"), *tabv(n, n + K))
+            carry(1)
+            new_cols(1)
             unpack(n, n + K)
             y_product(n, n + K)
-            for par in range(2):
-                tt(v("dif", K * par, K * par + K), v("p" + "ab"[par] + str(t + 1), par, E2, 2), v("ps4", 0, K), A.subtract)
-                act(v("z", par, E2, 2), v("dif", K * par, K * par + K), AF.Abs)
+            scores(0)
+            scores(1)
             if t == 2:
-                store(0, ND, "sssss")
+                store_codes("s", 0, ND)
+                store_scales("ssss", 0, ND)
         else:
-            mm(v("ps6", 0, K), v("qv"), v("qvs"), *tabv(n, n + K))
-            store(ND, NT, "sssaa")
-            cp(v("ysb", ND, NT), v("ps6", 0, K))
-            store_y("a", ND, NT)
+            new_cols(1)
+            carry(1)
+            store_codes("s", ND, NT)
+            cp(v("ysb", ND, ND + 128), v("ps0", 0, 128))
+            dma("a", lambda: T.el[:], lambda: T.elb[0:128:16, :], [v("elb")], [])
+            store_scales("ssaa", ND, NT)
+            cp(v("ysb", ND + 128, NT), v("ps1", 0, K - 128))
+            store_y("s", ND, NT)
     emit()
     g.wait_ge(T.sem.sent, sent[0])

@@ -5,21 +5,24 @@ C, K, R = 320, 208, 3
 E2 = 2 * K
 NT = C + R * K
 ND = C + (R - 1) * K
-S15 = 2.0 ** 15
+UN = 32.0
+TOP = 2.0 ** 70
+PAD = 2.0 ** 90
 X4, U8, BF, F32, I32, U16 = "float8_e4m3fn_x4", "uint8", "bfloat16", "float32", "int32", "uint16"
 
 SCRATCH = {}
 for _d, _bufs in (
-    (BF, {"xt": 4 * C, "ut": 512, "vt": 512, "et": 2048, "diag": 128, "z0": E2, "junk": E2, "res": E2,
-          "gt": E2, "ge": E2, "cap": E2, "cum": E2, "qn": E2, "dh": 4 * ND, "mt": 1024, "rt": 1024,
+    (BF, {"xt": 4 * C, "ut": 512, "vt": 512, "et": 2048, "diag": 128, "junk": E2 + 2, "res": E2 + 2, "zb": E2 + 2, "fl": E2, "sc": K,
+          "gt": E2 + 2, "ge": E2, "cap": E2, "cum": E2, "qn": E2, "dh": 4 * C, "mt": 1024, "rt": 1024, "tlb": 96, "ttb": 324,
           "mall": 4 * E2, "da1": 4 * E2, "db1": 4 * E2, "da2": 4 * E2, "db2": 4 * E2}),
     (X4, {"wq": 512, "wq1": 512, "wq2": 512, "wq3": 512, "tab": NT + 48, "qu": 128, "qg": 128, "qv": 128, "qe": 512, "qm": 256}),
     (U8, {"wp": 512, "wp1": 512, "wp2": 512, "wp3": 512, "tabs": NT + 48, "qus": 128, "qgs": 128, "qvs": 128, "qes": 512, "qms": 256}),
-    (I32, {"eab": 52, "uoi": 8, "pidx": 1, "pbit": 2}),
-    (U16, {"eabu": 52, "uou": 8, "ecu": 2, "lu1": 14, "lu2": 14, "lu3": 14}),
-    (F32, {"rh": 2, "num": E2, "kilo": E2, "half": 32, "k0": 32, "k1": 32, "k8b": 32, "pw": 32, "ca": 24, "cv": 8,
-           "ptab": C, "pa1": E2, "pb1": E2, "dif": E2, "z": E2, "cnt": 16, "bias": 16, "step": 10, "tl": 32, "tt": 96, "tl8": 64, "tt8": 96,
-           "a1": E2, "b1": E2, "dkc": E2, "sa": E2, "kq": 16, "qrow": 16, "xe": 16,
+    (I32, {"eab": 52, "uoi": 8, "pidx": 1, "pbit": 3}),
+    (U16, {"eabu": 52, "uou": 8, "ecu": 4, "lu1": 14, "lu2": 14, "lu3": 14}),
+    (F32, {"rh": 3, "num": C, "undo": 13 * (K + 1), "half": 64, "cidx": 64, "c32": 16, "cim": 64, "k0": 64, "pw": 24, "ca": 24, "cv": 12,
+           "row2": 64, "tla": 64, "tta": 96, "ek": 2,
+           "ptab": C, "pa1": E2, "pb1": E2, "dif": E2, "z": E2 + 2, "cnt": 16, "bias": 16, "tl": 32, "tt": 128,
+           "a1": E2, "b1": E2, "dkc": E2, "sa": E2, "kq": 16, "xe": 16,
            "pa2": E2, "pb2": E2, "pa3": E2, "pb3": E2, "a2": E2, "b2": E2, "a3": E2, "b3": E2, "elb": 2 * E2, "ysb": NT}),
 ):
     for _n in _bufs:
@@ -27,14 +30,31 @@ for _d, _bufs in (
 for _i in range(8):
     SCRATCH["ps%d" % _i] = ("psum", [128, 512], F32)
 
-POOL = {"v": 44, "a": 44, "t": 14, "g": 16}
-NDMA = 26
+POOL = {"v": 38, "a": 34, "t": 14, "g": 28}
+NDMA = 27
 SEMAPHORES = ["arr1", "arr2", "arr3", "sent"] + ["d%d" % _i for _i in range(NDMA)]
 for _q in POOL:
     SEMAPHORES += ["%s%d" % (_q, _i) for _i in range(POOL[_q])]
 
 A = AluOpType
 AF = ActivationFunctionType
+
+CFG = {"p": ["w2 f e0 e1", "eu e2 e3 un", "cn", "", "k0 rec cim c3", "row"],
+       "co": "pa03 pa01 pa12 pv00 pv02 pv13 pa11 pv10 L0 L1 c0 el ev01 ev02 ev10 ea00 ea03 ev12 ea11 ea13 N0 c1 N1 c2"}
+PLAN = {
+    1: {"v": ["k0 k1", "k2", "ev1 mida0", "mid1 lc0", "mid2", "lc1 qv yp midb0", "mid3"],
+        "w": ["k5 k4", "k3", "zf0", "k7", "", "zf1", "k6 k8"], "s3": "st",
+        "a": ["z ev0", "eb0 ev2", "eb1", "eb2 ev3", "eb3", "res k9", "ea0 yo"],
+        "l1": "ea1", "l2": "pa1"},
+    2: {"v": ["", "", "n2 o3 st", "m3 m2 m1", "m0 o5", "m5 o7", "m7 m4 m6"],
+        "w": [""] * 7, "s3": "",
+        "a": ["z o0", "o1 o2", "ea2", "ea3", "o4 o6", "res", "np"],
+        "l1": "yo n3 n1 n0", "l2": "r1"},
+    3: {"v": ["", "", "g1 st", "g3 g0", "g4 g5", "g6", "g7 g2"],
+        "w": [""] * 7, "s3": "",
+        "a": ["z d0", "d2 d1", "e11", "", "e21 d3", "res yo", "r0"],
+        "l1": "e10", "l2": "e20"},
+}
 
 
 def v(name, a=0, b=None, s=1):
@@ -76,7 +96,9 @@ def program(g, T):
             if x[3]:
                 w = w.bitcast(dt.uint32)
             return w.indirect(ap(x[2]))
-        return T[x[1]][:, x[2]:x[3]] if x[4] == 1 else T[x[1]][:, x[2]:x[3]:x[4]]
+        if x[4] == 1:
+            return T[x[1]][:, x[2]:x[3]]
+        return T[x[1]][:, x[2]:(x[3] if x[3] >= 0 else None):x[4]]
 
     def views(xs):
         out = []
@@ -205,6 +227,13 @@ def rank_program(g, core, T, topo):
         else:
             add("g", lambda: g.iota(ap(out), pattern, base, cm, allow_small_or_imprecise_dtypes=True), [], [out])
 
+    def gcopy(out, in_, n):
+        add("g", lambda: g.affine_select(ap(out), ap(in_), [[0, n]], A.is_gt, 0.0, 1, 0), [in_], [out])
+
+    def gfill(out, c):
+        src = col("cidx" if SCRATCH[out[1]][2] == F32 else "diag", 0)
+        add("g", lambda: g.affine_select(ap(out), ap(src), [[0, 1]], A.is_gt, c, 0, 0), [src], [out])
+
     def dma(q, out, in_, reads, writes):
         eng = g.sync if q == "s" else g.scalar
         add(q, lambda: eng.dma_start(out(), in_()), reads, writes, "d")
@@ -229,56 +258,82 @@ def rank_program(g, core, T, topo):
         for i in range(4):
             mm(v("ps%d" % (4 + i), 0, b - a), v("qe", 128 * i, 128 * i + 128), v("qes", 128 * i, 128 * i + 128), *tabv(a, b))
 
-    rr, hh = col("rh", 0), col("rh", 1)
-    C2, CC, RP1, INITB, RM, SROW = 0, 2, 7, 8, 9, 12
-    SC2, T6, BIAS1, M12, BCNT = 0, 1, 2, 3, 4
+    r32, i32, hh = col("rh", 0), col("rh", 1), col("rh", 2)
+    X, AV, INITB, CAPI, CN0 = col("ca", 0), col("ca", 1), col("ca", 2), col("ca", 3), col("ca", 4)
+    KR, CROW, WROW = 5, 8, 12
+    T8, W2, M12, BCNT, REC = col("cv", 0), col("cv", 1), col("cv", 2), col("cv", 3), 4
+    F16 = col("tta", 31)
     H = C // 2
 
     dma("a", lambda: T.ut[:], lambda: T.u[:], [], [v("ut")])
     dma("s", lambda: T.xt[:, 0:4 * H], lambda: T.x[:, 0:4 * H], [], [v("xt", 0, 4 * H)])
     dma("s", lambda: T.xt[:, 4 * H:4 * C], lambda: T.x[:, 4 * H:4 * C], [], [v("xt", 4 * H, 4 * C)])
-    dma("a", lambda: T.eab[:, 0:26], lambda: T.ea[:], [], [v("eab", 0, 26)])
-    dma("a", lambda: T.eab[:, 26:52], lambda: T.eb[:], [], [v("eab", 26, 52)])
+    dma("s", lambda: T.eab[:, 26:52], lambda: T.eb[:], [], [v("eab", 26, 52)])
+    dma("s", lambda: T.eab[:, 0:26], lambda: T.ea[:], [], [v("eab", 0, 26)])
     dma("s", lambda: codes(v("wq")), lambda: T.wc[:], [v("xt")], [v("wq")])
     dma("s", lambda: T.wp[:], lambda: T.ws[:], [], [v("wp")])
     dma("s", lambda: T.vt[:], lambda: T.v[:], [], [v("vt")])
 
-    iota(v("pidx"), [[0, 1]], 0, 1)
+    iota(v("pidx"), [[0, 1]], 0, 32)
     iota(v("uoi"), [[16, 8]], 0, 0)
+    iota(v("c32"), [[32, 16]], 32, 0)
     iota(v("diag"), [[-1, 128]], 0, 1)
-    iota(v("half"), [[1, 2], [0, 16]], 0, 0)
-    iota(v("num"), [[1, E2]], 0, 0)
-    iota(v("kilo"), [[1024, E2]], 0, 0)
-    iota(v("dkc"), [[0, E2]], -1024, 0)
-    fill(v("et"), 0.0)
-    ts(col("pbit", 0), v("pidx"), 15, A.bitwise_and)
-    ts(col("pbit", 1), v("pidx"), 4, A.arith_shift_right, 1, A.bitwise_and)
+    iota(v("cidx"), [[16, 2], [0, 2], [1, 16]], 1, 0)
+    gfill(col("pw", 19), 2.0 ** -8)
+    iota(v("half"), [[0, 2], [512, 2], [0, 16]], 0, 0)
+    gfill(col("zb", E2), PAD)
+    gfill(col("tta", 30), -TOP)
+    gfill(col("ca", KR + 1), 0.5)
+    gfill(col("ca", KR + 2), 8.0)
+    gfill(col("z", E2), PAD)
+    gfill(col("ca", WROW + 3), 2.0 ** -8)
+    gfill(col("res", E2), PAD)
+    gfill(col("gt", E2), 0.0)
+    gfill(col("ek", 0), float(E2))
+    iota(v("dkc"), [[0, E2]], -1, 0)
+    fill(v("et", 0, 1024), 0.0)
+    for j, bits in enumerate((15, 3, 16)):
+        ts(col("pbit", j), v("pidx"), 32 * bits, A.bitwise_and)
+    fill(v("et", 1024, 1536), 0.0)
+    cp(v("rh"), v("pbit"))
     cp(v("uou"), v("uoi"))
+    fill(v("et", 1536, 2048), 0.0)
+    ts(v("pw", 0, 16), v("c32"), r32, A.is_gt, 2.0 ** -8, A.max)
+    ts(v("pw", 16, 19), v("c32", 3, 12, 4), r32, A.is_le, 0.5, A.max)
     for b in range(4):
-        ts(v("et", 513 * b, 512 * (b + 1), 4), v("diag"), 0.0, A.is_equal)
-        if b == 1:
-            cp(v("rh"), v("pbit"))
+        ts(v("et", 513 * b, 512 * (b + 1), 4), v("diag"), 0.0, A.is_equal, 0.5, A.mult)
+    red(T8, v("pw", 0, 16), A.mult)
 
-    def lin(out, a, b):
-        act(out, rr, AF.Identity, bias=float(b), scale=float(a))
+    def lin(out, a, b, x=r32):
+        act(out, x, AF.Identity, bias=b if isinstance(b, tuple) else float(b), scale=a if isinstance(a, tuple) else float(a))
 
-    st = [2.0 ** (-4 * (k + 1)) for k in range(5)]
+    def quant_e(b):
+        quant(v("qe", 128 * b, 128 * b + 128), v("qes", 128 * b, 128 * b + 128), v("et", 512 * b, 512 * b + 512))
+
+    def start(j):
+        rec_in, rec_out = v("tta", 29, 32, 2), v("cv", REC, REC + 2)
+        for name in CFG["p"][j].split():
+            if name[0] == "e" and name != "eu":
+                quant_e(int(name[1]))
+            else:
+                {"eu": lambda: cp(v("eabu"), v("eab")),
+                 "w2": lambda: red(W2, v("pw", 16, 20), A.mult),
+                 "k0": lambda: ts(v("k0"), v("half"), hh, A.not_equal, 10000.0, A.mult),
+                 "cn": lambda: ts(CN0, r32, -7.0, A.add, 0.5, A.min),
+                 "cim": lambda: tt(v("cim"), v("cidx"), v("k0"), A.subtract),
+                 "c3": lambda: ts(col("ca", CROW + 3), i32, 0.0, A.is_equal, CN0, A.mult),
+                 "f": lambda: lin(F16, W2, 0, X),
+                 "row": lambda: lin(v("row2"), W2, F16, v("cim")),
+                 "un": lambda: unpack(0, C),
+                 "rec": lambda: add("v", lambda: V.reciprocal(ap(rec_out), ap(rec_in)), [rec_in], [rec_out]),
+                 }[name]()
+
+    lin(X, 1, 128, i32)
+    lin(col("tta", 29), -1, -144.5, i32)
+    lin(col("ca", KR), 1 / 1024, 1 / 32)
+    start(0)
     quant(v("qu"), v("qus"), v("ut"))
-    for k in range(5):
-        lin(col("ca", SROW + k), 0, st[k])
-    lin(col("ca", SROW + 5), 0, 2.0 ** -23)
     act(v("qgs"), ind(v("qus"), v("uou")), AF.Copy)
-    lin(col("ca", RM), -S15, -89 * S15)
-    lin(col("ca", C2), 1 / 32, 0.5)
-    lin(col("ca", C2 + 1), 0, 0.5)
-    for k in range(4):
-        lin(col("ca", CC + k), st[k + 1] - st[k], -st[k])
-
-    def late_constants():
-        lin(col("ca", CC + 4), -st[4], -st[4])
-        lin(col("ca", RP1), 1, 0.5)
-        lin(col("ca", INITB), S15, 104.5 * S15)
-        lin(col("z0", 0), S15, -103.5 * S15)
 
     sent = [0]
     for t in range(1, R + 1):
@@ -292,6 +347,8 @@ def rank_program(g, core, T, topo):
             [v("wp")], [], "x")
         src = T.cores[(rank + t) % n_ranks]
         add("g", None, [], [v("wq%d" % t), v("wp%d" % t)], "r", ("arr%d" % t, 2 * send_mask(T, topo, src, core)[1]))
+    iota(v("undo"), [[16 + 16 * int(UN), 13], [1, K + 1]], 15 - 6 * 16 * int(UN), 0)
+    iota(v("num"), [[1, C]], 0, 0)
     for t, (ra, rb, o) in enumerate((("a2", "b2", 0), ("a3", "b3", 0), ("elb", "elb", E2))):
         iota(v(ra, 1, E2, 2), [[1, K]], C + t * K, 0)
         iota(v(rb, o, o + E2, 2), [[1, K]], C + t * K, 0)
@@ -302,198 +359,205 @@ def rank_program(g, core, T, topo):
     mm(v("ps0", 0, H), v("qg"), v("qgs"), *tabv(0, H))
     mm(v("ps1", 0, H), v("qg"), v("qgs"), *tabv(H, C))
     act(v("ptab", 0, H), v("ps0", 0, H), AF.Copy)
-    late_constants()
-    ts(v("pw", 16, 32), v("num", 1, 17), rr, A.is_gt, 2.0 ** -6, A.max)
-    ts(v("pw", 0, 16), v("num", 1, 17), rr, A.is_gt, 0.5, A.max)
-    ts(v("k0"), v("half"), hh, A.not_equal, 1000.0, A.mult)
-    ts(v("k8b"), v("half"), hh, A.is_equal, K * S15, A.mult)
-    cp(v("eabu"), v("eab"))
-    red(col("cv", T6), v("pw", 16, 32), A.mult)
+    start(1)
     cp(v("ptab", H, C), v("ps1", 0, H))
-    red(col("cv", SC2), v("pw", 0, 16), A.mult)
-    ts(col("cv", M12), rr, 12.0, A.min, 16 * S15, A.mult)
-    ts(col("cv", BIAS1), col("cv", T6), -2.0 ** 80, A.mult, col("cv", T6), A.mult)
-    cp(v("pb1", 0, 128), ind(v("ptab"), v("eabu", 26, 34)))
-    for a, b in ((8, 18), (18, 26)):
-        act(v("pb1", 16 * a, 16 * b), ind(v("ptab"), v("eabu", 26 + a, 26 + b)), AF.Copy)
-    cp(v("pa1", 0, 96), ind(v("ptab"), v("eabu", 0, 6)))
-    for a, b in ((0, 8), (8, 18), (18, 26)):
-        tt(v("dif", 16 * a, 16 * b), ind(v("ptab"), v("eabu", a, b)), v("pb1", 16 * a, 16 * b), A.subtract)
-        act(v("z", 16 * a, 16 * b), v("dif", 16 * a, 16 * b), AF.Abs)
-    quant(v("qe"), v("qes"), v("et"))
-    unpack(0, C)
+    start(2)
+    cuts = (0, 96, 256, E2)
+    cp(v("pb1", 0, cuts[1]), ind(v("ptab"), v("eabu", 26, 26 + cuts[1] // 16)))
+    for a, b in zip(cuts[1:], cuts[2:]):
+        act(v("pb1", a, b), ind(v("ptab"), v("eabu", 26 + a // 16, 26 + b // 16)), AF.Copy)
+    start(3)
+    for a, b in zip(cuts, cuts[1:]):
+        tt(v("dif", a, b), ind(v("ptab"), v("eabu", a // 16, b // 16)), v("pb1", a, b), A.subtract)
+        act(v("zb", a, b), v("dif", a, b), AF.Abs)
+    start(4)
 
     HS = ((0, 128), (128, K))
+
+    def move(q, out, src):
+        if q == "v":
+            cp(out, src)
+        else:
+            act(out, src, AF.Copy)
+
+    def affine(q, out, a, b, x):
+        if q == "a":
+            lin(out, a, b, x)
+        elif b == 0:
+            ts(out, x, a, A.mult)
+        else:
+            ts(out, x, a, A.mult, b, A.add)
 
     def split(t, a=0, c=K):
         return v("lu%d" % t, a // 16, c // 16)
 
-    def next_ends(t, par):
+    def next_ends(t, par, q="a"):
         src = ind(v("ab"[par] + str(t)), split(t))
-        act(v("ab"[par] + str(t + 1), par, E2, 2) if t < R else v("elb", par * (E2 + 1), (par + 1) * E2, 2), src, AF.Copy)
+        move(q, v("ab"[par] + str(t + 1), par, E2, 2) if t < R else v("elb", par * (E2 + 1), (par + 1) * E2, 2), src)
 
     def y_product(a, b):
         mm(v("ps2", 0, b - a), v("qv"), v("qvs"), *tabv(a, b))
 
-    def y_out(a, b):
-        act(v("ysb", a, b), v("ps2", 0, b - a), AF.Copy)
-        store_y("s", a, b)
-
     def plane(name, b, a=0, s=1):
         return v(name, E2 * b + a, E2 * (b + 1), s)
 
-    def first_row(par):
-        return lambda: act(v("ab"[par] + "1"), ind(v("num", 0, C), v("eabu", 26 * par, 26 * par + 26)), AF.Copy)
-
-    def rows(t):
-        return [lambda: next_ends(t, 0), lambda: next_ends(t, 1)]
-
-    def list_constants():
-        tt(col("cv", BCNT), col("cv", M12), col("ca", RM), A.add)
-        ts(v("qrow"), v("num", 0, 16), -6.0, A.add, 16 * S15, A.mult)
-
-    def first_p(a, b):
-        return lambda: cp(v("pa1", 16 * a, 16 * b), ind(v("ptab"), v("eabu", a, b)))
+    def bias(k):
+        return col("bias", k)
 
     for t in range(1, R + 1):
         n = C + (t - 1) * K
         n0 = 0 if t == 1 else n - K
 
-        def new_d(b):
-            return v("dh", ND * b + n0, ND * b + n)
+        def bank(b, a=0, c=n - n0):
+            return v("ps%d" % (4 + b), a, c)
 
-        def half_d(b):
-            if b % 2:
-                return lambda: act(new_d(b), v("ps%d" % (4 + b), 0, n - n0), AF.Identity, scale=0.5)
-            return lambda: ts(new_d(b), v("ps%d" % (4 + b), 0, n - n0), 0.5, A.mult)
+        def old(j):
+            return plane("d%s%d" % ("ab"[j % 2], 4 - t), j // 2, j % 2, 2)
 
-        def end_d(par, b):
-            return lambda: act(plane("d%s1" % "ab"[par], b), ind(new_d(b), v("eabu", 26 * par, 26 * par + 26)), AF.Copy)
+        def old_src(j):
+            return ind(plane("d%s%d" % ("ab"[j % 2], t - 1), j // 2), split(t - 1))
 
-        def mid1(b):
-            return lambda: tt(plane("mall", b), ind(new_d(b), v("eabu", 0, 26)), plane("db1", b), A.add)
-
-        def all_mid(j):
-            b, par = j // 2, j % 2
-            return lambda: tt(plane("mall", b, par, 2), ind(plane("d%s%d" % ("ab"[par], t - 1), b), split(t - 1)), new_d(b), A.add)
-
-        def carry_d(par, b):
-            name = "d%s2" % "ab"[par]
-
-            def f():
-                act(plane(name, b, par, 2), ind(plane("d%s1" % "ab"[par], b), split(1)), AF.Copy)
-                act(plane(name, b, 1 - par, 2), new_d(b), AF.Copy)
-            return f
-
-        def new_p(par):
-            def f():
+        def task(q, name):
+            j = int(name[-1]) if name[-1].isdigit() else 0
+            w = name.rstrip("0123456789")
+            dx = v("dh", C * j, C * j + C)
+            if w == "z":
+                act(v("z", 0, E2), v("dif"), AF.Abs)
+            elif w == "ev":
+                move(q, dx, bank(j))
+            elif w in ("ea", "eb"):
+                par = "ab".index(w[1])
+                move(q, plane("d%s1" % w[1], j), ind(dx, v("eabu", 26 * par, 26 * par + 26)))
+            elif w in ("mid", "mida", "midb"):
+                a, c = {"mid": (0, 26), "mida": (0, 14), "midb": (14, 26)}[w]
+                tt(v("mall", E2 * j + 16 * a, E2 * j + 16 * c), ind(dx, v("eabu", a, c)), v("db1", E2 * j + 16 * a, E2 * j + 16 * c), A.add)
+            elif w == "st":
+                affine(q, v("tt", 91, 96), bias(9), 0, v("ca", WROW, WROW + 5))
+            elif w == "res":
+                affine(q, v("res", 0, E2), 2.0 ** 15, bias(12), v("z", 0, E2))
+            elif w == "t":
+                for o, c in {5: ((31, 91), (64, 92)), 7: ((31, 93),)}.get(j, ((31, 91),)):
+                    affine(q, col("tt", o), 16.0 if j < 7 else 1 / 16, col("tt", c), bias(j))
+            elif w == "o":
+                move(q, old(j), old_src(j))
+            elif w == "m":
+                tt(plane("mall", j // 2, j % 2, 2), old(j), bank(j // 2), A.add)
+            elif w == "d":
+                move(q, v("dh", C * j, C * j + K), bank(j))
+            elif w == "g":
+                tt(plane("mall", j // 2, j % 2, 2), old_src(j), v("dh", C * (j // 2), C * (j // 2) + K), A.add)
+            elif w == "n":
+                move(q, plane("da2", j, 1, 2), bank(j))
+                gcopy(plane("db2", j, 0, 2), plane("da2", j, 1, 2), K)
+            elif w == "np":
                 for h, (a, c) in enumerate(HS):
-                    act(v("p%s2" % "ab"[par], 2 * a + 1 - par, 2 * c, 2), v("ps%d" % h, 0, c - a), AF.Copy)
-            return f
+                    move(q, v("pa2", 2 * a + 1, 2 * c, 2), v("ps%d" % h, 0, c - a))
+                gcopy(v("pb2", 0, E2, 2), v("pa2", 1, E2, 2), K)
+            elif w == "pa":
+                move(q, v("pa1"), ind(v("ptab"), v("eabu", 0, 26)))
+            elif w == "r":
+                move(q, v("ab"[j] + "1"), ind(v("num"), v("eabu", 26 * j, 26 * j + 26)))
+            elif w == "e":
+                next_ends(int(name[1]), j, q)
+            elif w == "yp":
+                y_product(n0, n)
+            elif w == "yo":
+                move(q, v("ysb", n0, n), v("ps2", 0, n - n0))
+                store_y("s", n0, n)
+            elif w == "qv":
+                quant(v("qv"), v("qvs"), v("vt"))
+            elif w == "k":
+                affine(q, *((AV, col("cv", REC), 0, X), (v("ca", CROW, CROW + 3), col("cv", REC + 1), 0, v("ca", KR, KR + 3)),
+                            (col("ca", WROW), -15 / 512, -15 / 16, r32), (col("ca", WROW + 1), -1 / 32, -1 + 120 / 256, r32),
+                            (col("ca", WROW + 2), -1 / 8192, -1 / 512, r32), (col("ca", WROW + 4), 1 / 512, -119.5 / 16, r32),
+                            (INITB, UN / 32, 104.5 * UN, r32), (CAPI, UN / 32, -103.5 * UN, r32),
+                            (BCNT, -UN / 32, M12, r32),
+                            (col("ek", 1), 2 * (K - 15) / (16 * UN), 89 * 2 * (K - 15) / 16 + E2 - 30, M12))[j])
+            elif w == "lc":
+                if j == 0:
+                    ts(M12, r32, 12.0 * 32, A.min, UN / 2, A.mult)
+                else:
+                    ts(M12, M12, -89 * UN, A.add)
+            elif w == "zf":
+                fill(v("mt" if j else "rt", 4 * K, 1024), 0.0)
+            else:
+                raise ValueError(name)
 
+        def tasks(q, s):
+            for name in s.split():
+                task(q, name)
+
+        def side(k):
+            tasks("v", PLAN[t]["v"][k - 1])
+
+        def turn(k, out, in_):
+            tr(out, in_)
+            tasks("v", PLAN[t]["w"][k - 1])
+            tasks("a", PLAN[t]["a"][k - 1])
+
+        nbase, all_, mid, k0 = bias(9), v("junk", 0, E2 + 1), v("tt", 32, 64), v("k0", 0, 32)
+        cv_ = col("sc", K - 1)
+
+        def vector_count(init):
+            scan(v("sc"), v("fl", 0, K), v("fl", K, E2), init, A.add, A.add)
+
+        act(all_, v("zb", 0, E2 + 1), AF.Sign, bias=T8, scale=-16 / TOP / (1 + 2.0 ** -8), acc=col("cnt", 1))
+        for a, b in ((0, 256), (256, E2)):
+            ts(v("fl", a, b), v("zb", a, b), 256 / TOP, A.mult, T8, A.is_le)
+        vector_count(-1.0 - K)
+        side(1)
+        ts(v("tla", 0, 32), k0, col("cnt", 1), A.is_gt, 1 / 16, A.max)
+        ts(v("tla", 32, 64), k0, cv_, A.is_gt, 1 / 16, A.max)
+        turn(1, v("tta", 32, 96), v("tla"))
         if t == 1:
-            side = [[lambda: fill(v("z0", 1, E2), 0.0)], [half_d(0), half_d(2), lambda: fill(v("mt", 4 * K, 1024), 0.0)],
-                    [first_p(6, 26), lambda: fill(v("rt", 4 * K, 1024), 0.0)],
-                    [mid1(0), list_constants], [mid1(1), lambda: quant(v("qv"), v("qvs"), v("vt")), lambda: y_product(0, C)], [mid1(2)],
-                    [lambda: cp(v("ysb", 0, C), v("ps2", 0, C)), lambda: store_y("s", 0, C)], [mid1(3)]]
-            aside = [[half_d(1), half_d(3)], [end_d(1, 0)], [end_d(1, 1)], [end_d(1, 2)], [end_d(1, 3)], [end_d(0, 0)], [end_d(0, 1)],
-                     [end_d(0, 2), end_d(0, 3)]]
-        else:
-            yo = [lambda: y_out(n0, n)]
-            side = [[half_d(0), half_d(2)], [all_mid(0), all_mid(1)], [all_mid(2)], [all_mid(3), all_mid(4)], [all_mid(5)],
-                    [all_mid(6)], [], [all_mid(7)]]
-            if t == 2:
-                aside = [[half_d(1), half_d(3), new_p(0)], [carry_d(0, 0)] + yo, [carry_d(0, 1), new_p(1)], [carry_d(0, 2)],
-                         [carry_d(0, 3)], [carry_d(1, 0)], [carry_d(1, 1)], [carry_d(1, 2), carry_d(1, 3)]]
-            else:
-                aside = [[half_d(1), half_d(3)] + yo, [first_row(0)], [first_row(1)], rows(1), rows(2), [], [], []]
-        z = v("z")
-        mid = v("tt", 32, 64)
-        nbase, nulp, rulp = col("step", 6), col("step", 7), col("step", 8)
-
-        def bias(k):
-            return col("bias", k)
-
-        for k in range(1, 8):
+            start(5)
+        red(bias(2), v("tta", 30, 96), A.mult)
+        act(all_, v("z", 0, E2 + 1), AF.Sign, bias=bias(2), acc=col("cnt", 2))
+        ts(v("fl"), v("zb", 0, E2), AV, A.mult, bias(2), A.is_lt)
+        affine("v", v("ttb", 31, 323, 97), bias(2), 0, v("ca", CROW, CROW + 4))
+        vector_count(1.0 - K)
+        move("a", v("bias", 10, 12), v("ttb", 225, 323, 97))
+        side(2)
+        ts(v("tlb", 0, 32), v("row2", 0, 32), col("cnt", 2), A.min, bias(10), A.mult)
+        ts(v("tlb", 32, 64), v("row2", 32, 64), cv_, A.min, col("ttb", 225), A.mult)
+        ts(v("tlb", 64, 96), k0, col("cnt", 2), A.is_lt, bias(11), A.mult)
+        turn(2, v("ttb", 32, 96), v("tlb", 0, 64))
+        tr(v("ttb", 96, 128), v("tlb", 64, 96))
+        red(bias(3), v("ttb", 31, 96), A.min)
+        red(nbase, v("ttb", 96, 129), A.add)
+        for k, scale in ((3, 8.0), (4, 2.0 ** 7), (5, 2.0 ** 11), (6, 2.0 ** 15), (7, 16.0)):
             s = col("cnt", k)
-            if k == 1:
-                act(v("junk", 0, K), v("z", 0, K), AF.Sign, bias=col("cv", BIAS1), acc=col("cnt", 9))
-                act(v("junk", K, E2), v("z", K, E2), AF.Sign, bias=col("cv", BIAS1), acc=s)
-            elif k == 2:
-                act(v("junk"), z, AF.Sign, bias=bias(2), scale=col("cv", SC2), acc=s)
+            act(all_, v("z" if k < 7 else "res", 0, E2 + 1), AF.Sign, bias=bias(k), scale=scale, acc=s)
+            side(k)
+            if k == 3:
+                tasks("a", PLAN[t]["s3"])
+            ts(v("tl"), k0, s, A.is_lt, nbase if k < 7 else col("tt", 94), A.mult)
+            if k != 6:
+                task("v", "t%d" % k)
+            turn(k, mid if k != 6 else v("tt", 96, 128), v("tl"))
+            if k == 6:
+                red(bias(7), v("tt", 95, 128), A.add)
             else:
-                act(v("junk"), z, AF.Sign, bias=bias(k), acc=s)
-                if k == 3:
-                    ts(v("step", 0, 6), v("ca", SROW, SROW + 6), nbase, A.mult)
-                if k == 7:
-                    ts(v("res"), z, bias(7), A.add)
-            for f in side[k - 1] + aside[k - 1]:
-                f()
-            if k == 1:
-                ts(v("k1"), v("k0"), col("cnt", 9), A.subtract)
-                ts(v("tl"), v("k1"), s, A.is_le, col("cv", BIAS1), A.mult)
-            elif k == 2:
-                ts(v("tl"), v("k0"), s, A.is_le, 1.0, A.add)
-                ts(v("tt", 31, 65, 33), v("ca", C2, C2 + 2), bias(2), A.mult)
-            else:
-                ts(v("tl"), v("k0"), s, A.is_le, col("step", k - 3), A.mult)
-                if k < 7:
-                    ts(col("tt", 31), col("ca", CC + k - 3), nbase, A.mult, bias(k), A.add)
-                if k == 4:
-                    ts(nulp, col("step", 5), -2.0 ** -115, A.min)
-                if k == 5:
-                    ts(rulp, col("ca", RP1), nulp, A.mult)
-                if k == 6:
-                    ts(col("tt", 64), col("ca", CC + 4), nbase, A.mult, rulp, A.add)
-            tr(mid, v("tl"))
-            if k == 1:
-                red(bias(2), mid, A.min)
-            elif k == 2:
-                red(bias(3), v("tt", 31, 64), A.mult)
-                red(nbase, v("tt", 32, 65), A.mult)
-            elif k < 7:
-                red(bias(k + 1), v("tt", 31, 64), A.add)
-            else:
-                red(bias(8), v("tt", 32, 65), A.add)
-        tot, tot2 = col("cnt", 10), col("cnt", 11)
-        act(v("junk"), v("res"), AF.Sign, bias=bias(8), acc=tot)
-        for f in side[7] + aside[7]:
-            f()
-        ts(col("tt8", 31), rulp, -1.0, A.mult, bias(8), A.add)
-        ts(tot2, tot, S15 / 2, A.mult, K * S15, A.add)
-        ts(v("tl8", 0, 32), v("k0"), tot, A.is_le, nulp, A.mult)
-        ts(v("tl8", 32, 64), v("k8b"), tot2, A.is_gt, tot2, A.mult)
-        tr(v("tt8", 32, 64), v("tl8", 0, 32))
-        tr(v("tt8", 64, 96), v("tl8", 32, 64))
-        red(bias(10), v("tt8", 31, 64), A.add, negate=True)
-        red(bias(11), v("tt8", 64, 96), A.max)
-        ts(v("gt"), v("res"), bias(10), A.is_gt, -S15, A.mult)
-        ts(v("ge"), v("res"), bias(10), A.is_ge, -S15, A.mult)
-        scan(v("cap"), v("z0"), v("gt"), bias(11), A.add, A.add)
-        scan(v("cum"), v("ge"), v("cap"), col("ca", INITB), A.add, A.max)
-        act(v("junk"), v("cum"), AF.Sign, bias=col("cv", BCNT), acc=col("cnt", 8))
-        ts(v("qn"), v("cum"), 1.5 * 2.0 ** 42, A.add, 1.5 * 2.0 ** 42, A.subtract)
-        ec = col("ecu", 0)
-        scan(v("sa", 0, K), v("dkc", 0, K), v("qn", 0, K), 2.0 ** 23, A.add, A.min)
-        ts(ec, col("cnt", 8), 0.5, A.mult, float(K), A.add)
-        scan(v("sa", K, E2), v("dkc", K, E2), v("qn", K, E2), col("sa", K - 1), A.add, A.min)
-        tt(v("kq"), ind(v("kilo"), ec), v("qrow"), A.add)
-        tt(v("xe"), ind(v("sa"), ec), v("kq"), A.add)
-        ts(v("lu%d" % t), v("xe", 0, 14), 2.0 ** -10, A.mult)
+                red(bias(k + 1), v("tt", 31, 64), A.add, negate=k == 7)
+            if k == 5:
+                red(bias(12), v("tt", 32, 65), A.add)
+        tasks("a", PLAN[t]["l1"])
+        ts(v("gt", 0, E2), v("res", 0, E2), bias(8), A.is_gt, UN / 2, A.mult)
+        ts(v("ge"), v("res", 0, E2), bias(8), A.is_ge, -UN, A.mult)
+        scan(v("cap", E2 - 1, -1, -1), v("gt", E2, 0, -1), v("gt", E2, 0, -1), CAPI, A.add, A.add)
+        scan(v("cum"), v("ge"), v("cap"), INITB, A.add, A.max)
+        act(v("junk", 0, E2), v("cum"), AF.Sign, bias=BCNT, acc=col("cnt", 8))
+        tasks("a", PLAN[t]["l2"])
+        big = 1.5 * 2.0 ** 23 * 16 * UN
+        ts(v("qn"), v("cum"), big, A.add, big, A.subtract)
+        ts(v("ecu", 0, 4, 2), v("ek"), col("cnt", 8), A.add, 0.5, A.mult)
+        act(v("kq"), ind(v("undo"), col("ecu", 2)), AF.Copy)
+        scan(v("sa"), v("dkc"), v("qn"), 256 * UN, A.add, A.min)
+        tt(v("xe"), ind(v("sa"), col("ecu", 0)), v("kq"), A.add)
+        cp(v("lu%d" % t), v("xe", 0, 14))
 
-        def pick(h, b):
-            a, c = HS[h]
-            src, out = ind(plane("mall", b), split(t, a, c)), v("mt", 4 * a + b, 4 * c, 4)
-            if b % 2:
-                cp(out, src)
-            else:
-                act(out, src, AF.Copy)
-
-        def carry(par):
-            if t < R:
-                act(v("p%s%d" % ("ab"[par], t + 1), par, E2, 2), ind(v("p%s%d" % ("ab"[par], t)), split(t)), AF.Copy)
-            else:
-                next_ends(t, par)
+        def carry(par, a=0, c=K):
+            move("a", v("p%s%d" % ("ab"[par], t + 1), 2 * a + par, 2 * c, 2), ind(v("p%s%d" % ("ab"[par], t)), split(t, a, c)))
 
         def layer(h):
             a = 128 * h
@@ -501,14 +565,6 @@ def rank_program(g, core, T, topo):
             for b in range(4):
                 mm(v("ps%d" % (4 * h + b), 0, 128), v("wq%d" % t, 128 * b, 128 * b + 128), v("wp%d" % t, 128 * b, 128 * b + 128),
                    v("qm", a, a + 128), v("qms", a, a + 128))
-
-        def evac(h, b):
-            a, c = HS[h]
-            out, src = v("rt", 4 * a + b, 4 * c, 4), v("ps%d" % (4 * h + b), 0, c - a)
-            if b % 2 and (h == 0 or b == 3):
-                ts(out, src, 0.03125, A.mult)
-            else:
-                act(out, src, AF.Identity, scale=0.03125)
 
         def new_cols(h):
             a = 128 * h
@@ -520,23 +576,35 @@ def rank_program(g, core, T, topo):
             a, c = HS[h]
             for par in range(2):
                 tt(v("dif", 2 * a + par, 2 * c, 2), v("p" + "ab"[par] + str(t + 1), 2 * a + par, 2 * c, 2), v("ps%d" % h, 0, c - a), A.subtract)
-            act(v("z", 2 * a, 2 * c), v("dif", 2 * a, 2 * c), AF.Abs)
+                if h == 0:
+                    act(v("zb", 2 * a + par, 2 * c, 2), v("dif", 2 * a + par, 2 * c, 2), AF.Abs)
+            if h == 1:
+                act(v("zb", 2 * a, 2 * c), v("dif", 2 * a, 2 * c), AF.Abs)
 
-        for h in range(2):
-            for b in range(4):
-                pick(h, b)
-        layer(0)
-        carry(0)
-        layer(1)
-        for b in range(4):
-            evac(0, b)
-        evac(1, 3)
-        new_cols(0)
-        for b in range(3):
-            evac(1, b)
+        for w in CFG["co"].split():
+            if w == "el":
+                if t == R:
+                    next_ends(t, 1, "v")
+                    dma("s", lambda: T.el[:], lambda: T.elb[0:128:16, :], [v("elb")], [])
+            elif w[0] in "pe":
+                h, b = int(w[2]), int(w[3])
+                a, c = HS[h]
+                if w[0] == "p":
+                    move(w[1], v("mt", 4 * a + b, 4 * c, 4), ind(plane("mall", b), split(t, a, c)))
+                else:
+                    affine(w[1], v("rt", 4 * a + b, 4 * c, 4), 0.03125, 0, v("ps%d" % (4 * h + b), 0, c - a))
+            elif w[0] == "L":
+                layer(int(w[1]))
+            elif w[0] == "N":
+                new_cols(int(w[1]))
+            elif w == "c0":
+                if t < R:
+                    carry(0)
+                else:
+                    next_ends(t, 0)
+            elif t < R:
+                carry(1, *HS[int(w[1]) - 1])
         if t < R:
-            carry(1)
-            new_cols(1)
             unpack(n, n + K)
             y_product(n, n + K)
             scores(0)
@@ -545,13 +613,10 @@ def rank_program(g, core, T, topo):
                 store_codes("s", 0, ND)
                 store_scales("ssss", 0, ND)
         else:
-            new_cols(1)
-            carry(1)
+            move("a", v("ysb", ND, ND + 128), v("ps0", 0, 128))
             store_codes("s", ND, NT)
-            cp(v("ysb", ND, ND + 128), v("ps0", 0, 128))
-            dma("a", lambda: T.el[:], lambda: T.elb[0:128:16, :], [v("elb")], [])
-            store_scales("ssaa", ND, NT)
             cp(v("ysb", ND + 128, NT), v("ps1", 0, K - 128))
+            store_scales("aaaa", ND, NT)
             store_y("s", ND, NT)
     emit()
     g.wait_ge(T.sem.sent, sent[0])

@@ -13,15 +13,15 @@ X4, U8, BF, F32, I32, U16 = "float8_e4m3fn_x4", "uint8", "bfloat16", "float32", 
 SCRATCH = {}
 for _d, _bufs in (
     (BF, {"xt": 4 * C, "ut": 512, "vt": 512, "et": 2048, "diag": 128, "junk": E2 + 2, "res": E2 + 2, "zb": E2 + 2, "fl": E2, "sc": K,
-          "gt": E2 + 2, "ge": E2, "cap": E2, "cum": E2, "qn": E2, "dh": 4 * C, "mt": 1024, "rt": 1024, "tlb": 96, "ttb": 324,
+          "gt": E2 + 2, "ge": E2, "cap": E2, "cum": E2, "qn": E2, "dh": 4 * C, "mt": 1024, "rt": 1024, "nbb": 2,
           "mall": 4 * E2, "da1": 4 * E2, "db1": 4 * E2, "da2": 4 * E2, "db2": 4 * E2}),
     (X4, {"wq": 512, "wq1": 512, "wq2": 512, "wq3": 512, "tab": NT + 48, "qu": 128, "qg": 128, "qv": 128, "qe": 512, "qm": 256}),
     (U8, {"wp": 512, "wp1": 512, "wp2": 512, "wp3": 512, "tabs": NT + 48, "qus": 128, "qgs": 128, "qvs": 128, "qes": 512, "qms": 256}),
-    (I32, {"eab": 52, "uoi": 8, "pidx": 1, "pbit": 3}),
-    (U16, {"eabu": 52, "uou": 8, "ecu": 4, "lu1": 14, "lu2": 14, "lu3": 14}),
-    (F32, {"rh": 3, "num": C, "undo": 13 * (K + 1), "half": 64, "cidx": 64, "c32": 16, "cim": 64, "k0": 64, "pw": 24, "ca": 24, "cv": 12,
-           "row2": 64, "tla": 64, "tta": 96, "ek": 2,
-           "ptab": C, "pa1": E2, "pb1": E2, "dif": E2, "z": E2 + 2, "cnt": 16, "bias": 16, "tl": 32, "tt": 128,
+    (I32, {"eab": 52, "uoi": 8, "pidx": 1, "pbit": 2}),
+    (U16, {"eabu": 52, "uou": 8, "ecu": 4, "of2": 4, "of1": 4, "lu1": 14, "lu2": 14, "lu3": 14}),
+    (F32, {"rh": 2, "num": C, "undo": 13 * (K + 1), "c32": 16, "pw": 24, "ca": 24, "cv": 12,
+           "ta": 40, "tb": 40, "tn": 40, "four": 32, "cell": 8, "got": 96, "ek": 2,
+           "ptab": C, "pa1": E2, "pb1": E2, "dif": E2, "z": E2 + 2, "cnt": 16, "bias": 16,
            "a1": E2, "b1": E2, "dkc": E2, "sa": E2, "kq": 16, "xe": 16,
            "pa2": E2, "pb2": E2, "pa3": E2, "pb3": E2, "a2": E2, "b2": E2, "a3": E2, "b3": E2, "elb": 2 * E2, "ysb": NT}),
 ):
@@ -30,7 +30,7 @@ for _d, _bufs in (
 for _i in range(8):
     SCRATCH["ps%d" % _i] = ("psum", [128, 512], F32)
 
-POOL = {"v": 38, "a": 34, "t": 14, "g": 28}
+POOL = {"v": 32, "a": 28, "t": 12, "g": 44}
 NDMA = 27
 SEMAPHORES = ["arr1", "arr2", "arr3", "sent"] + ["d%d" % _i for _i in range(NDMA)]
 for _q in POOL:
@@ -39,21 +39,24 @@ for _q in POOL:
 A = AluOpType
 AF = ActivationFunctionType
 
-CFG = {"p": ["w2 f e0 e1", "eu e2 e3 un", "cn", "", "k0 rec cim c3", "row"],
+CFG = {"p": ["w2 f a0 a1 e0 e1", "eu e2 e3 un", "o2", "", "ta rec", ""],
        "co": "pa03 pa01 pa12 pv00 pv02 pv13 pa11 pv10 L0 L1 c0 el ev01 ev02 ev10 ea00 ea03 ev12 ea11 ea13 N0 c1 N1 c2"}
 PLAN = {
-    1: {"v": ["k0 k1", "k2", "ev1 mida0", "mid1 lc0", "mid2", "lc1 qv yp midb0", "mid3"],
-        "w": ["k5 k4", "k3", "zf0", "k7", "", "zf1", "k6 k8"], "s3": "st",
-        "a": ["z ev0", "eb0 ev2", "eb1", "eb2 ev3", "eb3", "res k9", "ea0 yo"],
-        "l1": "ea1", "l2": "pa1"},
-    2: {"v": ["", "", "n2 o3 st", "m3 m2 m1", "m0 o5", "m5 o7", "m7 m4 m6"],
-        "w": [""] * 7, "s3": "",
-        "a": ["z o0", "o1 o2", "ea2", "ea3", "o4 o6", "res", "np"],
-        "l1": "yo n3 n1 n0", "l2": "r1"},
-    3: {"v": ["", "", "g1 st", "g3 g0", "g4 g5", "g6", "g7 g2"],
-        "w": [""] * 7, "s3": "",
-        "a": ["z d0", "d2 d1", "e11", "", "e21 d3", "res yo", "r0"],
-        "l1": "e10", "l2": "e20"},
+    1: {"v": ["k0", "", "ev1 ev2 st eb0", "mida0 midb0 midb1", "", "ref lc1 res", "qv"],
+        "w": ["b1 b2 zf1 b0 oc0 b3", "ev0", "", "lc0 mida1 ev3 zf0", "mida2 oc1", "midb3 mida3", "midb2 yp"],
+        "a": ["z0", "k3 k4 z1", "eb1", "eb2", "eb3", "k9 k8", "ea0"],
+        "b": ["k2 k5 k1", "", "k7", "", "k6", "", ""],
+        "l1": "ea1 yo", "l2": "pa1"},
+    2: {"v": ["", "", "st o1", "m1 ea2", "m0", "m4 ref o5 res", ""],
+        "w": ["o2", "n1 o0", "", "ea3", "", "m6 m7 m3 m2", "m5"],
+        "a": ["z0", "z1", "", "o3", "o4", "o7", "n0"],
+        "b": ["", "", "", "", "o6", "", "yo"],
+        "l1": "n3 np n2", "l2": "r1"},
+    3: {"v": ["", "", "st", "o3 m0 m3 m1", "o5 m4 m5", "m2 ref res", "o7 r0 m7"],
+        "w": ["o2", "o0 o4", "", "", "", "", "m6"],
+        "a": ["z0", "z1", "o1", "", "", "o6", "e11"],
+        "b": ["", "", "", "", "", "", "yo e10 e21"],
+        "l1": "", "l2": "e20"},
 }
 
 
@@ -199,14 +202,11 @@ def rank_program(g, core, T, topo):
     def cp(out, in_):
         add("v", lambda: V.tensor_copy(ap(out), ap(in_)), [in_], [out])
 
-    def red(out, in_, op, negate=False):
-        add("v", lambda: V.tensor_reduce(ap(out), ap(in_), AxisListType.X, op, negate=negate), [in_], [out])
+    def red(out, in_, op):
+        add("v", lambda: V.tensor_reduce(ap(out), ap(in_), AxisListType.X, op), [in_], [out])
 
     def scan(out, d0, d1, init, op0, op1):
         add("v", lambda: V.tensor_tensor_scan(ap(out), ap(d0), ap(d1), ap(init), op0, op1), [d0, d1, init], [out])
-
-    def tr(out, in_):
-        add("v", lambda: V.transpose(ap(out), ap(in_)), [in_], [out])
 
     def fill(out, c):
         add("v", lambda: V.memset(ap(out), c), [], [out])
@@ -231,7 +231,7 @@ def rank_program(g, core, T, topo):
         add("g", lambda: g.affine_select(ap(out), ap(in_), [[0, n]], A.is_gt, 0.0, 1, 0), [in_], [out])
 
     def gfill(out, c):
-        src = col("cidx" if SCRATCH[out[1]][2] == F32 else "diag", 0)
+        src = col("c32" if SCRATCH[out[1]][2] == F32 else "diag", 0)
         add("g", lambda: g.affine_select(ap(out), ap(src), [[0, 1]], A.is_gt, c, 0, 0), [src], [out])
 
     def dma(q, out, in_, reads, writes):
@@ -258,11 +258,12 @@ def rank_program(g, core, T, topo):
         for i in range(4):
             mm(v("ps%d" % (4 + i), 0, b - a), v("qe", 128 * i, 128 * i + 128), v("qes", 128 * i, 128 * i + 128), *tabv(a, b))
 
-    r32, i32, hh = col("rh", 0), col("rh", 1), col("rh", 2)
-    X, AV, INITB, CAPI, CN0 = col("ca", 0), col("ca", 1), col("ca", 2), col("ca", 3), col("ca", 4)
-    KR, CROW, WROW = 5, 8, 12
+    r32, i32 = col("rh", 0), col("rh", 1)
+    X, INITB, CAPI, IDX0, IDX1, C1, A1, U = (col("ca", j) for j in range(8))
+    AV, AS = col("ca", 8), col("ca", 9)
+    RIN, WROW = 10, 14
     T8, W2, M12, BCNT, REC = col("cv", 0), col("cv", 1), col("cv", 2), col("cv", 3), 4
-    F16 = col("tta", 31)
+    F16 = col("ca", RIN + 2)
     H = C // 2
 
     dma("a", lambda: T.ut[:], lambda: T.u[:], [], [v("ut")])
@@ -274,35 +275,44 @@ def rank_program(g, core, T, topo):
     dma("s", lambda: T.wp[:], lambda: T.ws[:], [], [v("wp")])
     dma("s", lambda: T.vt[:], lambda: T.v[:], [], [v("vt")])
 
+    def const(name, a, b, c, s=1):
+        iota(v(name, a, b, s), [[0, len(range(a, b, s))]], c, 0)
+
     iota(v("pidx"), [[0, 1]], 0, 32)
     iota(v("uoi"), [[16, 8]], 0, 0)
     iota(v("c32"), [[32, 16]], 32, 0)
     iota(v("diag"), [[-1, 128]], 0, 1)
-    iota(v("cidx"), [[16, 2], [0, 2], [1, 16]], 1, 0)
     gfill(col("pw", 19), 2.0 ** -8)
-    iota(v("half"), [[0, 2], [512, 2], [0, 16]], 0, 0)
+    const("four", 0, 32, 4)
     gfill(col("zb", E2), PAD)
-    gfill(col("tta", 30), -TOP)
-    gfill(col("ca", KR + 1), 0.5)
-    gfill(col("ca", KR + 2), 8.0)
+    const("ta", 0, 40, 0, 39)
+    const("ta", 34, 39, 0)
+    const("tb", 0, 40, 0, 39)
+    const("tb", 35, 39, 0)
+    for j in range(4):
+        const("tb", 3 + 8 * j, 11 + 8 * j, 32 << j)
+    const("tn", 0, 40, 0)
+    const("cell", 0, 8, 0)
+    iota(v("tn", 1, 3), [[-15 * 256, 2]], 8 * 256, 0)
+    for j in range(3):
+        const("tn", 10 + 8 * j, 11 + 8 * j, 256 << j)
     gfill(col("z", E2), PAD)
-    gfill(col("ca", WROW + 3), 2.0 ** -8)
+    gfill(col("ca", WROW), 2.0 ** -8)
     gfill(col("res", E2), PAD)
     gfill(col("gt", E2), 0.0)
     gfill(col("ek", 0), float(E2))
-    iota(v("dkc"), [[0, E2]], -1, 0)
     fill(v("et", 0, 1024), 0.0)
-    for j, bits in enumerate((15, 3, 16)):
+    for j, bits in enumerate((15, 3)):
         ts(col("pbit", j), v("pidx"), 32 * bits, A.bitwise_and)
     fill(v("et", 1024, 1536), 0.0)
     cp(v("rh"), v("pbit"))
     cp(v("uou"), v("uoi"))
     fill(v("et", 1536, 2048), 0.0)
-    ts(v("pw", 0, 16), v("c32"), r32, A.is_gt, 2.0 ** -8, A.max)
+    ts(v("pw", 0, 15), v("c32", 0, 15), r32, A.is_le, 2.0 ** -8, A.max)
     ts(v("pw", 16, 19), v("c32", 3, 12, 4), r32, A.is_le, 0.5, A.max)
     for b in range(4):
         ts(v("et", 513 * b, 512 * (b + 1), 4), v("diag"), 0.0, A.is_equal, 0.5, A.mult)
-    red(T8, v("pw", 0, 16), A.mult)
+    red(T8, v("pw", 0, 15), A.mult)
 
     def lin(out, a, b, x=r32):
         act(out, x, AF.Identity, bias=b if isinstance(b, tuple) else float(b), scale=a if isinstance(a, tuple) else float(a))
@@ -311,26 +321,27 @@ def rank_program(g, core, T, topo):
         quant(v("qe", 128 * b, 128 * b + 128), v("qes", 128 * b, 128 * b + 128), v("et", 512 * b, 512 * b + 512))
 
     def start(j):
-        rec_in, rec_out = v("tta", 29, 32, 2), v("cv", REC, REC + 2)
+        rec_in, rec_out = v("ca", RIN, RIN + 3), v("cv", REC, REC + 3)
         for name in CFG["p"][j].split():
             if name[0] == "e" and name != "eu":
                 quant_e(int(name[1]))
             else:
                 {"eu": lambda: cp(v("eabu"), v("eab")),
                  "w2": lambda: red(W2, v("pw", 16, 20), A.mult),
-                 "k0": lambda: ts(v("k0"), v("half"), hh, A.not_equal, 10000.0, A.mult),
-                 "cn": lambda: ts(CN0, r32, -7.0, A.add, 0.5, A.min),
-                 "cim": lambda: tt(v("cim"), v("cidx"), v("k0"), A.subtract),
-                 "c3": lambda: ts(col("ca", CROW + 3), i32, 0.0, A.is_equal, CN0, A.mult),
                  "f": lambda: lin(F16, W2, 0, X),
-                 "row": lambda: lin(v("row2"), W2, F16, v("cim")),
+                 "a0": lambda: lin(col("ta", 1), -TOP * 2.0 ** -64 * 2.0 ** -64, 0, F16),
+                 "a1": lambda: lin(A1, -TOP * 2.0 ** -64 * 2.0 ** -64 * 15 / 16, 0, F16),
+                 "ta": lambda: scan(v("ta", 2, 34), v("four"), v("four"), A1, A.mult, A.mult),
+                 "o2": lambda: ts(col("of2", 2), r32, 0.0, A.is_equal),
                  "un": lambda: unpack(0, C),
                  "rec": lambda: add("v", lambda: V.reciprocal(ap(rec_out), ap(rec_in)), [rec_in], [rec_out]),
                  }[name]()
 
     lin(X, 1, 128, i32)
-    lin(col("tta", 29), -1, -144.5, i32)
-    lin(col("ca", KR), 1 / 1024, 1 / 32)
+    lin(col("ca", RIN), -1, -144.5, i32)
+    lin(col("ca", RIN + 1), 1, 128.5, i32)
+    lin(IDX0, 1 / 16, 2)
+    lin(IDX1, 1 / 16, 3)
     start(0)
     quant(v("qu"), v("qus"), v("ut"))
     act(v("qgs"), ind(v("qus"), v("uou")), AF.Copy)
@@ -347,7 +358,9 @@ def rank_program(g, core, T, topo):
             [v("wp")], [], "x")
         src = T.cores[(rank + t) % n_ranks]
         add("g", None, [], [v("wq%d" % t), v("wp%d" % t)], "r", ("arr%d" % t, 2 * send_mask(T, topo, src, core)[1]))
-    iota(v("undo"), [[16 + 16 * int(UN), 13], [1, K + 1]], 15 - 6 * 16 * int(UN), 0)
+        if t == 1:
+            iota(v("dkc"), [[0, E2]], -1, 0)
+            iota(v("undo"), [[16 + 16 * int(UN), 13], [1, K + 1]], 15 - 6 * 16 * int(UN), 0)
     iota(v("num"), [[1, C]], 0, 0)
     for t, (ra, rb, o) in enumerate((("a2", "b2", 0), ("a3", "b3", 0), ("elb", "elb", E2))):
         iota(v(ra, 1, E2, 2), [[1, K]], C + t * K, 0)
@@ -414,38 +427,32 @@ def rank_program(g, core, T, topo):
         def old(j):
             return plane("d%s%d" % ("ab"[j % 2], 4 - t), j // 2, j % 2, 2)
 
-        def old_src(j):
-            return ind(plane("d%s%d" % ("ab"[j % 2], t - 1), j // 2), split(t - 1))
-
         def task(q, name):
             j = int(name[-1]) if name[-1].isdigit() else 0
             w = name.rstrip("0123456789")
             dx = v("dh", C * j, C * j + C)
             if w == "z":
-                act(v("z", 0, E2), v("dif"), AF.Abs)
+                act(v("z", K * j, K * j + K), v("dif", K * j, K * j + K), AF.Abs)
             elif w == "ev":
                 move(q, dx, bank(j))
             elif w in ("ea", "eb"):
                 par = "ab".index(w[1])
                 move(q, plane("d%s1" % w[1], j), ind(dx, v("eabu", 26 * par, 26 * par + 26)))
-            elif w in ("mid", "mida", "midb"):
-                a, c = {"mid": (0, 26), "mida": (0, 14), "midb": (14, 26)}[w]
+            elif w in ("mida", "midb"):
+                a, c = {"mida": (0, 14), "midb": (14, 26)}[w]
                 tt(v("mall", E2 * j + 16 * a, E2 * j + 16 * c), ind(dx, v("eabu", a, c)), v("db1", E2 * j + 16 * a, E2 * j + 16 * c), A.add)
             elif w == "st":
-                affine(q, v("tt", 91, 96), bias(9), 0, v("ca", WROW, WROW + 5))
+                affine(q, v("cell", 3, 8), col("cell", 1), 0, v("ca", WROW, WROW + 5))
+            elif w == "ref":
+                affine(q, bias(12), 1.0, col("cell", 6), bias(6))
             elif w == "res":
                 affine(q, v("res", 0, E2), 2.0 ** 15, bias(12), v("z", 0, E2))
             elif w == "t":
-                for o, c in {5: ((31, 91), (64, 92)), 7: ((31, 93),)}.get(j, ((31, 91),)):
-                    affine(q, col("tt", o), 16.0 if j < 7 else 1 / 16, col("tt", c), bias(j))
+                affine(q, col("cell", 2), {3: 128.0, 7: 1 / 16}.get(j, 16.0), col("cell", 5 if j < 7 else 7), bias(j))
             elif w == "o":
-                move(q, old(j), old_src(j))
+                move(q, old(j), ind(plane("d%s%d" % ("ab"[j % 2], t - 1), j // 2), split(t - 1)))
             elif w == "m":
                 tt(plane("mall", j // 2, j % 2, 2), old(j), bank(j // 2), A.add)
-            elif w == "d":
-                move(q, v("dh", C * j, C * j + K), bank(j))
-            elif w == "g":
-                tt(plane("mall", j // 2, j % 2, 2), old_src(j), v("dh", C * (j // 2), C * (j // 2) + K), A.add)
             elif w == "n":
                 move(q, plane("da2", j, 1, 2), bank(j))
                 gcopy(plane("db2", j, 0, 2), plane("da2", j, 1, 2), K)
@@ -467,12 +474,17 @@ def rank_program(g, core, T, topo):
             elif w == "qv":
                 quant(v("qv"), v("qvs"), v("vt"))
             elif w == "k":
-                affine(q, *((AV, col("cv", REC), 0, X), (v("ca", CROW, CROW + 3), col("cv", REC + 1), 0, v("ca", KR, KR + 3)),
-                            (col("ca", WROW), -15 / 512, -15 / 16, r32), (col("ca", WROW + 1), -1 / 32, -1 + 120 / 256, r32),
-                            (col("ca", WROW + 2), -1 / 8192, -1 / 512, r32), (col("ca", WROW + 4), 1 / 512, -119.5 / 16, r32),
+                affine(q, *((v("ca", 8, 10), X, 0, v("cv", REC, REC + 2)), (C1, 2.0 ** -12, 0, col("cv", REC + 2)),
+                            (col("ca", WROW + 2), -15 / 512, -15 / 16, r32), (col("ca", WROW + 3), -1 / 512, -1 / 16 + 120 / 256, r32),
+                            (col("ca", WROW + 4), -1 / 8192, -1 / 512, r32), (col("ca", WROW + 1), 1 / 512, -119.5 / 16, r32),
                             (INITB, UN / 32, 104.5 * UN, r32), (CAPI, UN / 32, -103.5 * UN, r32),
                             (BCNT, -UN / 32, M12, r32),
                             (col("ek", 1), 2 * (K - 15) / (16 * UN), 89 * 2 * (K - 15) / 16 + E2 - 30, M12))[j])
+            elif w == "b":
+                affine(q, *((col("tb", 1), 0.5, 16, r32), (col("tb", 2), -14 / 32, 242, r32), (U, 1 / 512, 34 / 32, r32),
+                            (v("tb", 10, 27, 8), U, 0, v("tb", 3, 20, 8)))[j])
+            elif w == "oc":
+                ts(col("of1", 1 + 2 * j), r32, 0.0, A.is_equal, 2.0 + 2 * j, A.mult)
             elif w == "lc":
                 if j == 0:
                     ts(M12, r32, 12.0 * 32, A.min, UN / 2, A.mult)
@@ -490,13 +502,11 @@ def rank_program(g, core, T, topo):
         def side(k):
             tasks("v", PLAN[t]["v"][k - 1])
 
-        def turn(k, out, in_):
-            tr(out, in_)
+        def turn(k, table, off, scale=1.0):
             tasks("v", PLAN[t]["w"][k - 1])
-            tasks("a", PLAN[t]["a"][k - 1])
+            act(v("got", 0, 16 * (off[3] - off[2])), ind(table, off), AF.Identity, scale=scale, acc=bias(k + 1))
 
-        nbase, all_, mid, k0 = bias(9), v("junk", 0, E2 + 1), v("tt", 32, 64), v("k0", 0, 32)
-        cv_ = col("sc", K - 1)
+        all_, cv_ = v("junk", 0, E2 + 1), col("sc", K - 1)
 
         def vector_count(init):
             scan(v("sc"), v("fl", 0, K), v("fl", K, E2), init, A.add, A.add)
@@ -506,41 +516,34 @@ def rank_program(g, core, T, topo):
             ts(v("fl", a, b), v("zb", a, b), 256 / TOP, A.mult, T8, A.is_le)
         vector_count(-1.0 - K)
         side(1)
-        ts(v("tla", 0, 32), k0, col("cnt", 1), A.is_gt, 1 / 16, A.max)
-        ts(v("tla", 32, 64), k0, cv_, A.is_gt, 1 / 16, A.max)
-        turn(1, v("tta", 32, 96), v("tla"))
-        if t == 1:
-            start(5)
-        red(bias(2), v("tta", 30, 96), A.mult)
-        act(all_, v("z", 0, E2 + 1), AF.Sign, bias=bias(2), acc=col("cnt", 2))
+        tasks("a", PLAN[t]["a"][0])
+        ts(col("of2", 0), col("cnt", 1), 0.0, A.is_lt, IDX1, A.mult)
+        ts(col("of2", 1), cv_, 0.0, A.is_lt, IDX0, A.mult)
+        turn(1, v("ta"), v("of2", 0, 3))
+        tasks("a", PLAN[t]["b"][0])
+        act(all_, v("zb", 0, E2 + 1), AF.Sign, bias=bias(2), scale=AS, acc=col("cnt", 2))
         ts(v("fl"), v("zb", 0, E2), AV, A.mult, bias(2), A.is_lt)
-        affine("v", v("ttb", 31, 323, 97), bias(2), 0, v("ca", CROW, CROW + 4))
+        ts(col("nbb", 0), bias(2), C1, A.mult)
         vector_count(1.0 - K)
-        move("a", v("bias", 10, 12), v("ttb", 225, 323, 97))
+        cp(bias(10), col("nbb", 0))
         side(2)
-        ts(v("tlb", 0, 32), v("row2", 0, 32), col("cnt", 2), A.min, bias(10), A.mult)
-        ts(v("tlb", 32, 64), v("row2", 32, 64), cv_, A.min, col("ttb", 225), A.mult)
-        ts(v("tlb", 64, 96), k0, col("cnt", 2), A.is_lt, bias(11), A.mult)
-        turn(2, v("ttb", 32, 96), v("tlb", 0, 64))
-        tr(v("ttb", 96, 128), v("tlb", 64, 96))
-        red(bias(3), v("ttb", 31, 96), A.min)
-        red(nbase, v("ttb", 96, 129), A.add)
-        for k, scale in ((3, 8.0), (4, 2.0 ** 7), (5, 2.0 ** 11), (6, 2.0 ** 15), (7, 16.0)):
+        tasks("a", PLAN[t]["a"][1])
+        ts(col("of2", 0), col("cnt", 2), 0.0, A.is_gt, IDX0, A.mult)
+        ts(col("of2", 1), cv_, 0.0, A.is_gt, IDX1, A.mult)
+        turn(2, v("tb"), v("of2", 0, 3), bias(10))
+        act(v("got", 48, 96), ind(v("tn"), v("of2", 0, 3)), AF.Identity, scale=bias(10), acc=col("cell", 1))
+        tasks("a", PLAN[t]["b"][1])
+        for k, scale in ((3, 1.0), (4, 2.0 ** 7), (5, 2.0 ** 11), (6, 2.0 ** 15), (7, 16.0)):
             s = col("cnt", k)
             act(all_, v("z" if k < 7 else "res", 0, E2 + 1), AF.Sign, bias=bias(k), scale=scale, acc=s)
             side(k)
-            if k == 3:
-                tasks("a", PLAN[t]["s3"])
-            ts(v("tl"), k0, s, A.is_lt, nbase if k < 7 else col("tt", 94), A.mult)
             if k != 6:
                 task("v", "t%d" % k)
-            turn(k, mid if k != 6 else v("tt", 96, 128), v("tl"))
-            if k == 6:
-                red(bias(7), v("tt", 95, 128), A.add)
-            else:
-                red(bias(k + 1), v("tt", 31, 64), A.add, negate=k == 7)
-            if k == 5:
-                red(bias(12), v("tt", 32, 65), A.add)
+            tasks("a", PLAN[t]["a"][k - 1])
+            o = 2 if k == 6 else 0
+            ts(col("of1", o), s, 0.0, A.is_gt, 3.0 if k == 7 else 1.0, A.mult)
+            turn(k, v("cell"), v("of1", o, o + 2), -1.0 if k == 7 else 1.0)
+            tasks("a", PLAN[t]["b"][k - 1])
         tasks("a", PLAN[t]["l1"])
         ts(v("gt", 0, E2), v("res", 0, E2), bias(8), A.is_gt, UN / 2, A.mult)
         ts(v("ge"), v("res", 0, E2), bias(8), A.is_ge, -UN, A.mult)

import numpy as np
from concourse.mybir import dt, AluOpType, AxisListType, ActivationFunctionType

C, K, R = 320, 208, 3
E2 = 2 * K
NT = C + R * K
ND = C + (R - 1) * K
UN = 32.0
TOP = 2.0 ** 70
PAD = 2.0 ** 90
X4, U8, BF, F32, I32, U16 = "float8_e4m3fn_x4", "uint8", "bfloat16", "float32", "int32", "uint16"

SCRATCH = {}
for _d, _bufs in (
    (BF, {"xt": 4 * C, "ut": 512, "vt": 512, "et": 2048, "diag": 128, "junk": E2 + 2, "res": E2 + 2, "zb": E2 + 2, "fl": E2, "sc": K,
          "gt": E2 + 2, "ge": E2, "cap": E2, "cum": E2, "qn": E2, "dh": 4 * C, "mt": 1024, "rt": 1024, "nbb": 2,
          "mall": 4 * E2, "da1": 4 * E2, "db1": 4 * E2, "da2": 4 * E2, "db2": 4 * E2}),
    (X4, {"wq": 512, "wq1": 512, "wq2": 512, "wq3": 512, "tab": NT + 48, "qu": 128, "qg": 128, "qv": 128, "qe": 512, "qm": 256}),
    (U8, {"wp": 512, "wp1": 512, "wp2": 512, "wp3": 512, "tabs": NT + 48, "qus": 128, "qgs": 128, "qvs": 128, "qes": 512, "qms": 256}),
    (I32, {"eab": 52, "uoi": 8, "pidx": 1, "pbit": 2}),
    (U16, {"eabu": 52, "uou": 8, "ecu": 4, "of2": 4, "of1": 4, "lu1": 14, "lu2": 14, "lu3": 14}),
    (F32, {"rh": 2, "num": C, "undo": 13 * (K + 1), "c32": 16, "pw": 24, "ca": 24, "cv": 12,
           "ta": 40, "tb": 40, "tn": 40, "four": 32, "cell": 8, "got": 96, "ek": 2,
           "ptab": C, "pa1": E2, "pb1": E2, "dif": E2, "z": E2 + 2, "cnt": 16, "bias": 16,
           "a1": E2, "b1": E2, "dkc": E2, "sa": E2, "kq": 16, "xe": 16,
           "pa2": E2, "pb2": E2, "pa3": E2, "pb3": E2, "a2": E2, "b2": E2, "a3": E2, "b3": E2, "elb": 2 * E2, "ysb": NT}),
):
    for _n in _bufs:
        SCRATCH[_n] = ("sbuf", [128, _bufs[_n]], _d)
for _i in range(8):
    SCRATCH["ps%d" % _i] = ("psum", [128, 512], F32)

POOL = {"v": 32, "a": 28, "t": 12, "g": 44}
NDMA = 27
SEMAPHORES = ["arr1", "arr2", "arr3", "sent"] + ["d%d" % _i for _i in range(NDMA)]
for _q in POOL:
    SEMAPHORES += ["%s%d" % (_q, _i) for _i in range(POOL[_q])]

A = AluOpType
AF = ActivationFunctionType

CFG = {"p": ["w2 f a0 a1 e0 e1", "eu e2 e3 un", "o2", "", "ta rec", ""],
       "co": "pa03 pa01 pa12 pv00 pv02 pv13 pa11 pv10 L0 L1 c0 el ev01 ev02 ev10 ea00 ea03 ev12 ea11 ea13 N0 c1 N1 c2"}
PLAN = {
    1: {"v": ["k0", "", "ev1 ev2 st eb0", "mida0 midb0 midb1", "", "ref lc1 res", "qv"],
        "w": ["b1 b2 zf1 b0 oc0 b3", "ev0", "", "lc0 mida1 ev3 zf0", "mida2 oc1", "midb3 mida3", "midb2 yp"],
        "a": ["z0", "k3 k4 z1", "eb1", "eb2", "eb3", "k9 k8", "ea0"],
        "b": ["k2 k5 k1", "", "k7", "", "k6", "", ""],
        "l1": "ea1 yo", "l2": "pa1"},
    2: {"v": ["", "", "st o1", "m1 ea2", "m0", "m4 ref o5 res", ""],
        "w": ["o2", "n1 o0", "", "ea3", "", "m6 m7 m3 m2", "m5"],
        "a": ["z0", "z1", "", "o3", "o4", "o7", "n0"],
        "b": ["", "", "", "", "o6", "", "yo"],
        "l1": "n3 np n2", "l2": "r1"},
    3: {"v": ["", "", "st", "o3 m0 m3 m1", "o5 m4 m5", "m2 ref res", "o7 r0 m7"],
        "w": ["o2", "o0 o4", "", "", "", "", "m6"],
        "a": ["z0", "z1", "o1", "", "", "o6", "e11"],
        "b": ["", "", "", "", "", "", "yo e10 e21"],
        "l1": "", "l2": "e20"},
}


def v(name, a=0, b=None, s=1):
    return ("v", name, a, SCRATCH[name][1][1] if b is None else b, s)


def col(name, j):
    return v(name, j, j + 1)


def ind(win, off, words=False):
    return ("i", win, off, words)


def send_mask(T, topo, src, dst):
    far = set()
    for c in T.cores:
        if topo.chip(c) != topo.chip(src):
            far |= set(topo.engines(src, c))
    es = topo.engines(src, dst)
    if topo.chip(src) == topo.chip(dst):
        rest = [e for e in es if e not in far]
        if rest and 128 % len(rest) == 0:
            es = rest
    return sum(1 << e for e in es), len(es)


def program(g, T):
    ops = []
    last_w = {n: np.full(SCRATCH[n][1][1], -1) for n in SCRATCH}
    readers = {n: [] for n in SCRATCH}
    queue = {"v": g.vector, "a": g.scalar, "t": g.tensor, "g": g, "s": g.sync}

    def ap(x):
        if not isinstance(x, tuple):
            return x
        if x[0] == "i":
            w = ap(x[1])
            if x[3]:
                w = w.bitcast(dt.uint32)
            return w.indirect(ap(x[2]))
        if x[4] == 1:
            return T[x[1]][:, x[2]:x[3]]
        return T[x[1]][:, x[2]:(x[3] if x[3] >= 0 else None):x[4]]

    def views(xs):
        out = []
        for x in xs:
            if isinstance(x, tuple):
                out += [x[1], x[2]] if x[0] == "i" else [x]
        return out

    def cols(x):
        return np.arange(512) if SCRATCH[x[1]][0] == "psum" else np.arange(x[2], x[3], x[4])

    def add(q, fn, reads, writes, kind="c", sem=None):
        me, deps = len(ops), set()
        for x in views(reads):
            n = x[1]
            if SCRATCH[n][0] == "psum":
                deps |= {o for o, ix in readers[n] if ops[o]["q"] != q}
            deps |= set(int(o) for o in last_w[n][cols(x)])
        for x in views(writes):
            n, idx = x[1], cols(x)
            deps |= set(int(o) for o in last_w[n][idx])
            m = np.zeros(len(last_w[n]), bool)
            m[idx] = True
            deps |= {o for o, ix in readers[n] if m[ix].any()}
            readers[n] = [(o, ix[~m[ix]]) for o, ix in readers[n] if not m[ix].all()]
            last_w[n][idx] = me
        for x in views(reads):
            readers[x[1]].append((me, cols(x)))
        deps.discard(-1)
        deps.discard(me)
        ops.append({"q": q, "fn": fn, "deps": deps, "kind": kind, "sem": sem})

    def emit():
        known = {q: 0 for q in queue}
        after, waits, needed = [], [], set()
        for i, o in enumerate(ops):
            w = []
            if o["kind"] != "r":
                for d in sorted(o["deps"], reverse=True):
                    if not known[o["q"]] >> d & 1:
                        w.append(d)
                        known[o["q"]] |= after[d]
                o["known"] = known[o["q"]]
            after.append((o["known"] if o["kind"] != "r" else 0) | 1 << i)
            waits.append(w)
            needed |= set(w)
        pool = {q: [[None, 0] for j in range(POOL[q])] for q in POOL}
        nd, turn, tail = [0], {q: 0 for q in POOL}, []
        for i, o in enumerate(ops):
            if o["kind"] == "r":
                continue
            q = o["q"]
            for d in reversed(waits[i]):
                queue[q].wait_ge(T.sem[ops[d]["sem"][0]], ops[d]["sem"][1])
            ins = o["fn"]()
            if o["kind"] == "d":
                o["sem"] = ("d%d" % nd[0], 16)
                nd[0] += 1
                ins.then_inc(T.sem[o["sem"][0]], 16)
                if i not in needed:
                    tail.append((q, o["sem"]))
            elif o["kind"] == "c" and i in needed:
                for k in range(POOL[q]):
                    j = (turn[q] + k) % POOL[q]
                    p = pool[q][j]
                    if p[0] is None or o["known"] >> p[0] & 1:
                        break
                else:
                    raise ValueError("no free semaphore on " + q)
                turn[q] = j + 1
                p[0] = i
                p[1] += 1
                o["sem"] = ("%s%d" % (q, j), p[1])
                ins.then_inc(T.sem[o["sem"][0]], 1)
        for q, s in tail:
            queue[q].wait_ge(T.sem[s[0]], s[1])

    return ap, add, emit


def rank_program(g, core, T, topo):
    rank = T.rank_of(core)
    if rank is None:
        return
    n_ranks = len(T.cores)
    ap, add, emit = program(g, T)
    V, S, PE = g.vector, g.scalar, g.tensor

    def ts(out, in0, s1, op0, s2=None, op1=None):
        if op1 is None:
            add("v", lambda: V.tensor_scalar(ap(out), ap(in0), ap(s1), None, op0), [in0, s1], [out])
        else:
            add("v", lambda: V.tensor_scalar(ap(out), ap(in0), ap(s1), ap(s2), op0, op1), [in0, s1, s2], [out])

    def tt(out, in0, in1, op):
        add("v", lambda: V.tensor_tensor(ap(out), ap(in0), ap(in1), op), [in0, in1], [out])

    def cp(out, in_):
        add("v", lambda: V.tensor_copy(ap(out), ap(in_)), [in_], [out])

    def red(out, in_, op):
        add("v", lambda: V.tensor_reduce(ap(out), ap(in_), AxisListType.X, op), [in_], [out])

    def scan(out, d0, d1, init, op0, op1):
        add("v", lambda: V.tensor_tensor_scan(ap(out), ap(d0), ap(d1), ap(init), op0, op1), [d0, d1, init], [out])

    def fill(out, c):
        add("v", lambda: V.memset(ap(out), c), [], [out])

    def quant(q, s, in_):
        add("v", lambda: V.quantize_mx(ap(q), ap(s), ap(in_)), [in_], [q, s])

    def act(out, in_, f, bias=None, scale=None, acc=None):
        kw = {k: x for k, x in (("bias", bias), ("scale", scale), ("accum_out", acc)) if x is not None}
        add("a", lambda: S.activation(ap(out), ap(in_), f, **{k: ap(x) for k, x in kw.items()}), [in_, bias, scale], [out, acc])

    def mm(out, wq, ws, xq, xs):
        add("t", lambda: PE.matmul_mx(ap(out), ap(wq), ap(ws), ap(xq), ap(xs), True, True), [wq, ws, xq, xs], [out])

    def iota(out, pattern, base, cm):
        if SCRATCH[out[1]][2] == I32:
            add("g", lambda: g.iota(ap(out), pattern, base, cm), [], [out])
        else:
            add("g", lambda: g.iota(ap(out), pattern, base, cm, allow_small_or_imprecise_dtypes=True), [], [out])

    def gcopy(out, in_, n):
        add("g", lambda: g.affine_select(ap(out), ap(in_), [[0, n]], A.is_gt, 0.0, 1, 0), [in_], [out])

    def gfill(out, c):
        src = col("c32" if SCRATCH[out[1]][2] == F32 else "diag", 0)
        add("g", lambda: g.affine_select(ap(out), ap(src), [[0, 1]], A.is_gt, c, 0, 0), [src], [out])

    def dma(q, out, in_, reads, writes):
        eng = g.sync if q == "s" else g.scalar
        add(q, lambda: eng.dma_start(out(), in_()), reads, writes, "d")

    def codes(x):
        return ap(x).bitcast(dt.uint8)

    def tabv(a, b):
        return v("tab", a, b), v("tabs", a, b)

    def store_y(q, a, b):
        dma(q, lambda: T.y[:, a:b], lambda: T.ysb[:, a:b], [v("ysb", a, b)], [])

    def store_codes(q, a, b):
        dma(q, lambda: T.oc[:, 4 * a:4 * b], lambda: codes(v("tab", a, b)), [v("tab", a, b)], [])

    def store_scales(qs, a, b):
        for k in range(4):
            dma(qs[k], lambda k=k: T.osc[4 * k:4 * k + 4, a:b], lambda k=k: T.tabs[32 * k:32 * k + 4, a:b], [v("tabs", a, b)], [])

    def unpack(a, b):
        for i in range(4):
            mm(v("ps%d" % (4 + i), 0, b - a), v("qe", 128 * i, 128 * i + 128), v("qes", 128 * i, 128 * i + 128), *tabv(a, b))

    r32, i32 = col("rh", 0), col("rh", 1)
    X, INITB, CAPI, IDX0, IDX1, C1, A1, U = (col("ca", j) for j in range(8))
    AV, AS = col("ca", 8), col("ca", 9)
    RIN, WROW = 10, 14
    T8, W2, M12, BCNT, REC = col("cv", 0), col("cv", 1), col("cv", 2), col("cv", 3), 4
    F16 = col("ca", RIN + 2)
    H = C // 2

    dma("a", lambda: T.ut[:], lambda: T.u[:], [], [v("ut")])
    dma("s", lambda: T.xt[:, 0:4 * H], lambda: T.x[:, 0:4 * H], [], [v("xt", 0, 4 * H)])
    dma("s", lambda: T.xt[:, 4 * H:4 * C], lambda: T.x[:, 4 * H:4 * C], [], [v("xt", 4 * H, 4 * C)])
    dma("s", lambda: T.eab[:, 26:52], lambda: T.eb[:], [], [v("eab", 26, 52)])
    dma("s", lambda: T.eab[:, 0:26], lambda: T.ea[:], [], [v("eab", 0, 26)])
    dma("s", lambda: codes(v("wq")), lambda: T.wc[:], [v("xt")], [v("wq")])
    dma("s", lambda: T.wp[:], lambda: T.ws[:], [], [v("wp")])
    dma("s", lambda: T.vt[:], lambda: T.v[:], [], [v("vt")])

    def const(name, a, b, c, s=1):
        iota(v(name, a, b, s), [[0, len(range(a, b, s))]], c, 0)

    iota(v("pidx"), [[0, 1]], 0, 32)
    iota(v("uoi"), [[16, 8]], 0, 0)
    iota(v("c32"), [[32, 16]], 32, 0)
    iota(v("diag"), [[-1, 128]], 0, 1)
    gfill(col("pw", 19), 2.0 ** -8)
    const("four", 0, 32, 4)
    gfill(col("zb", E2), PAD)
    const("ta", 0, 40, 0, 39)
    const("ta", 34, 39, 0)
    const("tb", 0, 40, 0, 39)
    const("tb", 35, 39, 0)
    for j in range(4):
        const("tb", 3 + 8 * j, 11 + 8 * j, 32 << j)
    const("tn", 0, 40, 0)
    const("cell", 0, 8, 0)
    iota(v("tn", 1, 3), [[-15 * 256, 2]], 8 * 256, 0)
    for j in range(3):
        const("tn", 10 + 8 * j, 11 + 8 * j, 256 << j)
    gfill(col("z", E2), PAD)
    gfill(col("ca", WROW), 2.0 ** -8)
    gfill(col("res", E2), PAD)
    gfill(col("gt", E2), 0.0)
    gfill(col("ek", 0), float(E2))
    fill(v("et", 0, 1024), 0.0)
    for j, bits in enumerate((15, 3)):
        ts(col("pbit", j), v("pidx"), 32 * bits, A.bitwise_and)
    fill(v("et", 1024, 1536), 0.0)
    cp(v("rh"), v("pbit"))
    cp(v("uou"), v("uoi"))
    fill(v("et", 1536, 2048), 0.0)
    ts(v("pw", 0, 15), v("c32", 0, 15), r32, A.is_le, 2.0 ** -8, A.max)
    ts(v("pw", 16, 19), v("c32", 3, 12, 4), r32, A.is_le, 0.5, A.max)
    for b in range(4):
        ts(v("et", 513 * b, 512 * (b + 1), 4), v("diag"), 0.0, A.is_equal, 0.5, A.mult)
    red(T8, v("pw", 0, 15), A.mult)

    def lin(out, a, b, x=r32):
        act(out, x, AF.Identity, bias=b if isinstance(b, tuple) else float(b), scale=a if isinstance(a, tuple) else float(a))

    def quant_e(b):
        quant(v("qe", 128 * b, 128 * b + 128), v("qes", 128 * b, 128 * b + 128), v("et", 512 * b, 512 * b + 512))

    def start(j):
        rec_in, rec_out = v("ca", RIN, RIN + 3), v("cv", REC, REC + 3)
        for name in CFG["p"][j].split():
            if name[0] == "e" and name != "eu":
                quant_e(int(name[1]))
            else:
                {"eu": lambda: cp(v("eabu"), v("eab")),
                 "w2": lambda: red(W2, v("pw", 16, 20), A.mult),
                 "f": lambda: lin(F16, W2, 0, X),
                 "a0": lambda: lin(col("ta", 1), -TOP * 2.0 ** -64 * 2.0 ** -64, 0, F16),
                 "a1": lambda: lin(A1, -TOP * 2.0 ** -64 * 2.0 ** -64 * 15 / 16, 0, F16),
                 "ta": lambda: scan(v("ta", 2, 34), v("four"), v("four"), A1, A.mult, A.mult),
                 "o2": lambda: ts(col("of2", 2), r32, 0.0, A.is_equal),
                 "un": lambda: unpack(0, C),
                 "rec": lambda: add("v", lambda: V.reciprocal(ap(rec_out), ap(rec_in)), [rec_in], [rec_out]),
                 }[name]()

    lin(X, 1, 128, i32)
    lin(col("ca", RIN), -1, -144.5, i32)
    lin(col("ca", RIN + 1), 1, 128.5, i32)
    lin(IDX0, 1 / 16, 2)
    lin(IDX1, 1 / 16, 3)
    start(0)
    quant(v("qu"), v("qus"), v("ut"))
    act(v("qgs"), ind(v("qus"), v("uou")), AF.Copy)

    sent = [0]
    for t in range(1, R + 1):
        dst = T.cores[(rank - t) % n_ranks]
        rid, pid = topo.addr(dst)[0], topo.addr(dst)[1]
        m, ne = send_mask(T, topo, core, dst)
        sent[0] += 2 * ne
        add("g", lambda t=t, rid=rid, pid=pid, m=m: g.remote_dma(codes(v("wq%d" % t)), codes(v("wq")), T.sem["arr%d" % t], T.sem.sent, pid, rid, m),
            [v("wq")], [], "x")
        add("g", lambda t=t, rid=rid, pid=pid, m=m: g.remote_dma(ap(v("wp%d" % t)), ap(v("wp")), T.sem["arr%d" % t], T.sem.sent, pid, rid, m),
            [v("wp")], [], "x")
        src = T.cores[(rank + t) % n_ranks]
        add("g", None, [], [v("wq%d" % t), v("wp%d" % t)], "r", ("arr%d" % t, 2 * send_mask(T, topo, src, core)[1]))
        if t == 1:
            iota(v("dkc"), [[0, E2]], -1, 0)
            iota(v("undo"), [[16 + 16 * int(UN), 13], [1, K + 1]], 15 - 6 * 16 * int(UN), 0)
    iota(v("num"), [[1, C]], 0, 0)
    for t, (ra, rb, o) in enumerate((("a2", "b2", 0), ("a3", "b3", 0), ("elb", "elb", E2))):
        iota(v(ra, 1, E2, 2), [[1, K]], C + t * K, 0)
        iota(v(rb, o, o + E2, 2), [[1, K]], C + t * K, 0)

    quant(*tabv(0, H), v("xt", 0, 4 * H))
    add("v", lambda: V.tensor_copy(ap(v("qg")).bitcast(dt.uint32), ap(ind(v("qu"), v("uou"), True))), [ind(v("qu"), v("uou"))], [v("qg")])
    quant(*tabv(H, C), v("xt", 4 * H, 4 * C))
    mm(v("ps0", 0, H), v("qg"), v("qgs"), *tabv(0, H))
    mm(v("ps1", 0, H), v("qg"), v("qgs"), *tabv(H, C))
    act(v("ptab", 0, H), v("ps0", 0, H), AF.Copy)
    start(1)
    cp(v("ptab", H, C), v("ps1", 0, H))
    start(2)
    cuts = (0, 96, 256, E2)
    cp(v("pb1", 0, cuts[1]), ind(v("ptab"), v("eabu", 26, 26 + cuts[1] // 16)))
    for a, b in zip(cuts[1:], cuts[2:]):
        act(v("pb1", a, b), ind(v("ptab"), v("eabu", 26 + a // 16, 26 + b // 16)), AF.Copy)
    start(3)
    for a, b in zip(cuts, cuts[1:]):
        tt(v("dif", a, b), ind(v("ptab"), v("eabu", a // 16, b // 16)), v("pb1", a, b), A.subtract)
        act(v("zb", a, b), v("dif", a, b), AF.Abs)
    start(4)

    HS = ((0, 128), (128, K))

    def move(q, out, src):
        if q == "v":
            cp(out, src)
        else:
            act(out, src, AF.Copy)

    def affine(q, out, a, b, x):
        if q == "a":
            lin(out, a, b, x)
        elif b == 0:
            ts(out, x, a, A.mult)
        else:
            ts(out, x, a, A.mult, b, A.add)

    def split(t, a=0, c=K):
        return v("lu%d" % t, a // 16, c // 16)

    def next_ends(t, par, q="a"):
        src = ind(v("ab"[par] + str(t)), split(t))
        move(q, v("ab"[par] + str(t + 1), par, E2, 2) if t < R else v("elb", par * (E2 + 1), (par + 1) * E2, 2), src)

    def y_product(a, b):
        mm(v("ps2", 0, b - a), v("qv"), v("qvs"), *tabv(a, b))

    def plane(name, b, a=0, s=1):
        return v(name, E2 * b + a, E2 * (b + 1), s)

    def bias(k):
        return col("bias", k)

    for t in range(1, R + 1):
        n = C + (t - 1) * K
        n0 = 0 if t == 1 else n - K

        def bank(b, a=0, c=n - n0):
            return v("ps%d" % (4 + b), a, c)

        def old(j):
            return plane("d%s%d" % ("ab"[j % 2], 4 - t), j // 2, j % 2, 2)

        def task(q, name):
            j = int(name[-1]) if name[-1].isdigit() else 0
            w = name.rstrip("0123456789")
            dx = v("dh", C * j, C * j + C)
            if w == "z":
                act(v("z", K * j, K * j + K), v("dif", K * j, K * j + K), AF.Abs)
            elif w == "ev":
                move(q, dx, bank(j))
            elif w in ("ea", "eb"):
                par = "ab".index(w[1])
                move(q, plane("d%s1" % w[1], j), ind(dx, v("eabu", 26 * par, 26 * par + 26)))
            elif w in ("mida", "midb"):
                a, c = {"mida": (0, 14), "midb": (14, 26)}[w]
                tt(v("mall", E2 * j + 16 * a, E2 * j + 16 * c), ind(dx, v("eabu", a, c)), v("db1", E2 * j + 16 * a, E2 * j + 16 * c), A.add)
            elif w == "st":
                affine(q, v("cell", 3, 8), col("cell", 1), 0, v("ca", WROW, WROW + 5))
            elif w == "ref":
                affine(q, bias(12), 1.0, col("cell", 6), bias(6))
            elif w == "res":
                affine(q, v("res", 0, E2), 2.0 ** 15, bias(12), v("z", 0, E2))
            elif w == "t":
                affine(q, col("cell", 2), {3: 128.0, 7: 1 / 16}.get(j, 16.0), col("cell", 5 if j < 7 else 7), bias(j))
            elif w == "o":
                move(q, old(j), ind(plane("d%s%d" % ("ab"[j % 2], t - 1), j // 2), split(t - 1)))
            elif w == "m":
                tt(plane("mall", j // 2, j % 2, 2), old(j), bank(j // 2), A.add)
            elif w == "n":
                move(q, plane("da2", j, 1, 2), bank(j))
                gcopy(plane("db2", j, 0, 2), plane("da2", j, 1, 2), K)
            elif w == "np":
                for h, (a, c) in enumerate(HS):
                    move(q, v("pa2", 2 * a + 1, 2 * c, 2), v("ps%d" % h, 0, c - a))
                gcopy(v("pb2", 0, E2, 2), v("pa2", 1, E2, 2), K)
            elif w == "pa":
                move(q, v("pa1"), ind(v("ptab"), v("eabu", 0, 26)))
            elif w == "r":
                move(q, v("ab"[j] + "1"), ind(v("num"), v("eabu", 26 * j, 26 * j + 26)))
            elif w == "e":
                next_ends(int(name[1]), j, q)
            elif w == "yp":
                y_product(n0, n)
            elif w == "yo":
                move(q, v("ysb", n0, n), v("ps2", 0, n - n0))
                store_y("s", n0, n)
            elif w == "qv":
                quant(v("qv"), v("qvs"), v("vt"))
            elif w == "k":
                affine(q, *((v("ca", 8, 10), X, 0, v("cv", REC, REC + 2)), (C1, 2.0 ** -12, 0, col("cv", REC + 2)),
                            (col("ca", WROW + 2), -15 / 512, -15 / 16, r32), (col("ca", WROW + 3), -1 / 512, -1 / 16 + 120 / 256, r32),
                            (col("ca", WROW + 4), -1 / 8192, -1 / 512, r32), (col("ca", WROW + 1), 1 / 512, -119.5 / 16, r32),
                            (INITB, UN / 32, 104.5 * UN, r32), (CAPI, UN / 32, -103.5 * UN, r32),
                            (BCNT, -UN / 32, M12, r32),
                            (col("ek", 1), 2 * (K - 15) / (16 * UN), 89 * 2 * (K - 15) / 16 + E2 - 30, M12))[j])
            elif w == "b":
                affine(q, *((col("tb", 1), 0.5, 16, r32), (col("tb", 2), -14 / 32, 242, r32), (U, 1 / 512, 34 / 32, r32),
                            (v("tb", 10, 27, 8), U, 0, v("tb", 3, 20, 8)))[j])
            elif w == "oc":
                ts(col("of1", 1 + 2 * j), r32, 0.0, A.is_equal, 2.0 + 2 * j, A.mult)
            elif w == "lc":
                if j == 0:
                    ts(M12, r32, 12.0 * 32, A.min, UN / 2, A.mult)
                else:
                    ts(M12, M12, -89 * UN, A.add)
            elif w == "zf":
                fill(v("mt" if j else "rt", 4 * K, 1024), 0.0)
            else:
                raise ValueError(name)

        def tasks(q, s):
            for name in s.split():
                task(q, name)

        def side(k):
            tasks("v", PLAN[t]["v"][k - 1])

        def turn(k, table, off, scale=1.0):
            tasks("v", PLAN[t]["w"][k - 1])
            act(v("got", 0, 16 * (off[3] - off[2])), ind(table, off), AF.Identity, scale=scale, acc=bias(k + 1))

        all_, cv_ = v("junk", 0, E2 + 1), col("sc", K - 1)

        def vector_count(init):
            scan(v("sc"), v("fl", 0, K), v("fl", K, E2), init, A.add, A.add)

        act(all_, v("zb", 0, E2 + 1), AF.Sign, bias=T8, scale=-16 / TOP / (1 + 2.0 ** -8), acc=col("cnt", 1))
        for a, b in ((0, 256), (256, E2)):
            ts(v("fl", a, b), v("zb", a, b), 256 / TOP, A.mult, T8, A.is_le)
        vector_count(-1.0 - K)
        side(1)
        tasks("a", PLAN[t]["a"][0])
        ts(col("of2", 0), col("cnt", 1), 0.0, A.is_lt, IDX1, A.mult)
        ts(col("of2", 1), cv_, 0.0, A.is_lt, IDX0, A.mult)
        turn(1, v("ta"), v("of2", 0, 3))
        tasks("a", PLAN[t]["b"][0])
        act(all_, v("zb", 0, E2 + 1), AF.Sign, bias=bias(2), scale=AS, acc=col("cnt", 2))
        ts(v("fl"), v("zb", 0, E2), AV, A.mult, bias(2), A.is_lt)
        ts(col("nbb", 0), bias(2), C1, A.mult)
        vector_count(1.0 - K)
        cp(bias(10), col("nbb", 0))
        side(2)
        tasks("a", PLAN[t]["a"][1])
        ts(col("of2", 0), col("cnt", 2), 0.0, A.is_gt, IDX0, A.mult)
        ts(col("of2", 1), cv_, 0.0, A.is_gt, IDX1, A.mult)
        turn(2, v("tb"), v("of2", 0, 3), bias(10))
        act(v("got", 48, 96), ind(v("tn"), v("of2", 0, 3)), AF.Identity, scale=bias(10), acc=col("cell", 1))
        tasks("a", PLAN[t]["b"][1])
        for k, scale in ((3, 1.0), (4, 2.0 ** 7), (5, 2.0 ** 11), (6, 2.0 ** 15), (7, 16.0)):
            s = col("cnt", k)
            act(all_, v("z" if k < 7 else "res", 0, E2 + 1), AF.Sign, bias=bias(k), scale=scale, acc=s)
            side(k)
            if k != 6:
                task("v", "t%d" % k)
            tasks("a", PLAN[t]["a"][k - 1])
            o = 2 if k == 6 else 0
            ts(col("of1", o), s, 0.0, A.is_gt, 3.0 if k == 7 else 1.0, A.mult)
            turn(k, v("cell"), v("of1", o, o + 2), -1.0 if k == 7 else 1.0)
            tasks("a", PLAN[t]["b"][k - 1])
        tasks("a", PLAN[t]["l1"])
        ts(v("gt", 0, E2), v("res", 0, E2), bias(8), A.is_gt, UN / 2, A.mult)
        ts(v("ge"), v("res", 0, E2), bias(8), A.is_ge, -UN, A.mult)
        scan(v("cap", E2 - 1, -1, -1), v("gt", E2, 0, -1), v("gt", E2, 0, -1), CAPI, A.add, A.add)
        scan(v("cum"), v("ge"), v("cap"), INITB, A.add, A.max)
        act(v("junk", 0, E2), v("cum"), AF.Sign, bias=BCNT, acc=col("cnt", 8))
        tasks("a", PLAN[t]["l2"])
        big = 1.5 * 2.0 ** 23 * 16 * UN
        ts(v("qn"), v("cum"), big, A.add, big, A.subtract)
        ts(v("ecu", 0, 4, 2), v("ek"), col("cnt", 8), A.add, 0.5, A.mult)
        act(v("kq"), ind(v("undo"), col("ecu", 2)), AF.Copy)
        scan(v("sa"), v("dkc"), v("qn"), 256 * UN, A.add, A.min)
        tt(v("xe"), ind(v("sa"), col("ecu", 0)), v("kq"), A.add)
        cp(v("lu%d" % t), v("xe", 0, 14))

        def carry(par, a=0, c=K):
            move("a", v("p%s%d" % ("ab"[par], t + 1), 2 * a + par, 2 * c, 2), ind(v("p%s%d" % ("ab"[par], t)), split(t, a, c)))

        def layer(h):
            a = 128 * h
            quant(v("qm", a, a + 128), v("qms", a, a + 128), v("mt", 4 * a, 4 * a + 512))
            for b in range(4):
                mm(v("ps%d" % (4 * h + b), 0, 128), v("wq%d" % t, 128 * b, 128 * b + 128), v("wp%d" % t, 128 * b, 128 * b + 128),
                   v("qm", a, a + 128), v("qms", a, a + 128))

        def new_cols(h):
            a = 128 * h
            quant(*tabv(n + a, n + a + 128), v("rt", 4 * a, 4 * a + 512))
            by = ("qg", "qgs") if t < R else ("qv", "qvs")
            mm(v("ps%d" % h, 0, 128), v(by[0]), v(by[1]), *tabv(n + a, n + a + 128))

        def scores(h):
            a, c = HS[h]
            for par in range(2):
                tt(v("dif", 2 * a + par, 2 * c, 2), v("p" + "ab"[par] + str(t + 1), 2 * a + par, 2 * c, 2), v("ps%d" % h, 0, c - a), A.subtract)
                if h == 0:
                    act(v("zb", 2 * a + par, 2 * c, 2), v("dif", 2 * a + par, 2 * c, 2), AF.Abs)
            if h == 1:
                act(v("zb", 2 * a, 2 * c), v("dif", 2 * a, 2 * c), AF.Abs)

        for w in CFG["co"].split():
            if w == "el":
                if t == R:
                    next_ends(t, 1, "v")
                    dma("s", lambda: T.el[:], lambda: T.elb[0:128:16, :], [v("elb")], [])
            elif w[0] in "pe":
                h, b = int(w[2]), int(w[3])
                a, c = HS[h]
                if w[0] == "p":
                    move(w[1], v("mt", 4 * a + b, 4 * c, 4), ind(plane("mall", b), split(t, a, c)))
                else:
                    affine(w[1], v("rt", 4 * a + b, 4 * c, 4), 0.03125, 0, v("ps%d" % (4 * h + b), 0, c - a))
            elif w[0] == "L":
                layer(int(w[1]))
            elif w[0] == "N":
                new_cols(int(w[1]))
            elif w == "c0":
                if t < R:
                    carry(0)
                else:
                    next_ends(t, 0)
            elif t < R:
                carry(1, *HS[int(w[1]) - 1])
        if t < R:
            unpack(n, n + K)
            y_product(n, n + K)
            scores(0)
            scores(1)
            if t == 2:
                store_codes("s", 0, ND)
                store_scales("ssss", 0, ND)
        else:
            move("a", v("ysb", ND, ND + 128), v("ps0", 0, 128))
            store_codes("s", ND, NT)
            cp(v("ysb", ND + 128, NT), v("ps1", 0, K - 128))
            store_scales("aaaa", ND, NT)
            store_y("s", ND, NT)
    emit()
    g.wait_ge(T.sem.sent, sent[0])
